import numpy as np
import ml_dtypes


def mxq(x, axis, fmt="e4m3"):
    dtype, down = {"e4m3": (ml_dtypes.float8_e4m3fn, 7), "e5m2": (ml_dtypes.float8_e5m2, 14)}[fmt]
    v = np.moveaxis(np.asarray(x, np.float32).astype(ml_dtypes.bfloat16).astype(np.float64), axis, -1)
    blocks = v.reshape(v.shape[:-1] + (-1, 32))
    amax = np.abs(blocks).max(-1, keepdims=True)
    byte = np.maximum(np.where(amax > 0, np.frexp(amax)[1] - 1 + 127, 0) - down, 1)
    scale = np.exp2(byte - 127.0)
    codes = (blocks / scale).astype(np.float32).astype(dtype).astype(np.float64)
    return np.moveaxis((codes * scale).reshape(v.shape), -1, axis)


WIDE = False


def mx_kscale(k):
    if not WIDE:
        return np.ones(k)
    levels = np.array([10, -10, 5, -5, 0])
    if k % 512:
        return np.exp2(np.random.permutation(np.resize(levels, k // 32))).repeat(32)
    a = np.empty((k // 512, 16))
    for p in range(k // 512):
        a[p, :8] = np.random.permutation(np.resize(levels, 8))
        for g in range(8):
            far = levels[np.abs(levels - a[p, g]) >= 10]
            a[p, g + 8] = far[np.random.randint(len(far))]
    return np.exp2(a.ravel()).repeat(32)


def f64(x):
    return np.asarray(x).astype(np.float64)


def striped(idx):
    return np.tile(idx.reshape(-1, 16).T, (8, 1)).astype(np.uint16)


def unstriped(offs):
    return offs[:16].T.reshape(-1).astype(np.int64)


E2M1 = np.array([0.0, 0.5, 1.0, 1.5, 2.0, 3.0, 4.0, 6.0, -0.0, -0.5, -1.0, -1.5, -2.0, -3.0, -4.0, -6.0])


def pack_weight(w, fmt):
    k, n = w.shape
    w = f64(np.asarray(w, np.float32).astype(ml_dtypes.bfloat16)).reshape(k // 32, 32, n)
    amax = np.abs(w).max(1)
    if fmt == "e4m3":
        byte = np.frexp(amax)[1] - 1 + 127 - 7
    else:
        mant, ex = np.frexp(amax / 6.0)
        byte = np.where(mant > 0.5, ex, ex - 1) + 127
    byte = np.clip(np.where(amax > 0, byte, 1), 1, 254)
    scaled = (w * np.exp2(127.0 - byte)[:, None, :]).reshape(k, n).astype(np.float32)
    by_word = np.ascontiguousarray(scaled.reshape(k // 512, 128, 4, n).transpose(0, 1, 3, 2))
    if fmt == "e4m3":
        words = by_word.astype(ml_dtypes.float8_e4m3fn).view(np.uint8)
    else:
        c = by_word.astype(ml_dtypes.float4_e2m1fn).view(np.uint8) & 0xF
        words = (c[..., 0::2] | (c[..., 1::2] << 4)).reshape(k // 512, 128, 2 * n)
    return np.ascontiguousarray(words), np.ascontiguousarray(byte.astype(np.uint8).reshape(k // 512, 16, n))


def unpack_weight(words, scales, fmt):
    g, _, n = scales.shape
    words = np.ascontiguousarray(words).reshape(g, 128, n, -1)
    if fmt == "e4m3":
        vals = words.view(ml_dtypes.float8_e4m3fn).astype(np.float64)
    else:
        nib = np.empty((g, 128, n, 4), np.uint8)
        nib[..., 0::2] = words & 0xF
        nib[..., 1::2] = words >> 4
        vals = E2M1[nib]
    vals = vals * np.repeat(np.exp2(scales.astype(np.float64) - 127.0), 8, axis=1)[..., None]
    return vals.transpose(0, 1, 3, 2).reshape(g * 512, n)


def gelu(v):
    return 0.5 * v * (1.0 + np.tanh(np.sqrt(2.0 / np.pi) * (v + 0.044715 * v**3)))


D, T, E, C, H, N = 2, 768, 12, 128, 512, 256


def by_expert(wq, xq):
    return np.concatenate([wq[e].T @ xq[:, e * C:(e + 1) * C] for e in range(E)], axis=1)


def setup_inputs():
    n = np.random.standard_normal
    s = np.tile(mx_kscale(H), D)
    u = mx_kscale(H)
    slot_sub = np.random.permutation(D * T)
    x = pack_weight(n((D * H, T)) * s[:, None], "e4m3")
    return {
        "x_words": x[0],
        "x_scales": x[1],
        "w": (n((E, H, H)) / np.sqrt(H) / s[None, :H, None] * u).astype(np.float32),
        "wm": (n((D * H, N)) / np.sqrt(D * H) / np.tile(u, D)[:, None]).astype(np.float32),
        "gate": np.tile(np.random.uniform(0.2, 1.0, E * C), (128, 1)).astype(np.float32),
        "offs": striped(slot_sub),
    }


def reference(x_words, x_scales, w, wm, gate, offs):
    wq = mxq(f64(w), 1, "e4m3")
    wmq = mxq(f64(wm), 0, "e4m3")
    idx = unstriped(offs)
    x = unpack_weight(x_words, x_scales, "e4m3")
    sub = x.reshape(D, H, T).transpose(1, 0, 2).reshape(H, D * T)
    y = gelu(by_expert(wq, sub[:, idx]))
    c = np.zeros((H, D * T))
    c[:, idx] = f64(gate[:1]) * y
    cq = mxq(c, 0, "e4m3").reshape(H, D, T).transpose(1, 0, 2).reshape(D * H, T)
    return wmq.T @ cq

@@ -1,0 +1,223 @@
+from contextlib import ExitStack
+
+import concourse.mybir as mybir
+
+D, T, E, C, H, N = 2, 768, 12, 128, 512, 256
+S = E * C
+FLOPS = 2 * H * H * S + 2 * D * H * N * T
+
+F32 = mybir.dt.float32
+BF16 = mybir.dt.bfloat16
+I32 = mybir.dt.int32
+U32 = mybir.dt.uint32
+U16 = mybir.dt.uint16
+U8 = mybir.dt.uint8
+FP8X4 = mybir.dt.float8_e4m3fn_x4
+GELU = mybir.ActivationFunctionType.Gelu_apprx_tanh
+MULT = mybir.AluOpType.mult
+
+P = 128
+PACK = 4
+SCALE_CUTS = [0,768,1536]
+GATHER_CUTS = [0,256,768,1536]
+GATHER_STEP = [1,2,3]
+PIECES = [[0,0,256],[2,0,192],[1,0,384],[3,0,512],[2,192,640],[0,256,768],[1,384,896],[3,512,1024],[2,640,1152],[0,768,1280],[1,896,1344],[0,1280,1536],[1,1344,1536],[3,1024,1536],[2,1152,1536]]
+TOKEN_CUTS = [0,128,384,640,768]
+LOAD_CUTS = [[0,256,512],[0,256,512],[0,512],[0,512],[0,512],[0,512],[0,512],[0,512],[0,512],[0,512],[0,512],[0,512]]
+CAST_ENG = [["s","s"],["s","s"],["s"],["s"],["s"],["s"],["s"],["s"],["s"],["s"],["s"],["s"]]
+GATE_CUTS = [0,512,1536]
+GATE_AFTER = [1,3]
+FUSED = False
+WM_STEP = 12
+WM_LOAD_AFTER = 11
+X_AFTER = 0
+
+
+def tile_moe_mhm_gelu_kernel(tc, x_words, x_scales, w, wm, gate, offs, out):
+    nc = tc.nc
+    with ExitStack() as ctx:
+        keep = ctx.enter_context(tc.tile_pool(name="keep", bufs=1))
+        ring = ctx.enter_context(tc.tile_pool(name="ring", bufs=3))
+        psum = ctx.enter_context(tc.psum_pool(name="psum", bufs=3))
+
+        offsets = keep.tile([P, S // 16], U16, name="offsets")
+        xw = keep.tile([P, D * T], I32, name="xw", align_bytes=64)
+        xs = keep.tile([P, D * T], U8, name="xs", align_bytes=64)
+        gs = keep.tile([P, S], U8, name="gs", align_bytes=64)
+        gate_sb = keep.tile([P, S], F32, name="gate_sb")
+        warm_in = keep.tile([P, 8], F32, name="warm_in")
+        warm_out = keep.tile([P, 8], F32, name="warm_out")
+        w_raw = [keep.tile([P, PACK, H], F32, name="w_raw%d" % e) for e in range(E)]
+        wm_raw = keep.tile([P, D, PACK, N], F32, name="wm_raw")
+        wm_bf = keep.tile([P, D, N, PACK], BF16, name="wm_bf", align_bytes=64)
+        wm_codes = keep.tile([P, D * N], U32, name="wm_codes", align_bytes=64)
+        wm_scales = keep.tile([P, D * N], U8, name="wm_scales", align_bytes=64)
+        acts = keep.tile([P, PACK, S], F32, name="acts")
+        win = [keep.tile([P, D * T], F32, name="win%d" % j) for j in range(PACK)]
+
+        nc.vector.memset(xs[:].bitcast(I32), 0)
+        nc.sync.dma_start(offsets[:], offs)
+        xs_words = xs[:].bitcast(I32).rearrange("p (o t) -> p o t", o=D)
+        scale_rows = x_scales.bitcast(I32).rearrange("o b t -> b o t")
+        for q in range(4):
+            nc.scalar.dma_start(out=xs_words[32 * q : 32 * q + 4, :, :], in_=scale_rows[4 * q : 4 * q + 4, :, :])
+        nc.vector.memset(warm_in[:], 0.0)
+        nc.scalar.activation(out=warm_out[:], in_=warm_in[:], func=GELU)
+
+        for e in range(-1, E):
+            if e >= 0:
+                src = w[e].rearrange("(p j) c -> p j c", j=PACK)
+                cuts = LOAD_CUTS[e]
+                for a, b in zip(cuts, cuts[1:]):
+                    nc.sync.dma_start(out=w_raw[e][:, :, a:b], in_=src[:, :, a:b])
+            if e == X_AFTER:
+                nc.sync.dma_start(
+                    out=xw[:].rearrange("p (o t) -> p o t", o=D),
+                    in_=x_words.rearrange("o p t d -> p o (t d)").bitcast(I32),
+                )
+            for k in range(len(GATE_AFTER)):
+                if GATE_AFTER[k] == e:
+                    nc.sync.dma_start(out=gate_sb[:, GATE_CUTS[k] : GATE_CUTS[k + 1]], in_=gate[:, GATE_CUTS[k] : GATE_CUTS[k + 1]])
+            if e == WM_LOAD_AFTER:
+                nc.sync.dma_start(
+                    out=wm_raw[:].rearrange("p o j n -> p o (j n)"),
+                    in_=wm.rearrange("(o p j) n -> p o (j n)", o=D, j=PACK),
+                )
+
+        def copy_on(eng, d, s):
+            if eng == "v":
+                nc.vector.tensor_copy(out=d, in_=s)
+            else:
+                nc.scalar.copy(out=d, in_=s)
+
+        for a, b in zip(SCALE_CUTS, SCALE_CUTS[1:]):
+            nc.vector.tensor_copy(out=gs[:, a:b], in_=xs[:].indirect(offsets[:, a // 16 : b // 16]))
+
+        gw = {}
+
+        def gather(k):
+            a, b = GATHER_CUTS[k], GATHER_CUTS[k + 1]
+            gw[k] = ring.tile([P, b - a], U32, name="gw", bufs=2, align_bytes=64)
+            nc.vector.tensor_copy(out=gw[k][:], in_=xw[:].bitcast(U32).indirect(offsets[:, a // 16 : b // 16]))
+
+        w_bf, w_codes, w_scales = {}, {}, {}
+
+        def cast_w(e):
+            w_bf[e] = ring.tile([P, PACK, P, PACK], BF16, name="w_bf", align_bytes=64)
+            cuts = LOAD_CUTS[e]
+            for k in range(len(cuts) - 1):
+                a, b = cuts[k], cuts[k + 1]
+                copy_on(
+                    CAST_ENG[e][k],
+                    w_bf[e][:, :, a // PACK : b // PACK, :].rearrange("p t m j -> p m j t"),
+                    w_raw[e][:, :, a:b].rearrange("p j (m t) -> p m j t", t=PACK),
+                )
+
+        def quant_w(e):
+            w_codes[e] = ring.tile([P, H], U32, name="w_codes", align_bytes=64)
+            w_scales[e] = ring.tile([P, H], U8, name="w_scales", align_bytes=64)
+            nc.vector.quantize_mx(
+                out=w_codes[e][:].bitcast(FP8X4), scales=w_scales[e][:], in_=w_bf[e][:].rearrange("p t m j -> p (t m j)")
+            )
+
+        def expert(e):
+            slots = slice(e * C, (e + 1) * C)
+            k = max(i for i in range(len(GATHER_CUTS)) if GATHER_CUTS[i] <= e * C)
+            words = gw[k][:, e * C - GATHER_CUTS[k] : (e + 1) * C - GATHER_CUTS[k]]
+            sums = psum.tile([P, PACK, C], F32, name="sums")
+            for t in range(PACK):
+                cols = slice(t * P, (t + 1) * P)
+                nc.tensor.matmul_mx(
+                    out=sums[:, t, :], lhsT=w_codes[e][:, cols].bitcast(FP8X4), lhsT_scale=w_scales[e][:, cols],
+                    rhs=words.bitcast(FP8X4), rhs_scale=gs[:, slots], start=True, stop=True,
+                )
+            nc.scalar.activation(out=acts[:, :, slots], in_=sums[:], func=GELU)
+            if not FUSED:
+                nc.vector.tensor_tensor(acts[:, :, slots], acts[:, :, slots], gate_sb[:, slots].unsqueeze(1).to_broadcast([P, PACK, C]), MULT)
+
+        def scatter(t, a, b):
+            lst = offsets[:, a // 16 : b // 16]
+            if FUSED:
+                nc.vector.tensor_tensor(win[t][:].indirect(lst), acts[:, t, a:b], gate_sb[:, a:b], MULT)
+            else:
+                nc.vector.tensor_copy(out=win[t][:].indirect(lst), in_=acts[:, t, a:b])
+
+        def cast_wm():
+            for o in range(D):
+                nc.scalar.copy(
+                    out=wm_bf[:, o, :, :].rearrange("p (c i) j -> p c j i", i=4),
+                    in_=wm_raw[:, o, :, :].rearrange("p j (c i) -> p c j i", i=4),
+                )
+
+        def quant_wm():
+            nc.vector.quantize_mx(
+                out=wm_codes[:].bitcast(FP8X4), scales=wm_scales[:], in_=wm_bf[:].rearrange("p o n j -> p (o n j)")
+            )
+
+        nch = len(TOKEN_CUTS) - 1
+        widths = [TOKEN_CUTS[k + 1] - TOKEN_CUTS[k] for k in range(nch)]
+        pairs = [keep.tile([P, 2, D, widths[k], 2], BF16, name="pairs%d" % k) for k in range(nch)]
+        c_bf = [keep.tile([P, D, widths[k], 2], F32, name="c_bf%d" % k, align_bytes=64) for k in range(nch)]
+        c_codes = [keep.tile([P, D * widths[k]], U32, name="c_codes%d" % k, align_bytes=64) for k in range(nch)]
+        c_scales = [keep.tile([P, D * widths[k]], U8, name="c_scales%d" % k, align_bytes=64) for k in range(nch)]
+        result = [keep.tile([P, 2, widths[k]], F32, name="result%d" % k) for k in range(nch)]
+        out_v = out.rearrange("(h p) t -> p h t", p=P)
+
+        def round_window(t):
+            for k in range(nch):
+                t0, t1 = TOKEN_CUTS[k], TOKEN_CUTS[k + 1]
+                nc.scalar.copy(
+                    out=pairs[k][:, t // 2, :, :, t % 2], in_=win[t][:].rearrange("p (o t) -> p o t", o=D)[:, :, t0:t1]
+                )
+
+        for step in range(E + 2):
+            if step < E:
+                cast_w(step)
+            if 0 <= step - 1 < E:
+                quant_w(step - 1)
+            for k in range(len(GATHER_STEP)):
+                if GATHER_STEP[k] == step:
+                    gather(k)
+            if 0 <= step - 1 < E:
+                expert(step - 1)
+            if step == WM_STEP:
+                cast_wm()
+            if step == WM_STEP + 1:
+                quant_wm()
+            for t, a, b in PIECES:
+                if (b - 1) // C == step - 2:
+                    scatter(t, a, b)
+                    if b == S:
+                        round_window(t)
+
+        def interleave(k):
+            words = pairs[k][:].rearrange("p u o t e -> p (u o t e)").bitcast(F32)
+            nc.vector.tensor_copy(
+                out=c_bf[k][:].rearrange("p o t u -> p (o t) u"), in_=words.rearrange("p (u z) -> p z u", u=2)
+            )
+
+        def merge(k):
+            t0, t1 = TOKEN_CUTS[k], TOKEN_CUTS[k + 1]
+            width = t1 - t0
+            nc.vector.quantize_mx(
+                out=c_codes[k][:].bitcast(FP8X4), scales=c_scales[k][:],
+                in_=c_bf[k][:].rearrange("p o t u -> p (o t u)").bitcast(BF16),
+            )
+            acc = psum.tile([P, 2, width], F32, name="acc", tag="acc")
+            for h in range(2):
+                for o in range(D):
+                    ncols = slice(o * N + h * P, o * N + (h + 1) * P)
+                    tcols = slice(o * width, (o + 1) * width)
+                    nc.tensor.matmul_mx(
+                        out=acc[:, h, :], lhsT=wm_codes[:, ncols].bitcast(FP8X4), lhsT_scale=wm_scales[:, ncols],
+                        rhs=c_codes[k][:, tcols].bitcast(FP8X4), rhs_scale=c_scales[k][:, tcols],
+                        start=(o == 0), stop=(o == D - 1),
+                    )
+            nc.scalar.copy(out=result[k][:], in_=acc[:])
+            nc.sync.dma_start(out=out_v[:, :, t0:t1], in_=result[k][:])
+
+        for step in range(nch + 1):
+            if step < nch:
+                interleave(step)
+            if step >= 1:
+                merge(step - 1)

@@ -19,18 +19,18 @@ MULT = mybir.AluOpType.mult
 P = 128
 PACK = 4
 SCALE_CUTS = [0,768,1536]
-GATHER_CUTS = [0,256,768,1536]
-GATHER_STEP = [1,2,3]
-PIECES = [[0,0,256],[2,0,192],[1,0,384],[3,0,512],[2,192,640],[0,256,768],[1,384,896],[3,512,1024],[2,640,1152],[0,768,1280],[1,896,1344],[0,1280,1536],[1,1344,1536],[3,1024,1536],[2,1152,1536]]
+GATHER_CUTS = [0,256,512,1024,1536]
+GATHER_STEP = [1,1,3,5]
+PIECES = [[0,0,256],[2,0,192],[1,0,192],[3,0,384],[1,192,512],[0,256,448],[2,192,640],[3,384,768],[1,512,896],[0,448,928],[3,768,1024],[2,640,1056],[0,928,1280],[1,896,1344],[0,1280,1536],[1,1344,1536],[3,1024,1536],[2,1056,1536]]
 TOKEN_CUTS = [0,128,384,640,768]
 LOAD_CUTS = [[0,256,512],[0,256,512],[0,512],[0,512],[0,512],[0,512],[0,512],[0,512],[0,512],[0,512],[0,512],[0,512]]
 CAST_ENG = [["s","s"],["s","s"],["s"],["s"],["s"],["s"],["s"],["s"],["s"],["s"],["s"],["s"]]
-GATE_CUTS = [0,512,1536]
-GATE_AFTER = [1,3]
-FUSED = False
+GATE_CUTS = [0,256,768,1536]
+GATE_AFTER = [1,2,5]
+FUSED = True
 WM_STEP = 12
 WM_LOAD_AFTER = 11
-X_AFTER = 0
+X_AFTER = 1
 
 
 def tile_moe_mhm_gelu_kernel(tc, x_words, x_scales, w, wm, gate, offs, out):
@@ -55,13 +55,13 @@ def tile_moe_mhm_gelu_kernel(tc, x_words, x_scales, w, wm, gate, offs, out):
         acts = keep.tile([P, PACK, S], F32, name="acts")
         win = [keep.tile([P, D * T], F32, name="win%d" % j) for j in range(PACK)]
 
-        nc.vector.memset(xs[:].bitcast(I32), 0)
+        nc.gpsimd.memset(xs[:].bitcast(I32), 0)
         nc.sync.dma_start(offsets[:], offs)
         xs_words = xs[:].bitcast(I32).rearrange("p (o t) -> p o t", o=D)
         scale_rows = x_scales.bitcast(I32).rearrange("o b t -> b o t")
         for q in range(4):
-            nc.scalar.dma_start(out=xs_words[32 * q : 32 * q + 4, :, :], in_=scale_rows[4 * q : 4 * q + 4, :, :])
-        nc.vector.memset(warm_in[:], 0.0)
+            nc.sync.dma_start(out=xs_words[32 * q : 32 * q + 4, :, :], in_=scale_rows[4 * q : 4 * q + 4, :, :])
+        nc.gpsimd.memset(warm_in[:], 0.0)
         nc.scalar.activation(out=warm_out[:], in_=warm_in[:], func=GELU)
 
         for e in range(-1, E):

@@ -20,17 +20,17 @@ P = 128
 PACK = 4
 SCALE_CUTS = [0,768,1536]
 GATHER_CUTS = [0,256,512,1024,1536]
-GATHER_STEP = [1,1,3,5]
-PIECES = [[0,0,256],[2,0,192],[1,0,192],[3,0,384],[1,192,512],[0,256,448],[2,192,640],[3,384,768],[1,512,896],[0,448,928],[3,768,1024],[2,640,1056],[0,928,1280],[1,896,1344],[0,1280,1536],[1,1344,1536],[3,1024,1536],[2,1056,1536]]
+GATHER_STEP = [0,0,0,2]
+PIECES = [[0,0,256],[2,0,256],[1,0,256],[3,0,384],[1,256,512],[0,256,448],[2,256,640],[3,384,768],[1,512,896],[0,448,928],[3,768,960],[2,640,1056],[0,928,1280],[1,896,1344],[1,1344,1536],[0,1280,1536],[3,960,1536],[2,1056,1536]]
 TOKEN_CUTS = [0,128,384,640,768]
-LOAD_CUTS = [[0,256,512],[0,256,512],[0,512],[0,512],[0,512],[0,512],[0,512],[0,512],[0,512],[0,512],[0,512],[0,512]]
-CAST_ENG = [["s","s"],["s","s"],["s"],["s"],["s"],["s"],["s"],["s"],["s"],["s"],["s"],["s"]]
+LOAD_CUTS = [[0,256,512],[0,256,384,512],[0,512],[0,512],[0,512],[0,512],[0,512],[0,512],[0,512],[0,512],[0,512],[0,512]]
+CAST_ENG = [["s","s"],["s","s","s"],["s"],["s"],["s"],["s"],["s"],["s"],["s"],["s"],["s"],["s"]]
 GATE_CUTS = [0,256,768,1536]
 GATE_AFTER = [1,2,5]
 FUSED = True
 WM_STEP = 12
 WM_LOAD_AFTER = 11
-X_AFTER = 1
+X_AFTER = -1
 
 
 def tile_moe_mhm_gelu_kernel(tc, x_words, x_scales, w, wm, gate, offs, out):
@@ -38,6 +38,7 @@ def tile_moe_mhm_gelu_kernel(tc, x_words, x_scales, w, wm, gate, offs, out):
     with ExitStack() as ctx:
         keep = ctx.enter_context(tc.tile_pool(name="keep", bufs=1))
         ring = ctx.enter_context(tc.tile_pool(name="ring", bufs=3))
+        late = ctx.enter_context(tc.tile_pool(name="late", bufs=1))
         psum = ctx.enter_context(tc.psum_pool(name="psum", bufs=3))
 
         offsets = keep.tile([P, S // 16], U16, name="offsets")
@@ -47,13 +48,12 @@ def tile_moe_mhm_gelu_kernel(tc, x_words, x_scales, w, wm, gate, offs, out):
         gate_sb = keep.tile([P, S], F32, name="gate_sb")
         warm_in = keep.tile([P, 8], F32, name="warm_in")
         warm_out = keep.tile([P, 8], F32, name="warm_out")
-        w_raw = [keep.tile([P, PACK, H], F32, name="w_raw%d" % e) for e in range(E)]
-        wm_raw = keep.tile([P, D, PACK, N], F32, name="wm_raw")
-        wm_bf = keep.tile([P, D, N, PACK], BF16, name="wm_bf", align_bytes=64)
+        w_raw = [late.tile([P, PACK, H], F32, name="w_raw0", tag="slot_c")]
+        w_raw += [keep.tile([P, PACK, H], F32, name="w_raw%d" % e) for e in range(1, E)]
         wm_codes = keep.tile([P, D * N], U32, name="wm_codes", align_bytes=64)
         wm_scales = keep.tile([P, D * N], U8, name="wm_scales", align_bytes=64)
         acts = keep.tile([P, PACK, S], F32, name="acts")
-        win = [keep.tile([P, D * T], F32, name="win%d" % j) for j in range(PACK)]
+        win = {j: keep.tile([P, D * T], F32, name="win%d" % j) for j in (0, 2, 3)}
 
         nc.gpsimd.memset(xs[:].bitcast(I32), 0)
         nc.sync.dma_start(offsets[:], offs)
@@ -78,11 +78,6 @@ def tile_moe_mhm_gelu_kernel(tc, x_words, x_scales, w, wm, gate, offs, out):
             for k in range(len(GATE_AFTER)):
                 if GATE_AFTER[k] == e:
                     nc.sync.dma_start(out=gate_sb[:, GATE_CUTS[k] : GATE_CUTS[k + 1]], in_=gate[:, GATE_CUTS[k] : GATE_CUTS[k + 1]])
-            if e == WM_LOAD_AFTER:
-                nc.sync.dma_start(
-                    out=wm_raw[:].rearrange("p o j n -> p o (j n)"),
-                    in_=wm.rearrange("(o p j) n -> p o (j n)", o=D, j=PACK),
-                )
 
         def copy_on(eng, d, s):
             if eng == "v":
@@ -97,13 +92,21 @@ def tile_moe_mhm_gelu_kernel(tc, x_words, x_scales, w, wm, gate, offs, out):
 
         def gather(k):
             a, b = GATHER_CUTS[k], GATHER_CUTS[k + 1]
-            gw[k] = ring.tile([P, b - a], U32, name="gw", bufs=2, align_bytes=64)
+            if k == len(GATHER_CUTS) - 2:
+                gw[k] = late.tile([P, b - a], U32, name="gw_last", tag="slot_a", align_bytes=64)
+            else:
+                gw[k] = keep.tile([P, b - a], U32, name="gw%d" % k, align_bytes=64)
             nc.vector.tensor_copy(out=gw[k][:], in_=xw[:].bitcast(U32).indirect(offsets[:, a // 16 : b // 16]))
 
         w_bf, w_codes, w_scales = {}, {}, {}
 
         def cast_w(e):
-            w_bf[e] = ring.tile([P, PACK, P, PACK], BF16, name="w_bf", align_bytes=64)
+            if e == 1:
+                w_bf[e] = late.tile([P, PACK, P, PACK], BF16, name="w_bf_1", tag="slot_a", align_bytes=64)
+            elif e == 2:
+                w_bf[e] = late.tile([P, PACK, P, PACK], BF16, name="w_bf_2", tag="slot_b", align_bytes=64)
+            else:
+                w_bf[e] = ring.tile([P, PACK, P, PACK], BF16, name="w_bf", align_bytes=64)
             cuts = LOAD_CUTS[e]
             for k in range(len(cuts) - 1):
                 a, b = cuts[k], cuts[k + 1]
@@ -114,7 +117,12 @@ def tile_moe_mhm_gelu_kernel(tc, x_words, x_scales, w, wm, gate, offs, out):
                 )
 
         def quant_w(e):
-            w_codes[e] = ring.tile([P, H], U32, name="w_codes", align_bytes=64)
+            if e == E - 1:
+                w_codes[e] = late.tile([P, H], U32, name="w_codes_last", tag="late", align_bytes=64)
+            elif e == 1:
+                w_codes[e] = late.tile([P, H], U32, name="w_codes_1", tag="slot_b", align_bytes=64)
+            else:
+                w_codes[e] = ring.tile([P, H], U32, name="w_codes", align_bytes=64)
             w_scales[e] = ring.tile([P, H], U8, name="w_scales", align_bytes=64)
             nc.vector.quantize_mx(
                 out=w_codes[e][:].bitcast(FP8X4), scales=w_scales[e][:], in_=w_bf[e][:].rearrange("p t m j -> p (t m j)")
@@ -137,12 +145,23 @@ def tile_moe_mhm_gelu_kernel(tc, x_words, x_scales, w, wm, gate, offs, out):
 
         def scatter(t, a, b):
             lst = offsets[:, a // 16 : b // 16]
+            if t not in win:
+                win[t] = late.tile([P, D * T], F32, name="win1", tag="slot_b", align_bytes=64)
             if FUSED:
                 nc.vector.tensor_tensor(win[t][:].indirect(lst), acts[:, t, a:b], gate_sb[:, a:b], MULT)
             else:
                 nc.vector.tensor_copy(out=win[t][:].indirect(lst), in_=acts[:, t, a:b])
 
+        wm_bfs = []
+
         def cast_wm():
+            wm_raw = late.tile([P, D, PACK, N], F32, name="wm_raw", tag="slot_c")
+            nc.sync.dma_start(
+                out=wm_raw[:].rearrange("p o j n -> p o (j n)"),
+                in_=wm.rearrange("(o p j) n -> p o (j n)", o=D, j=PACK),
+            )
+            wm_bf = late.tile([P, D, N, PACK], BF16, name="wm_bf", tag="late", align_bytes=64)
+            wm_bfs.append(wm_bf)
             for o in range(D):
                 nc.scalar.copy(
                     out=wm_bf[:, o, :, :].rearrange("p (c i) j -> p c j i", i=4),
@@ -151,12 +170,12 @@ def tile_moe_mhm_gelu_kernel(tc, x_words, x_scales, w, wm, gate, offs, out):
 
         def quant_wm():
             nc.vector.quantize_mx(
-                out=wm_codes[:].bitcast(FP8X4), scales=wm_scales[:], in_=wm_bf[:].rearrange("p o n j -> p (o n j)")
+                out=wm_codes[:].bitcast(FP8X4), scales=wm_scales[:], in_=wm_bfs[0][:].rearrange("p o n j -> p (o n j)")
             )
 
         nch = len(TOKEN_CUTS) - 1
         widths = [TOKEN_CUTS[k + 1] - TOKEN_CUTS[k] for k in range(nch)]
-        pairs = [keep.tile([P, 2, D, widths[k], 2], BF16, name="pairs%d" % k) for k in range(nch)]
+        pairs = keep.tile([P, 2, D, T, 2], BF16, name="pairs")
         c_bf = [keep.tile([P, D, widths[k], 2], F32, name="c_bf%d" % k, align_bytes=64) for k in range(nch)]
         c_codes = [keep.tile([P, D * widths[k]], U32, name="c_codes%d" % k, align_bytes=64) for k in range(nch)]
         c_scales = [keep.tile([P, D * widths[k]], U8, name="c_scales%d" % k, align_bytes=64) for k in range(nch)]
@@ -164,14 +183,14 @@ def tile_moe_mhm_gelu_kernel(tc, x_words, x_scales, w, wm, gate, offs, out):
         out_v = out.rearrange("(h p) t -> p h t", p=P)
 
         def round_window(t):
-            for k in range(nch):
-                t0, t1 = TOKEN_CUTS[k], TOKEN_CUTS[k + 1]
+            cuts = TOKEN_CUTS if t == PIECES[-1][0] else [0, T]
+            for t0, t1 in zip(cuts, cuts[1:]):
                 nc.scalar.copy(
-                    out=pairs[k][:, t // 2, :, :, t % 2], in_=win[t][:].rearrange("p (o t) -> p o t", o=D)[:, :, t0:t1]
+                    out=pairs[:, t // 2, :, t0:t1, t % 2], in_=win[t][:].rearrange("p (o t) -> p o t", o=D)[:, :, t0:t1]
                 )
 
         for step in range(E + 2):
-            if step < E:
+            if step < E and step != 2:
                 cast_w(step)
             if 0 <= step - 1 < E:
                 quant_w(step - 1)
@@ -180,21 +199,21 @@ def tile_moe_mhm_gelu_kernel(tc, x_words, x_scales, w, wm, gate, offs, out):
                     gather(k)
             if 0 <= step - 1 < E:
                 expert(step - 1)
+            if step == 2:
+                cast_w(step)
             if step == WM_STEP:
                 cast_wm()
-            if step == WM_STEP + 1:
-                quant_wm()
             for t, a, b in PIECES:
                 if (b - 1) // C == step - 2:
                     scatter(t, a, b)
                     if b == S:
                         round_window(t)
 
-        def interleave(k):
-            words = pairs[k][:].rearrange("p u o t e -> p (u o t e)").bitcast(F32)
-            nc.vector.tensor_copy(
-                out=c_bf[k][:].rearrange("p o t u -> p (o t) u"), in_=words.rearrange("p (u z) -> p z u", u=2)
-            )
+        quant_wm()
+
+        def interleave(k, eng):
+            words = pairs[:].rearrange("p u o t e -> p (u o t e)").bitcast(F32).rearrange("p (u o t) -> p o t u", u=2, o=D)
+            copy_on(eng, c_bf[k][:], words[:, :, TOKEN_CUTS[k] : TOKEN_CUTS[k + 1], :])
 
         def merge(k):
             t0, t1 = TOKEN_CUTS[k], TOKEN_CUTS[k + 1]
@@ -216,8 +235,33 @@ def tile_moe_mhm_gelu_kernel(tc, x_words, x_scales, w, wm, gate, offs, out):
             nc.scalar.copy(out=result[k][:], in_=acc[:])
             nc.sync.dma_start(out=out_v[:, :, t0:t1], in_=result[k][:])
 
-        for step in range(nch + 1):
-            if step < nch:
-                interleave(step)
+        def last_chunk():
+            k = nch - 1
+            t0, t1 = TOKEN_CUTS[k], TOKEN_CUTS[k + 1]
+            width = t1 - t0
+            accs = [psum.tile([P, width], F32, name="acc_last%d" % h, tag="last", bufs=2) for h in range(2)]
+            for o in range(D):
+                tcols = slice(o * width, (o + 1) * width)
+                nc.vector.quantize_mx(
+                    out=c_codes[k][:, tcols].bitcast(FP8X4), scales=c_scales[k][:, tcols],
+                    in_=c_bf[k][:, o, :, :].rearrange("p t u -> p (t u)").bitcast(BF16),
+                )
+                for h in range(2):
+                    ncols = slice(o * N + h * P, o * N + (h + 1) * P)
+                    nc.tensor.matmul_mx(
+                        out=accs[h][:], lhsT=wm_codes[:, ncols].bitcast(FP8X4), lhsT_scale=wm_scales[:, ncols],
+                        rhs=c_codes[k][:, tcols].bitcast(FP8X4), rhs_scale=c_scales[k][:, tcols],
+                        start=(o == 0), stop=(o == D - 1),
+                    )
+            nc.scalar.copy(out=result[k][:, 0, :], in_=accs[0][:])
+            nc.sync.dma_start(out=out_v[:, 0, t0:t1], in_=result[k][:, 0, :])
+            nc.vector.tensor_copy(out=result[k][:, 1, :], in_=accs[1][:])
+            nc.sync.dma_start(out=out_v[:, 1, t0:t1], in_=result[k][:, 1, :])
+
+        interleave(nch - 1, "s")
+        for step in range(nch):
+            if step < nch - 1:
+                interleave(step, "v")
             if step >= 1:
                 merge(step - 1)
+        last_chunk()

@@ -21,7 +21,7 @@ PACK = 4
 SCALE_CUTS = [0,768,1536]
 GATHER_CUTS = [0,256,512,1024,1536]
 GATHER_STEP = [0,0,0,2]
-PIECES = [[0,0,256],[2,0,256],[1,0,256],[3,0,384],[1,256,512],[0,256,448],[2,256,640],[3,384,768],[1,512,896],[0,448,928],[3,768,960],[2,640,1056],[0,928,1280],[1,896,1344],[1,1344,1536],[0,1280,1536],[3,960,1536],[2,1056,1536]]
+PIECES = [[0,0,256],[2,0,192],[1,0,256],[3,0,384],[2,192,512],[0,256,448],[1,256,640],[3,384,768],[0,448,896],[2,512,960],[1,640,1088],[3,768,1216],[0,896,1344],[0,1344,1536],[3,1216,1536],[1,1088,1536],[2,960,1536]]
 TOKEN_CUTS = [0,128,384,640,768]
 LOAD_CUTS = [[0,256,512],[0,256,384,512],[0,512],[0,512],[0,512],[0,512],[0,512],[0,512],[0,512],[0,512],[0,512],[0,512]]
 CAST_ENG = [["s","s"],["s","s","s"],["s"],["s"],["s"],["s"],["s"],["s"],["s"],["s"],["s"],["s"]]

@@ -210,6 +210,12 @@ def tile_moe_mhm_gelu_kernel(tc, x_words, x_scales, w, wm, gate, offs, out):
                         round_window(t)
 
         quant_wm()
+        warm_ps = psum.tile([P, PACK * C], F32, name="warm_ps", tag="sums")
+        for rep in range(3):
+            nc.tensor.matmul_mx(
+                out=warm_ps[:], lhsT=wm_codes[:, 0:P].bitcast(FP8X4), lhsT_scale=wm_scales[:, 0:P],
+                rhs=wm_codes[:].bitcast(FP8X4), rhs_scale=wm_scales[:], start=True, stop=True,
+            )
 
         def interleave(k, eng):
             words = pairs[:].rearrange("p u o t e -> p (u o t e)").bitcast(F32).rearrange("p (u o t) -> p o t u", u=2, o=D)

@@ -18,19 +18,13 @@ MULT = mybir.AluOpType.mult
 
 P = 128
 PACK = 4
-SCALE_CUTS = [0,768,1536]
-GATHER_CUTS = [0,256,512,1024,1536]
-GATHER_STEP = [0,0,0,2]
-PIECES = [[0,0,256],[2,0,192],[1,0,256],[3,0,384],[2,192,512],[0,256,448],[1,256,640],[3,384,768],[0,448,896],[2,512,960],[1,640,1088],[3,768,1216],[0,896,1344],[0,1344,1536],[3,1216,1536],[1,1088,1536],[2,960,1536]]
-TOKEN_CUTS = [0,128,384,640,768]
-LOAD_CUTS = [[0,256,512],[0,256,384,512],[0,512],[0,512],[0,512],[0,512],[0,512],[0,512],[0,512],[0,512],[0,512],[0,512]]
-CAST_ENG = [["s","s"],["s","s","s"],["s"],["s"],["s"],["s"],["s"],["s"],["s"],["s"],["s"],["s"]]
-GATE_CUTS = [0,256,768,1536]
-GATE_AFTER = [1,2,5]
-FUSED = True
-WM_STEP = 12
-WM_LOAD_AFTER = 11
-X_AFTER = -1
+SCALE_CUTS = [0, 768, 1536]
+GATHER_CUTS = [0, 256, 768, 1536]
+TOKEN_CUTS = [0, 128, 384, 640, 768]
+GATE_CUTS = [0, 256, 768, 1536]
+GATE_AFTER = [1, 2, 5]
+LOAD_CUTS = [[0, 256, 512], [0, 256, 384, 512]] + [[0, 512]] * (E - 2)
+CUTS = [[0, 192, 384, 640, 896, 1152, 1344, 1536], [0, 256, 512, 768, 1024, 1280, 1536]]
 
 
 def tile_moe_mhm_gelu_kernel(tc, x_words, x_scales, w, wm, gate, offs, out):
@@ -38,7 +32,6 @@ def tile_moe_mhm_gelu_kernel(tc, x_words, x_scales, w, wm, gate, offs, out):
     with ExitStack() as ctx:
         keep = ctx.enter_context(tc.tile_pool(name="keep", bufs=1))
         ring = ctx.enter_context(tc.tile_pool(name="ring", bufs=3))
-        late = ctx.enter_context(tc.tile_pool(name="late", bufs=1))
         psum = ctx.enter_context(tc.psum_pool(name="psum", bufs=3))
 
         offsets = keep.tile([P, S // 16], U16, name="offsets")
@@ -48,15 +41,22 @@ def tile_moe_mhm_gelu_kernel(tc, x_words, x_scales, w, wm, gate, offs, out):
         gate_sb = keep.tile([P, S], F32, name="gate_sb")
         warm_in = keep.tile([P, 8], F32, name="warm_in")
         warm_out = keep.tile([P, 8], F32, name="warm_out")
-        w_raw = [late.tile([P, PACK, H], F32, name="w_raw0", tag="slot_c")]
-        w_raw += [keep.tile([P, PACK, H], F32, name="w_raw%d" % e) for e in range(1, E)]
+        w_raw = [keep.tile([P, PACK, H], F32, name="w_raw%d" % e) for e in range(E)]
+        wm_raw = keep.tile([P, D, PACK, N], F32, name="wm_raw")
+        wm_bf = keep.tile([P, D, N, PACK], BF16, name="wm_bf", align_bytes=64)
         wm_codes = keep.tile([P, D * N], U32, name="wm_codes", align_bytes=64)
         wm_scales = keep.tile([P, D * N], U8, name="wm_scales", align_bytes=64)
-        acts = keep.tile([P, PACK, S], F32, name="acts")
-        win = {j: keep.tile([P, D * T], F32, name="win%d" % j) for j in (0, 2, 3)}
+        gated = [keep.tile([P, S], F32, name="gated%d" % u) for u in range(2)]
+        win = [keep.tile([P, D * T], F32, name="win%d" % u) for u in range(2)]
+        both = keep.tile([P, 2, D, T], F32, name="both")
+
+        def load_w(e, k):
+            a, b = LOAD_CUTS[e][k], LOAD_CUTS[e][k + 1]
+            nc.sync.dma_start(out=w_raw[e][:, :, a:b], in_=w[e].rearrange("(p j) c -> p j c", j=PACK)[:, :, a:b])
 
         nc.gpsimd.memset(xs[:].bitcast(I32), 0)
         nc.sync.dma_start(offsets[:], offs)
+        load_w(0, 0)
         xs_words = xs[:].bitcast(I32).rearrange("p (o t) -> p o t", o=D)
         scale_rows = x_scales.bitcast(I32).rearrange("o b t -> b o t")
         for q in range(4):
@@ -64,13 +64,10 @@ def tile_moe_mhm_gelu_kernel(tc, x_words, x_scales, w, wm, gate, offs, out):
         nc.gpsimd.memset(warm_in[:], 0.0)
         nc.scalar.activation(out=warm_out[:], in_=warm_in[:], func=GELU)
 
-        for e in range(-1, E):
-            if e >= 0:
-                src = w[e].rearrange("(p j) c -> p j c", j=PACK)
-                cuts = LOAD_CUTS[e]
-                for a, b in zip(cuts, cuts[1:]):
-                    nc.sync.dma_start(out=w_raw[e][:, :, a:b], in_=src[:, :, a:b])
-            if e == X_AFTER:
+        for e in range(E):
+            for k in range(1 if e == 0 else 0, len(LOAD_CUTS[e]) - 1):
+                load_w(e, k)
+            if e == 0:
                 nc.sync.dma_start(
                     out=xw[:].rearrange("p (o t) -> p o t", o=D),
                     in_=x_words.rearrange("o p t d -> p o (t d)").bitcast(I32),
@@ -78,6 +75,10 @@ def tile_moe_mhm_gelu_kernel(tc, x_words, x_scales, w, wm, gate, offs, out):
             for k in range(len(GATE_AFTER)):
                 if GATE_AFTER[k] == e:
                     nc.sync.dma_start(out=gate_sb[:, GATE_CUTS[k] : GATE_CUTS[k + 1]], in_=gate[:, GATE_CUTS[k] : GATE_CUTS[k + 1]])
+        nc.sync.dma_start(
+            out=wm_raw[:].rearrange("p o j n -> p o (j n)"),
+            in_=wm.rearrange("(o p j) n -> p o (j n)", o=D, j=PACK),
+        )
 
         def copy_on(eng, d, s):
             if eng == "v":
@@ -92,37 +93,24 @@ def tile_moe_mhm_gelu_kernel(tc, x_words, x_scales, w, wm, gate, offs, out):
 
         def gather(k):
             a, b = GATHER_CUTS[k], GATHER_CUTS[k + 1]
-            if k == len(GATHER_CUTS) - 2:
-                gw[k] = late.tile([P, b - a], U32, name="gw_last", tag="slot_a", align_bytes=64)
-            else:
-                gw[k] = keep.tile([P, b - a], U32, name="gw%d" % k, align_bytes=64)
+            gw[k] = keep.tile([P, b - a], U32, name="gw%d" % k, align_bytes=64)
             nc.vector.tensor_copy(out=gw[k][:], in_=xw[:].bitcast(U32).indirect(offsets[:, a // 16 : b // 16]))
 
-        w_bf, w_codes, w_scales = {}, {}, {}
+        w_bf, w_codes, w_scales, acts = {}, {}, {}, {}
 
         def cast_w(e):
-            if e == 1:
-                w_bf[e] = late.tile([P, PACK, P, PACK], BF16, name="w_bf_1", tag="slot_a", align_bytes=64)
-            elif e == 2:
-                w_bf[e] = late.tile([P, PACK, P, PACK], BF16, name="w_bf_2", tag="slot_b", align_bytes=64)
-            else:
-                w_bf[e] = ring.tile([P, PACK, P, PACK], BF16, name="w_bf", align_bytes=64)
+            w_bf[e] = ring.tile([P, PACK, P, PACK], BF16, name="w_bf", align_bytes=64)
             cuts = LOAD_CUTS[e]
             for k in range(len(cuts) - 1):
                 a, b = cuts[k], cuts[k + 1]
                 copy_on(
-                    CAST_ENG[e][k],
+                    "s",
                     w_bf[e][:, :, a // PACK : b // PACK, :].rearrange("p t m j -> p m j t"),
                     w_raw[e][:, :, a:b].rearrange("p j (m t) -> p m j t", t=PACK),
                 )
 
         def quant_w(e):
-            if e == E - 1:
-                w_codes[e] = late.tile([P, H], U32, name="w_codes_last", tag="late", align_bytes=64)
-            elif e == 1:
-                w_codes[e] = late.tile([P, H], U32, name="w_codes_1", tag="slot_b", align_bytes=64)
-            else:
-                w_codes[e] = ring.tile([P, H], U32, name="w_codes", align_bytes=64)
+            w_codes[e] = ring.tile([P, H], U32, name="w_codes", align_bytes=64)
             w_scales[e] = ring.tile([P, H], U8, name="w_scales", align_bytes=64)
             nc.vector.quantize_mx(
                 out=w_codes[e][:].bitcast(FP8X4), scales=w_scales[e][:], in_=w_bf[e][:].rearrange("p t m j -> p (t m j)")
@@ -139,29 +127,18 @@ def tile_moe_mhm_gelu_kernel(tc, x_words, x_scales, w, wm, gate, offs, out):
                     out=sums[:, t, :], lhsT=w_codes[e][:, cols].bitcast(FP8X4), lhsT_scale=w_scales[e][:, cols],
                     rhs=words.bitcast(FP8X4), rhs_scale=gs[:, slots], start=True, stop=True,
                 )
-            nc.scalar.activation(out=acts[:, :, slots], in_=sums[:], func=GELU)
-            if not FUSED:
-                nc.vector.tensor_tensor(acts[:, :, slots], acts[:, :, slots], gate_sb[:, slots].unsqueeze(1).to_broadcast([P, PACK, C]), MULT)
+            acts[e] = ring.tile([P, 2, C, 2], F32, name="acts")
+            nc.scalar.activation(out=acts[e][:], in_=sums[:].rearrange("p (u v) s -> p u s v", u=2), func=GELU)
 
-        def scatter(t, a, b):
-            lst = offsets[:, a // 16 : b // 16]
-            if t not in win:
-                win[t] = late.tile([P, D * T], F32, name="win1", tag="slot_b", align_bytes=64)
-            if FUSED:
-                nc.vector.tensor_tensor(win[t][:].indirect(lst), acts[:, t, a:b], gate_sb[:, a:b], MULT)
-            else:
-                nc.vector.tensor_copy(out=win[t][:].indirect(lst), in_=acts[:, t, a:b])
+        def apply_gate(e, u):
+            slots = slice(e * C, (e + 1) * C)
+            pairs = gated[u][:, slots].bitcast(BF16).rearrange("p (s v) -> p s v", v=2)
+            nc.vector.tensor_tensor(pairs, acts[e][:, u, :, :], gate_sb[:, slots].unsqueeze(2).to_broadcast([P, C, 2]), MULT)
 
-        wm_bfs = []
+        def scatter(u, a, b):
+            nc.vector.tensor_copy(out=win[u][:].indirect(offsets[:, a // 16 : b // 16]), in_=gated[u][:, a:b])
 
         def cast_wm():
-            wm_raw = late.tile([P, D, PACK, N], F32, name="wm_raw", tag="slot_c")
-            nc.sync.dma_start(
-                out=wm_raw[:].rearrange("p o j n -> p o (j n)"),
-                in_=wm.rearrange("(o p j) n -> p o (j n)", o=D, j=PACK),
-            )
-            wm_bf = late.tile([P, D, N, PACK], BF16, name="wm_bf", tag="late", align_bytes=64)
-            wm_bfs.append(wm_bf)
             for o in range(D):
                 nc.scalar.copy(
                     out=wm_bf[:, o, :, :].rearrange("p (c i) j -> p c j i", i=4),
@@ -170,44 +147,40 @@ def tile_moe_mhm_gelu_kernel(tc, x_words, x_scales, w, wm, gate, offs, out):
 
         def quant_wm():
             nc.vector.quantize_mx(
-                out=wm_codes[:].bitcast(FP8X4), scales=wm_scales[:], in_=wm_bfs[0][:].rearrange("p o n j -> p (o n j)")
+                out=wm_codes[:].bitcast(FP8X4), scales=wm_scales[:], in_=wm_bf[:].rearrange("p o n j -> p (o n j)")
             )
 
         nch = len(TOKEN_CUTS) - 1
         widths = [TOKEN_CUTS[k + 1] - TOKEN_CUTS[k] for k in range(nch)]
-        pairs = keep.tile([P, 2, D, T, 2], BF16, name="pairs")
         c_bf = [keep.tile([P, D, widths[k], 2], F32, name="c_bf%d" % k, align_bytes=64) for k in range(nch)]
         c_codes = [keep.tile([P, D * widths[k]], U32, name="c_codes%d" % k, align_bytes=64) for k in range(nch)]
         c_scales = [keep.tile([P, D * widths[k]], U8, name="c_scales%d" % k, align_bytes=64) for k in range(nch)]
         result = [keep.tile([P, 2, widths[k]], F32, name="result%d" % k) for k in range(nch)]
         out_v = out.rearrange("(h p) t -> p h t", p=P)
 
-        def round_window(t):
-            cuts = TOKEN_CUTS if t == PIECES[-1][0] else [0, T]
-            for t0, t1 in zip(cuts, cuts[1:]):
-                nc.scalar.copy(
-                    out=pairs[:, t // 2, :, t0:t1, t % 2], in_=win[t][:].rearrange("p (o t) -> p o t", o=D)[:, :, t0:t1]
-                )
-
-        for step in range(E + 2):
-            if step < E and step != 2:
+        for k in range(len(GATHER_CUTS) - 1):
+            gather(k)
+        for step in range(E + 3):
+            if step < E:
                 cast_w(step)
             if 0 <= step - 1 < E:
                 quant_w(step - 1)
-            for k in range(len(GATHER_STEP)):
-                if GATHER_STEP[k] == step:
-                    gather(k)
-            if 0 <= step - 1 < E:
                 expert(step - 1)
-            if step == 2:
-                cast_w(step)
-            if step == WM_STEP:
+            if step == E:
                 cast_wm()
-            for t, a, b in PIECES:
-                if (b - 1) // C == step - 2:
-                    scatter(t, a, b)
-                    if b == S:
-                        round_window(t)
+            if 0 <= step - 2 < E:
+                e = step - 2
+                first = 0 if e == E - 1 else e % 2
+                for u in (first, 1 - first):
+                    apply_gate(e, u)
+                for u in (first, 1 - first):
+                    for a, b in zip(CUTS[u], CUTS[u][1:]):
+                        if (b - 1) // C == e:
+                            scatter(u, a, b)
+
+        nc.scalar.copy(out=both[:, 0, :, :], in_=win[0][:].rearrange("p (o t) -> p o t", o=D))
+        for t0, t1 in zip(TOKEN_CUTS, TOKEN_CUTS[1:]):
+            nc.scalar.copy(out=both[:, 1, :, t0:t1], in_=win[1][:].rearrange("p (o t) -> p o t", o=D)[:, :, t0:t1])
 
         quant_wm()
         warm_ps = psum.tile([P, PACK * C], F32, name="warm_ps", tag="sums")
@@ -218,8 +191,7 @@ def tile_moe_mhm_gelu_kernel(tc, x_words, x_scales, w, wm, gate, offs, out):
             )
 
         def interleave(k, eng):
-            words = pairs[:].rearrange("p u o t e -> p (u o t e)").bitcast(F32).rearrange("p (u o t) -> p o t u", u=2, o=D)
-            copy_on(eng, c_bf[k][:], words[:, :, TOKEN_CUTS[k] : TOKEN_CUTS[k + 1], :])
+            copy_on(eng, c_bf[k][:], both[:, :, :, TOKEN_CUTS[k] : TOKEN_CUTS[k + 1]].rearrange("p u o t -> p o t u"))
 
         def merge(k):
             t0, t1 = TOKEN_CUTS[k], TOKEN_CUTS[k + 1]
@@ -264,10 +236,8 @@ def tile_moe_mhm_gelu_kernel(tc, x_words, x_scales, w, wm, gate, offs, out):
             nc.vector.tensor_copy(out=result[k][:, 1, :], in_=accs[1][:])
             nc.sync.dma_start(out=out_v[:, 1, t0:t1], in_=result[k][:, 1, :])
 
-        interleave(nch - 1, "s")
         for step in range(nch):
-            if step < nch - 1:
-                interleave(step, "v")
+            interleave(step, "v")
             if step >= 1:
                 merge(step - 1)
         last_chunk()

@@ -1,6 +1,7 @@
 from contextlib import ExitStack
 
 import concourse.mybir as mybir
+from concourse.masks import make_identity
 
 D, T, E, C, H, N = 2, 768, 12, 128, 512, 256
 S = E * C
@@ -20,11 +21,25 @@ P = 128
 PACK = 4
 SCALE_CUTS = [0, 768, 1536]
 GATHER_CUTS = [0, 256, 768, 1536]
-TOKEN_CUTS = [0, 128, 384, 640, 768]
-GATE_CUTS = [0, 256, 768, 1536]
-GATE_AFTER = [1, 2, 5]
+TOKEN_CUTS = [0, 128, 384, 512, 640, 768]
+GATHER_AFTER = [None, 1, 2]
+W1_V = 1
+V_TURNS = []
+V2 = 192
+EARLY = [1]
+RES_ENG = "ssss"
+W0_FIRST = True
+X_AFTER = 0
+ACT_AFTER = [0, 1]
+WM_AFTER = 10
+WM_COLS = 256
+V_TO = 12
+AHEAD = 3
+S_CHUNKS = [2]
+V_COLS = 96
+V_FROM = 2
 LOAD_CUTS = [[0, 256, 512], [0, 256, 384, 512]] + [[0, 512]] * (E - 2)
-CUTS = [[0, 192, 384, 640, 896, 1152, 1344, 1536], [0, 256, 512, 768, 1024, 1280, 1536]]
+CUTS = [[0, 256, 512, 768, 1024, 1280, 1536], [0, 192, 384, 640, 896, 1152, 1344, 1536]]
 
 
 def tile_moe_mhm_gelu_kernel(tc, x_words, x_scales, w, wm, gate, offs, out):
@@ -32,21 +47,22 @@ def tile_moe_mhm_gelu_kernel(tc, x_words, x_scales, w, wm, gate, offs, out):
     with ExitStack() as ctx:
         keep = ctx.enter_context(tc.tile_pool(name="keep", bufs=1))
         ring = ctx.enter_context(tc.tile_pool(name="ring", bufs=3))
+        shared = ctx.enter_context(tc.tile_pool(name="shared", bufs=1))
         psum = ctx.enter_context(tc.psum_pool(name="psum", bufs=3))
 
         offsets = keep.tile([P, S // 16], U16, name="offsets")
         xw = keep.tile([P, D * T], I32, name="xw", align_bytes=64)
         xs = keep.tile([P, D * T], U8, name="xs", align_bytes=64)
         gs = keep.tile([P, S], U8, name="gs", align_bytes=64)
-        gate_sb = keep.tile([P, S], F32, name="gate_sb")
+        gate_rows = keep.tile([P, C], F32, name="gate_rows")
+        gate_cols = keep.tile([P, E], F32, name="gate_cols")
+        ident = keep.tile([P, P], F32, name="ident")
         warm_in = keep.tile([P, 8], F32, name="warm_in")
         warm_out = keep.tile([P, 8], F32, name="warm_out")
-        w_raw = [keep.tile([P, PACK, H], F32, name="w_raw%d" % e) for e in range(E)]
+        w_raw = [shared.tile([P, PACK, H], F32, name="w_raw%d" % e, tag="raw%d" % e) for e in range(E)]
         wm_raw = keep.tile([P, D, PACK, N], F32, name="wm_raw")
-        wm_bf = keep.tile([P, D, N, PACK], BF16, name="wm_bf", align_bytes=64)
-        wm_codes = keep.tile([P, D * N], U32, name="wm_codes", align_bytes=64)
         wm_scales = keep.tile([P, D * N], U8, name="wm_scales", align_bytes=64)
-        gated = [keep.tile([P, S], F32, name="gated%d" % u) for u in range(2)]
+        turned = shared.tile([P, 2, S], F32, name="turned", tag="turned", align_bytes=64)
         win = [keep.tile([P, D * T], F32, name="win%d" % u) for u in range(2)]
         both = keep.tile([P, 2, D, T], F32, name="both")
 
@@ -54,31 +70,36 @@ def tile_moe_mhm_gelu_kernel(tc, x_words, x_scales, w, wm, gate, offs, out):
             a, b = LOAD_CUTS[e][k], LOAD_CUTS[e][k + 1]
             nc.sync.dma_start(out=w_raw[e][:, :, a:b], in_=w[e].rearrange("(p j) c -> p j c", j=PACK)[:, :, a:b])
 
-        nc.gpsimd.memset(xs[:].bitcast(I32), 0)
+        nc.vector.memset(xs[:].bitcast(I32), 0)
+        nc.vector.memset(gate_rows[:], 0.0)
         nc.sync.dma_start(offsets[:], offs)
-        load_w(0, 0)
+        if W0_FIRST:
+            load_w(0, 0)
         xs_words = xs[:].bitcast(I32).rearrange("p (o t) -> p o t", o=D)
         scale_rows = x_scales.bitcast(I32).rearrange("o b t -> b o t")
         for q in range(4):
             nc.sync.dma_start(out=xs_words[32 * q : 32 * q + 4, :, :], in_=scale_rows[4 * q : 4 * q + 4, :, :])
+        nc.sync.dma_start(out=gate_rows[0:E, :], in_=gate[0].rearrange("(e s) -> e s", s=C))
         nc.gpsimd.memset(warm_in[:], 0.0)
+        make_identity(nc, ident[:])
         nc.scalar.activation(out=warm_out[:], in_=warm_in[:], func=GELU)
 
         for e in range(E):
-            for k in range(1 if e == 0 else 0, len(LOAD_CUTS[e]) - 1):
+            for k in range(1 if e == 0 and W0_FIRST else 0, len(LOAD_CUTS[e]) - 1):
                 load_w(e, k)
-            if e == 0:
+            if e == X_AFTER:
                 nc.sync.dma_start(
                     out=xw[:].rearrange("p (o t) -> p o t", o=D),
                     in_=x_words.rearrange("o p t d -> p o (t d)").bitcast(I32),
                 )
-            for k in range(len(GATE_AFTER)):
-                if GATE_AFTER[k] == e:
-                    nc.sync.dma_start(out=gate_sb[:, GATE_CUTS[k] : GATE_CUTS[k + 1]], in_=gate[:, GATE_CUTS[k] : GATE_CUTS[k + 1]])
         nc.sync.dma_start(
             out=wm_raw[:].rearrange("p o j n -> p o (j n)"),
             in_=wm.rearrange("(o p j) n -> p o (j n)", o=D, j=PACK),
         )
+
+        gate_ps = psum.tile([P, P], F32, name="gate_ps", tag="acc")
+        nc.tensor.transpose(gate_ps[:], gate_rows[:], ident[:])
+        nc.scalar.copy(out=gate_cols[:], in_=gate_ps[:, 0:E])
 
         def copy_on(eng, d, s):
             if eng == "v":
@@ -93,59 +114,76 @@ def tile_moe_mhm_gelu_kernel(tc, x_words, x_scales, w, wm, gate, offs, out):
 
         def gather(k):
             a, b = GATHER_CUTS[k], GATHER_CUTS[k + 1]
-            gw[k] = keep.tile([P, b - a], U32, name="gw%d" % k, align_bytes=64)
+            gw[k] = shared.tile([P, b - a], U32, name="gw%d" % k, tag="after%d" % (GATHER_AFTER[k] or 0), align_bytes=64)
             nc.vector.tensor_copy(out=gw[k][:], in_=xw[:].bitcast(U32).indirect(offsets[:, a // 16 : b // 16]))
 
         w_bf, w_codes, w_scales, acts = {}, {}, {}, {}
 
         def cast_w(e):
-            w_bf[e] = ring.tile([P, PACK, P, PACK], BF16, name="w_bf", align_bytes=64)
-            cuts = LOAD_CUTS[e]
+            if e in GATHER_AFTER:
+                w_bf[e] = shared.tile([P, H, PACK], BF16, name="w_bf%d" % e, tag="after%d" % e, align_bytes=64)
+            else:
+                w_bf[e] = ring.tile([P, H, PACK], BF16, name="w_bf", align_bytes=64)
+            cuts = LOAD_CUTS[e] if e < V_FROM or e >= V_TO else [0, H - (V2 if e == 2 else V_COLS), H]
             for k in range(len(cuts) - 1):
                 a, b = cuts[k], cuts[k + 1]
                 copy_on(
-                    "s",
-                    w_bf[e][:, :, a // PACK : b // PACK, :].rearrange("p t m j -> p m j t"),
-                    w_raw[e][:, :, a:b].rearrange("p j (m t) -> p m j t", t=PACK),
+                    "v" if (e >= V_FROM and k == 1) or (e == 1 and k >= W1_V) else "s",
+                    w_bf[e][:, a:b, :].rearrange("p (c i) j -> p c j i", i=4),
+                    w_raw[e][:, :, a:b].rearrange("p j (c i) -> p c j i", i=4),
                 )
 
         def quant_w(e):
             w_codes[e] = ring.tile([P, H], U32, name="w_codes", align_bytes=64)
             w_scales[e] = ring.tile([P, H], U8, name="w_scales", align_bytes=64)
             nc.vector.quantize_mx(
-                out=w_codes[e][:].bitcast(FP8X4), scales=w_scales[e][:], in_=w_bf[e][:].rearrange("p t m j -> p (t m j)")
+                out=w_codes[e][:].bitcast(FP8X4), scales=w_scales[e][:], in_=w_bf[e][:].rearrange("p c j -> p (c j)")
             )
 
         def expert(e):
             slots = slice(e * C, (e + 1) * C)
             k = max(i for i in range(len(GATHER_CUTS)) if GATHER_CUTS[i] <= e * C)
             words = gw[k][:, e * C - GATHER_CUTS[k] : (e + 1) * C - GATHER_CUTS[k]]
-            sums = psum.tile([P, PACK, C], F32, name="sums")
-            for t in range(PACK):
-                cols = slice(t * P, (t + 1) * P)
-                nc.tensor.matmul_mx(
-                    out=sums[:, t, :], lhsT=w_codes[e][:, cols].bitcast(FP8X4), lhsT_scale=w_scales[e][:, cols],
-                    rhs=words.bitcast(FP8X4), rhs_scale=gs[:, slots], start=True, stop=True,
-                )
-            acts[e] = ring.tile([P, 2, C, 2], F32, name="acts")
-            nc.scalar.activation(out=acts[e][:], in_=sums[:].rearrange("p (u v) s -> p u s v", u=2), func=GELU)
+            sums = psum.tile([P, H], F32, name="sums")
+            nc.tensor.matmul_mx(
+                out=sums[:], lhsT=words.bitcast(FP8X4), lhsT_scale=gs[:, slots],
+                rhs=w_codes[e][:].bitcast(FP8X4), rhs_scale=w_scales[e][:], start=True, stop=True,
+            )
+            if e in ACT_AFTER:
+                acts[e] = shared.tile([P, 2, P, 2], F32, name="acts%d" % e, tag="raw%d" % (e + 1))
+            else:
+                acts[e] = ring.tile([P, 2, P, 2], F32, name="acts")
+            nc.scalar.activation(out=acts[e][:], in_=sums[:].rearrange("s (m u v) -> s u m v", u=2, v=2), func=GELU)
 
-        def apply_gate(e, u):
-            slots = slice(e * C, (e + 1) * C)
-            pairs = gated[u][:, slots].bitcast(BF16).rearrange("p (s v) -> p s v", v=2)
-            nc.vector.tensor_tensor(pairs, acts[e][:, u, :, :], gate_sb[:, slots].unsqueeze(2).to_broadcast([P, C, 2]), MULT)
+        gated = {}
+
+        def apply_gate(e):
+            if e == WM_AFTER:
+                gated[e] = shared.tile([P, H], BF16, name="gated_wm", tag="wm", align_bytes=64)
+            else:
+                gated[e] = ring.tile([P, H], BF16, name="gated")
+            nc.vector.tensor_scalar(gated[e][:], acts[e][:].rearrange("s u m v -> s (u m v)"), gate_cols[:, e : e + 1], None, MULT)
+
+        def turn(e):
+            ps = psum.tile([P, 2, C], F32, name="turn_ps", tag="acc")
+            for u in range(2):
+                nc.tensor.transpose(ps[:, u, :], gated[e][:].bitcast(F32)[:, u * P : (u + 1) * P], ident[:])
+            copy_on("v" if e in V_TURNS else "s", turned[:, :, e * C : (e + 1) * C], ps[:])
 
         def scatter(u, a, b):
-            nc.vector.tensor_copy(out=win[u][:].indirect(offsets[:, a // 16 : b // 16]), in_=gated[u][:, a:b])
+            nc.vector.tensor_copy(out=win[u][:].indirect(offsets[:, a // 16 : b // 16]), in_=turned[:, u, a:b])
 
         def cast_wm():
+            wm_bf = shared.tile([P, D, N, PACK], BF16, name="wm_bf", tag="wm", align_bytes=64)
             for o in range(D):
-                nc.scalar.copy(
-                    out=wm_bf[:, o, :, :].rearrange("p (c i) j -> p c j i", i=4),
-                    in_=wm_raw[:, o, :, :].rearrange("p j (c i) -> p c j i", i=4),
-                )
+                for a in range(0, N, WM_COLS):
+                    nc.scalar.copy(
+                        out=wm_bf[:, o, a : a + WM_COLS, :].rearrange("p (c i) j -> p c j i", i=4),
+                        in_=wm_raw[:, o, :, a : a + WM_COLS].rearrange("p j (c i) -> p c j i", i=4),
+                    )
+            return wm_bf
 
-        def quant_wm():
+        def quant_wm(wm_codes, wm_bf):
             nc.vector.quantize_mx(
                 out=wm_codes[:].bitcast(FP8X4), scales=wm_scales[:], in_=wm_bf[:].rearrange("p o n j -> p (o n j)")
             )
@@ -158,31 +196,43 @@ def tile_moe_mhm_gelu_kernel(tc, x_words, x_scales, w, wm, gate, offs, out):
         result = [keep.tile([P, 2, widths[k]], F32, name="result%d" % k) for k in range(nch)]
         out_v = out.rearrange("(h p) t -> p h t", p=P)
 
-        for k in range(len(GATHER_CUTS) - 1):
-            gather(k)
+        gather(0)
+        def finish(e):
+            apply_gate(e)
+            turn(e)
+
         for step in range(E + 3):
+            if step - 2 in EARLY:
+                finish(step - 2)
             if step < E:
                 cast_w(step)
             if 0 <= step - 1 < E:
                 quant_w(step - 1)
+                if step - 1 in GATHER_AFTER:
+                    gather(GATHER_AFTER.index(step - 1))
                 expert(step - 1)
-            if step == E:
-                cast_wm()
-            if 0 <= step - 2 < E:
-                e = step - 2
-                first = 0 if e == E - 1 else e % 2
-                for u in (first, 1 - first):
-                    apply_gate(e, u)
-                for u in (first, 1 - first):
-                    for a, b in zip(CUTS[u], CUTS[u][1:]):
-                        if (b - 1) // C == e:
-                            scatter(u, a, b)
+            if 0 <= step - 2 < E and step - 2 not in EARLY:
+                finish(step - 2)
+            for u in range(2):
+                for a, b in zip(CUTS[u], CUTS[u][1:]):
+                    if (b - 1) // C == step - 3:
+                        scatter(u, a, b)
 
-        nc.scalar.copy(out=both[:, 0, :, :], in_=win[0][:].rearrange("p (o t) -> p o t", o=D))
-        for t0, t1 in zip(TOKEN_CUTS, TOKEN_CUTS[1:]):
-            nc.scalar.copy(out=both[:, 1, :, t0:t1], in_=win[1][:].rearrange("p (o t) -> p o t", o=D)[:, :, t0:t1])
+        wm_bf = cast_wm()
 
-        quant_wm()
+        def side_by_side(u, k):
+            t0, t1 = TOKEN_CUTS[k], TOKEN_CUTS[k + 1]
+            nc.scalar.copy(out=both[:, u, :, t0:t1], in_=win[u][:].rearrange("p (o t) -> p o t", o=D)[:, :, t0:t1])
+
+        for k in range(AHEAD):
+            side_by_side(0, k)
+        for k in range(nch):
+            side_by_side(1, k)
+            if k + AHEAD < nch:
+                side_by_side(0, k + AHEAD)
+
+        wm_codes = shared.tile([P, D * N], U32, name="wm_codes", tag="turned", align_bytes=64)
+        quant_wm(wm_codes, wm_bf)
         warm_ps = psum.tile([P, PACK * C], F32, name="warm_ps", tag="sums")
         for rep in range(3):
             nc.tensor.matmul_mx(
@@ -210,7 +260,7 @@ def tile_moe_mhm_gelu_kernel(tc, x_words, x_scales, w, wm, gate, offs, out):
                         rhs=c_codes[k][:, tcols].bitcast(FP8X4), rhs_scale=c_scales[k][:, tcols],
                         start=(o == 0), stop=(o == D - 1),
                     )
-            nc.scalar.copy(out=result[k][:], in_=acc[:])
+            copy_on(RES_ENG[k], result[k][:], acc[:])
             nc.sync.dma_start(out=out_v[:, :, t0:t1], in_=result[k][:])
 
         def last_chunk():
@@ -237,7 +287,7 @@ def tile_moe_mhm_gelu_kernel(tc, x_words, x_scales, w, wm, gate, offs, out):
             nc.sync.dma_start(out=out_v[:, 1, t0:t1], in_=result[k][:, 1, :])
 
         for step in range(nch):
-            interleave(step, "v")
+            interleave(step, "s" if step in S_CHUNKS else "v")
             if step >= 1:
                 merge(step - 1)
         last_chunk()

@@ -20,26 +20,27 @@ MULT = mybir.AluOpType.mult
 P = 128
 PACK = 4
 SCALE_CUTS = [0, 768, 1536]
-GATHER_CUTS = [0, 256, 768, 1536]
-TOKEN_CUTS = [0, 128, 384, 512, 640, 768]
-GATHER_AFTER = [None, 1, 2]
-W1_V = 1
+GATHER_CUTS = [0, 256, 768, 1152, 1536]
+TOKEN_CUTS = [0, 256, 384, 512, 640, 768]
+GATHER_AFTER = [None, 0, 1, 2]
 V_TURNS = []
-V2 = 192
 EARLY = [1]
-RES_ENG = "ssss"
+WM_SLOT = False
+LAST_SPLIT = False
+GATE_AFTER = 1
+VC = [0, 0, 80, 224, 80, 80, 80, 80, 80, 80, 80, 80]
+S_MULT = []
+COPY = mybir.ActivationFunctionType.Copy
+RES_ENG = "ssssv"
 W0_FIRST = True
 X_AFTER = 0
 ACT_AFTER = [0, 1]
-WM_AFTER = 10
+WM_AFTER = 11
 WM_COLS = 256
-V_TO = 12
-AHEAD = 3
-S_CHUNKS = [2]
-V_COLS = 96
-V_FROM = 2
-LOAD_CUTS = [[0, 256, 512], [0, 256, 384, 512]] + [[0, 512]] * (E - 2)
-CUTS = [[0, 256, 512, 768, 1024, 1280, 1536], [0, 192, 384, 640, 896, 1152, 1344, 1536]]
+AHEAD = 2
+S_CHUNKS = [4]
+LOAD_CUTS = [[0, 256, 512], [0, 256, 512], [0, 512], [0, 512], [0, 512], [0, 512], [0, 512], [0, 512], [0, 512], [0, 512], [0, 512], [0, 512]]
+CUTS = [[0, 256, 512, 768, 1024, 1280, 1536], [0, 320, 576, 832, 1088, 1344, 1536]]
 
 
 def tile_moe_mhm_gelu_kernel(tc, x_words, x_scales, w, wm, gate, offs, out):
@@ -70,7 +71,7 @@ def tile_moe_mhm_gelu_kernel(tc, x_words, x_scales, w, wm, gate, offs, out):
             a, b = LOAD_CUTS[e][k], LOAD_CUTS[e][k + 1]
             nc.sync.dma_start(out=w_raw[e][:, :, a:b], in_=w[e].rearrange("(p j) c -> p j c", j=PACK)[:, :, a:b])
 
-        nc.vector.memset(xs[:].bitcast(I32), 0)
+        nc.gpsimd.memset(xs[:].bitcast(I32), 0)
         nc.vector.memset(gate_rows[:], 0.0)
         nc.sync.dma_start(offsets[:], offs)
         if W0_FIRST:
@@ -79,15 +80,17 @@ def tile_moe_mhm_gelu_kernel(tc, x_words, x_scales, w, wm, gate, offs, out):
         scale_rows = x_scales.bitcast(I32).rearrange("o b t -> b o t")
         for q in range(4):
             nc.sync.dma_start(out=xs_words[32 * q : 32 * q + 4, :, :], in_=scale_rows[4 * q : 4 * q + 4, :, :])
-        nc.sync.dma_start(out=gate_rows[0:E, :], in_=gate[0].rearrange("(e s) -> e s", s=C))
         nc.gpsimd.memset(warm_in[:], 0.0)
         make_identity(nc, ident[:])
         nc.scalar.activation(out=warm_out[:], in_=warm_in[:], func=GELU)
 
-        for e in range(E):
-            for k in range(1 if e == 0 and W0_FIRST else 0, len(LOAD_CUTS[e]) - 1):
+        pieces = [(e, k) for e in range(E) for k in range(len(LOAD_CUTS[e]) - 1)]
+        for n, (e, k) in enumerate(pieces):
+            if n > 0 or not W0_FIRST:
                 load_w(e, k)
-            if e == X_AFTER:
+            if n == GATE_AFTER:
+                nc.sync.dma_start(out=gate_rows[0:E, :], in_=gate[0].rearrange("(e s) -> e s", s=C))
+            if n == X_AFTER:
                 nc.sync.dma_start(
                     out=xw[:].rearrange("p (o t) -> p o t", o=D),
                     in_=x_words.rearrange("o p t d -> p o (t d)").bitcast(I32),
@@ -114,21 +117,23 @@ def tile_moe_mhm_gelu_kernel(tc, x_words, x_scales, w, wm, gate, offs, out):
 
         def gather(k):
             a, b = GATHER_CUTS[k], GATHER_CUTS[k + 1]
-            gw[k] = shared.tile([P, b - a], U32, name="gw%d" % k, tag="after%d" % (GATHER_AFTER[k] or 0), align_bytes=64)
+            gw[k] = shared.tile([P, b - a], U32, name="gw%d" % k, tag="after%d" % (100 + k if GATHER_AFTER[k] is None else GATHER_AFTER[k]), align_bytes=64)
             nc.vector.tensor_copy(out=gw[k][:], in_=xw[:].bitcast(U32).indirect(offsets[:, a // 16 : b // 16]))
 
         w_bf, w_codes, w_scales, acts = {}, {}, {}, {}
+
+        CAST_CUTS = [sorted(set(LOAD_CUTS[e] + [H - VC[e]])) for e in range(E)]
 
         def cast_w(e):
             if e in GATHER_AFTER:
                 w_bf[e] = shared.tile([P, H, PACK], BF16, name="w_bf%d" % e, tag="after%d" % e, align_bytes=64)
             else:
                 w_bf[e] = ring.tile([P, H, PACK], BF16, name="w_bf", align_bytes=64)
-            cuts = LOAD_CUTS[e] if e < V_FROM or e >= V_TO else [0, H - (V2 if e == 2 else V_COLS), H]
+            cuts = CAST_CUTS[e]
             for k in range(len(cuts) - 1):
                 a, b = cuts[k], cuts[k + 1]
                 copy_on(
-                    "v" if (e >= V_FROM and k == 1) or (e == 1 and k >= W1_V) else "s",
+                    "v" if a >= H - VC[e] else "s",
                     w_bf[e][:, a:b, :].rearrange("p (c i) j -> p c j i", i=4),
                     w_raw[e][:, :, a:b].rearrange("p j (c i) -> p c j i", i=4),
                 )
@@ -162,7 +167,10 @@ def tile_moe_mhm_gelu_kernel(tc, x_words, x_scales, w, wm, gate, offs, out):
                 gated[e] = shared.tile([P, H], BF16, name="gated_wm", tag="wm", align_bytes=64)
             else:
                 gated[e] = ring.tile([P, H], BF16, name="gated")
-            nc.vector.tensor_scalar(gated[e][:], acts[e][:].rearrange("s u m v -> s (u m v)"), gate_cols[:, e : e + 1], None, MULT)
+            if e in S_MULT:
+                nc.scalar.activation(out=gated[e][:], in_=acts[e][:].rearrange("s u m v -> s (u m v)"), func=COPY, scale=gate_cols[:, e : e + 1])
+            else:
+                nc.vector.tensor_scalar(gated[e][:], acts[e][:].rearrange("s u m v -> s (u m v)"), gate_cols[:, e : e + 1], None, MULT)
 
         def turn(e):
             ps = psum.tile([P, 2, C], F32, name="turn_ps", tag="acc")
@@ -196,7 +204,9 @@ def tile_moe_mhm_gelu_kernel(tc, x_words, x_scales, w, wm, gate, offs, out):
         result = [keep.tile([P, 2, widths[k]], F32, name="result%d" % k) for k in range(nch)]
         out_v = out.rearrange("(h p) t -> p h t", p=P)
 
-        gather(0)
+        for k in range(len(GATHER_AFTER)):
+            if GATHER_AFTER[k] is None:
+                gather(k)
         def finish(e):
             apply_gate(e)
             turn(e)
@@ -231,7 +241,7 @@ def tile_moe_mhm_gelu_kernel(tc, x_words, x_scales, w, wm, gate, offs, out):
             if k + AHEAD < nch:
                 side_by_side(0, k + AHEAD)
 
-        wm_codes = shared.tile([P, D * N], U32, name="wm_codes", tag="turned", align_bytes=64)
+        wm_codes = shared.tile([P, D * N], U32, name="wm_codes", tag="turned" if WM_SLOT else "wmc", align_bytes=64)
         quant_wm(wm_codes, wm_bf)
         warm_ps = psum.tile([P, PACK * C], F32, name="warm_ps", tag="sums")
         for rep in range(3):
@@ -268,12 +278,18 @@ def tile_moe_mhm_gelu_kernel(tc, x_words, x_scales, w, wm, gate, offs, out):
             t0, t1 = TOKEN_CUTS[k], TOKEN_CUTS[k + 1]
             width = t1 - t0
             accs = [psum.tile([P, width], F32, name="acc_last%d" % h, tag="last", bufs=2) for h in range(2)]
+            if not LAST_SPLIT:
+                nc.vector.quantize_mx(
+                    out=c_codes[k][:].bitcast(FP8X4), scales=c_scales[k][:],
+                    in_=c_bf[k][:].rearrange("p o t u -> p (o t u)").bitcast(BF16),
+                )
             for o in range(D):
                 tcols = slice(o * width, (o + 1) * width)
-                nc.vector.quantize_mx(
-                    out=c_codes[k][:, tcols].bitcast(FP8X4), scales=c_scales[k][:, tcols],
-                    in_=c_bf[k][:, o, :, :].rearrange("p t u -> p (t u)").bitcast(BF16),
-                )
+                if LAST_SPLIT:
+                    nc.vector.quantize_mx(
+                        out=c_codes[k][:, tcols].bitcast(FP8X4), scales=c_scales[k][:, tcols],
+                        in_=c_bf[k][:, o, :, :].rearrange("p t u -> p (t u)").bitcast(BF16),
+                    )
                 for h in range(2):
                     ncols = slice(o * N + h * P, o * N + (h + 1) * P)
                     nc.tensor.matmul_mx(

@@ -22,13 +22,16 @@ PACK = 4
 SCALE_CUTS = [0, 768, 1536]
 GATHER_CUTS = [0, 256, 768, 1152, 1536]
 TOKEN_CUTS = [0, 256, 384, 512, 640, 768]
-GATHER_AFTER = [None, 0, 1, 2]
+GATHER_AFTER = [None, ["bf", 0], ["bf", 1], ["bf", 2]]
 V_TURNS = []
 EARLY = [1]
+LATE = []
+G_MULT = [2, 3, 4, 5, 6, 7, 8, 9]
+ADD = mybir.AluOpType.add
 WM_SLOT = False
 LAST_SPLIT = False
 GATE_AFTER = 1
-VC = [0, 0, 80, 224, 80, 80, 80, 80, 80, 80, 80, 80]
+VC = [0, 0, 112, 224, 112, 112, 112, 112, 112, 112, 112, 112]
 S_MULT = []
 COPY = mybir.ActivationFunctionType.Copy
 RES_ENG = "ssssv"
@@ -60,7 +63,7 @@ def tile_moe_mhm_gelu_kernel(tc, x_words, x_scales, w, wm, gate, offs, out):
         ident = keep.tile([P, P], F32, name="ident")
         warm_in = keep.tile([P, 8], F32, name="warm_in")
         warm_out = keep.tile([P, 8], F32, name="warm_out")
-        w_raw = [shared.tile([P, PACK, H], F32, name="w_raw%d" % e, tag="raw%d" % e) for e in range(E)]
+        w_raw = [shared.tile([P, PACK, H], F32, name="w_raw%d" % e, tag="raw%d" % e, align_bytes=64) for e in range(E)]
         wm_raw = keep.tile([P, D, PACK, N], F32, name="wm_raw")
         wm_scales = keep.tile([P, D * N], U8, name="wm_scales", align_bytes=64)
         turned = shared.tile([P, 2, S], F32, name="turned", tag="turned", align_bytes=64)
@@ -114,10 +117,33 @@ def tile_moe_mhm_gelu_kernel(tc, x_words, x_scales, w, wm, gate, offs, out):
             nc.vector.tensor_copy(out=gs[:, a:b], in_=xs[:].indirect(offsets[:, a // 16 : b // 16]))
 
         gw = {}
+        hold = {("gw", k): tuple(GATHER_AFTER[k]) for k in range(len(GATHER_AFTER)) if GATHER_AFTER[k]}
+        for e in ACT_AFTER:
+            hold[("acts", e)] = ("raw", e + 1)
+        for e in G_MULT:
+            hold[("gated", e)] = ("bf", e + 1)
+        hold[("wm", 0)] = ("gated", WM_AFTER)
+
+        for e in range(4, E):
+            if e - 4 in G_MULT:
+                hold[("bf", e)] = ("gated", e - 4)
+
+        def root(key):
+            return root(hold[key]) if key in hold else key
+
+        def alloc(key, shape, dtype):
+            if key in hold or key in hold.values() or key[0] == "gw":
+                return shared.tile(shape, dtype, name="%s%d" % key, tag="%s%d" % root(key), align_bytes=64)
+            return ring.tile(shape, dtype, name=key[0], align_bytes=64)
+
+        def gathers_after(kinds, e):
+            for k in range(len(GATHER_AFTER)):
+                if GATHER_AFTER[k] and GATHER_AFTER[k][0] in kinds and GATHER_AFTER[k][1] == e:
+                    gather(k)
 
         def gather(k):
             a, b = GATHER_CUTS[k], GATHER_CUTS[k + 1]
-            gw[k] = shared.tile([P, b - a], U32, name="gw%d" % k, tag="after%d" % (100 + k if GATHER_AFTER[k] is None else GATHER_AFTER[k]), align_bytes=64)
+            gw[k] = alloc(("gw", k), [P, b - a], U32)
             nc.vector.tensor_copy(out=gw[k][:], in_=xw[:].bitcast(U32).indirect(offsets[:, a // 16 : b // 16]))
 
         w_bf, w_codes, w_scales, acts = {}, {}, {}, {}
@@ -125,10 +151,7 @@ def tile_moe_mhm_gelu_kernel(tc, x_words, x_scales, w, wm, gate, offs, out):
         CAST_CUTS = [sorted(set(LOAD_CUTS[e] + [H - VC[e]])) for e in range(E)]
 
         def cast_w(e):
-            if e in GATHER_AFTER:
-                w_bf[e] = shared.tile([P, H, PACK], BF16, name="w_bf%d" % e, tag="after%d" % e, align_bytes=64)
-            else:
-                w_bf[e] = ring.tile([P, H, PACK], BF16, name="w_bf", align_bytes=64)
+            w_bf[e] = alloc(("bf", e), [P, H, PACK], BF16)
             cuts = CAST_CUTS[e]
             for k in range(len(cuts) - 1):
                 a, b = cuts[k], cuts[k + 1]
@@ -139,7 +162,7 @@ def tile_moe_mhm_gelu_kernel(tc, x_words, x_scales, w, wm, gate, offs, out):
                 )
 
         def quant_w(e):
-            w_codes[e] = ring.tile([P, H], U32, name="w_codes", align_bytes=64)
+            w_codes[e] = alloc(("codes", e), [P, H], U32)
             w_scales[e] = ring.tile([P, H], U8, name="w_scales", align_bytes=64)
             nc.vector.quantize_mx(
                 out=w_codes[e][:].bitcast(FP8X4), scales=w_scales[e][:], in_=w_bf[e][:].rearrange("p c j -> p (c j)")
@@ -154,21 +177,17 @@ def tile_moe_mhm_gelu_kernel(tc, x_words, x_scales, w, wm, gate, offs, out):
                 out=sums[:], lhsT=words.bitcast(FP8X4), lhsT_scale=gs[:, slots],
                 rhs=w_codes[e][:].bitcast(FP8X4), rhs_scale=w_scales[e][:], start=True, stop=True,
             )
-            if e in ACT_AFTER:
-                acts[e] = shared.tile([P, 2, P, 2], F32, name="acts%d" % e, tag="raw%d" % (e + 1))
-            else:
-                acts[e] = ring.tile([P, 2, P, 2], F32, name="acts")
+            acts[e] = alloc(("acts", e), [P, 2, P, 2], F32)
             nc.scalar.activation(out=acts[e][:], in_=sums[:].rearrange("s (m u v) -> s u m v", u=2, v=2), func=GELU)
 
         gated = {}
 
         def apply_gate(e):
-            if e == WM_AFTER:
-                gated[e] = shared.tile([P, H], BF16, name="gated_wm", tag="wm", align_bytes=64)
-            else:
-                gated[e] = ring.tile([P, H], BF16, name="gated")
+            gated[e] = alloc(("gated", e), [P, H], BF16)
             if e in S_MULT:
                 nc.scalar.activation(out=gated[e][:], in_=acts[e][:].rearrange("s u m v -> s (u m v)"), func=COPY, scale=gate_cols[:, e : e + 1])
+            elif e in G_MULT:
+                nc.gpsimd.tensor_scalar(gated[e][:], acts[e][:].rearrange("s u m v -> s (u m v)"), gate_cols[:, e : e + 1], 0.0, MULT, ADD)
             else:
                 nc.vector.tensor_scalar(gated[e][:], acts[e][:].rearrange("s u m v -> s (u m v)"), gate_cols[:, e : e + 1], None, MULT)
 
@@ -182,7 +201,7 @@ def tile_moe_mhm_gelu_kernel(tc, x_words, x_scales, w, wm, gate, offs, out):
             nc.vector.tensor_copy(out=win[u][:].indirect(offsets[:, a // 16 : b // 16]), in_=turned[:, u, a:b])
 
         def cast_wm():
-            wm_bf = shared.tile([P, D, N, PACK], BF16, name="wm_bf", tag="wm", align_bytes=64)
+            wm_bf = alloc(("wm", 0), [P, D, N, PACK], BF16)
             for o in range(D):
                 for a in range(0, N, WM_COLS):
                     nc.scalar.copy(
@@ -209,23 +228,27 @@ def tile_moe_mhm_gelu_kernel(tc, x_words, x_scales, w, wm, gate, offs, out):
                 gather(k)
         def finish(e):
             apply_gate(e)
-            turn(e)
+            if e not in LATE:
+                turn(e)
+            if e - 1 in LATE:
+                turn(e - 1)
+            gathers_after(("acts", "gated"), e)
 
-        for step in range(E + 3):
+        for step in range(E + 4):
             if step - 2 in EARLY:
                 finish(step - 2)
             if step < E:
                 cast_w(step)
             if 0 <= step - 1 < E:
                 quant_w(step - 1)
-                if step - 1 in GATHER_AFTER:
-                    gather(GATHER_AFTER.index(step - 1))
+                gathers_after(("raw", "bf"), step - 1)
                 expert(step - 1)
+                gathers_after(("codes",), step - 1)
             if 0 <= step - 2 < E and step - 2 not in EARLY:
                 finish(step - 2)
             for u in range(2):
                 for a, b in zip(CUTS[u], CUTS[u][1:]):
-                    if (b - 1) // C == step - 3:
+                    if (b - 1) // C == step - (4 if (b - 1) // C in LATE else 3):
                         scatter(u, a, b)
 
         wm_bf = cast_wm()

@@ -20,29 +20,29 @@ MULT = mybir.AluOpType.mult
 P = 128
 PACK = 4
 SCALE_CUTS = [0, 768, 1536]
-GATHER_CUTS = [0, 256, 768, 1152, 1536]
+GATHER_CUTS = [0, 256, 1024, 1536]
 TOKEN_CUTS = [0, 256, 384, 512, 640, 768]
-GATHER_AFTER = [None, ["bf", 0], ["bf", 1], ["bf", 2]]
-V_TURNS = []
-EARLY = [1]
+GATHER_AFTER = [None, None, ["acts", 1]]
+V_TURNS = [0]
+EARLY = []
 LATE = []
 G_MULT = [2, 3, 4, 5, 6, 7, 8, 9]
 ADD = mybir.AluOpType.add
 WM_SLOT = False
 LAST_SPLIT = False
 GATE_AFTER = 1
-VC = [0, 0, 112, 224, 112, 112, 112, 112, 112, 112, 112, 112]
+VC = [0, 0, 224, 144, 144, 144, 144, 144, 144, 144, 144, 144]
 S_MULT = []
 COPY = mybir.ActivationFunctionType.Copy
-RES_ENG = "ssssv"
+RES_ENG = "sssss"
 W0_FIRST = True
-X_AFTER = 0
+X_AFTER = 2
 ACT_AFTER = [0, 1]
 WM_AFTER = 11
 WM_COLS = 256
 AHEAD = 2
-S_CHUNKS = [4]
-LOAD_CUTS = [[0, 256, 512], [0, 256, 512], [0, 512], [0, 512], [0, 512], [0, 512], [0, 512], [0, 512], [0, 512], [0, 512], [0, 512], [0, 512]]
+S_CHUNKS = [3]
+LOAD_CUTS = [[0, 256, 512], [0, 256, 384, 512], [0, 512], [0, 512], [0, 512], [0, 512], [0, 512], [0, 512], [0, 512], [0, 512], [0, 512], [0, 512]]
 CUTS = [[0, 256, 512, 768, 1024, 1280, 1536], [0, 320, 576, 832, 1088, 1344, 1536]]
 
 

@@ -21,10 +21,14 @@ P = 128
 PACK = 4
 SCALE_CUTS = [0, 768, 1536]
 GATHER_CUTS = [0, 256, 1024, 1536]
-TOKEN_CUTS = [0, 256, 384, 512, 640, 768]
+TOKEN_CUTS = [0, 128, 256, 384, 512, 640, 768]
 GATHER_AFTER = [None, None, ["acts", 1]]
 V_TURNS = [0]
 EARLY = []
+STORE_Q = "ssssss"
+LAST_Q = True
+LAST_PLAIN = False
+G_SIDE = True
 LATE = []
 G_MULT = [2, 3, 4, 5, 6, 7, 8, 9]
 ADD = mybir.AluOpType.add
@@ -34,15 +38,15 @@ GATE_AFTER = 1
 VC = [0, 0, 224, 144, 144, 144, 144, 144, 144, 144, 144, 144]
 S_MULT = []
 COPY = mybir.ActivationFunctionType.Copy
-RES_ENG = "sssss"
+RES_ENG = "ssssss"
 W0_FIRST = True
-X_AFTER = 2
+X_AFTER = 1
 ACT_AFTER = [0, 1]
 WM_AFTER = 11
 WM_COLS = 256
-AHEAD = 2
-S_CHUNKS = [3]
-LOAD_CUTS = [[0, 256, 512], [0, 256, 384, 512], [0, 512], [0, 512], [0, 512], [0, 512], [0, 512], [0, 512], [0, 512], [0, 512], [0, 512], [0, 512]]
+AHEAD = 4
+S_CHUNKS = [4, 5]
+LOAD_CUTS = [[0, 256, 512], [0, 256, 512], [0, 512], [0, 512], [0, 512], [0, 512], [0, 512], [0, 512], [0, 512], [0, 512], [0, 512], [0, 512]]
 CUTS = [[0, 256, 512, 768, 1024, 1280, 1536], [0, 320, 576, 832, 1088, 1344, 1536]]
 
 
@@ -259,9 +263,12 @@ def tile_moe_mhm_gelu_kernel(tc, x_words, x_scales, w, wm, gate, offs, out):
 
         for k in range(AHEAD):
             side_by_side(0, k)
+        if G_SIDE:
+            t0 = TOKEN_CUTS[AHEAD]
+            nc.gpsimd.tensor_copy(out=both[:, 0, :, t0:], in_=win[0][:].rearrange("p (o t) -> p o t", o=D)[:, :, t0:])
         for k in range(nch):
             side_by_side(1, k)
-            if k + AHEAD < nch:
+            if k + AHEAD < nch and not G_SIDE:
                 side_by_side(0, k + AHEAD)
 
         wm_codes = shared.tile([P, D * N], U32, name="wm_codes", tag="turned" if WM_SLOT else "wmc", align_bytes=64)
@@ -294,7 +301,7 @@ def tile_moe_mhm_gelu_kernel(tc, x_words, x_scales, w, wm, gate, offs, out):
                         start=(o == 0), stop=(o == D - 1),
                     )
             copy_on(RES_ENG[k], result[k][:], acc[:])
-            nc.sync.dma_start(out=out_v[:, :, t0:t1], in_=result[k][:])
+            (nc.scalar if STORE_Q[k] == "a" else nc.sync).dma_start(out=out_v[:, :, t0:t1], in_=result[k][:])
 
         def last_chunk():
             k = nch - 1
@@ -321,7 +328,7 @@ def tile_moe_mhm_gelu_kernel(tc, x_words, x_scales, w, wm, gate, offs, out):
                         start=(o == 0), stop=(o == D - 1),
                     )
             nc.scalar.copy(out=result[k][:, 0, :], in_=accs[0][:])
-            nc.sync.dma_start(out=out_v[:, 0, t0:t1], in_=result[k][:, 0, :])
+            (nc.scalar if LAST_Q else nc.sync).dma_start(out=out_v[:, 0, t0:t1], in_=result[k][:, 0, :])
             nc.vector.tensor_copy(out=result[k][:, 1, :], in_=accs[1][:])
             nc.sync.dma_start(out=out_v[:, 1, t0:t1], in_=result[k][:, 1, :])
 
@@ -329,4 +336,7 @@ def tile_moe_mhm_gelu_kernel(tc, x_words, x_scales, w, wm, gate, offs, out):
             interleave(step, "s" if step in S_CHUNKS else "v")
             if step >= 1:
                 merge(step - 1)
-        last_chunk()
+        if LAST_PLAIN:
+            merge(nch - 1)
+        else:
+            last_chunk()

@@ -273,12 +273,6 @@ def tile_moe_mhm_gelu_kernel(tc, x_words, x_scales, w, wm, gate, offs, out):
 
         wm_codes = shared.tile([P, D * N], U32, name="wm_codes", tag="turned" if WM_SLOT else "wmc", align_bytes=64)
         quant_wm(wm_codes, wm_bf)
-        warm_ps = psum.tile([P, PACK * C], F32, name="warm_ps", tag="sums")
-        for rep in range(3):
-            nc.tensor.matmul_mx(
-                out=warm_ps[:], lhsT=wm_codes[:, 0:P].bitcast(FP8X4), lhsT_scale=wm_scales[:, 0:P],
-                rhs=wm_codes[:].bitcast(FP8X4), rhs_scale=wm_scales[:], start=True, stop=True,
-            )
 
         def interleave(k, eng):
             copy_on(eng, c_bf[k][:], both[:, :, :, TOKEN_CUTS[k] : TOKEN_CUTS[k + 1]].rearrange("p u o t -> p o t u"))

@@ -15,39 +15,36 @@ U16 = mybir.dt.uint16
 U8 = mybir.dt.uint8
 FP8X4 = mybir.dt.float8_e4m3fn_x4
 GELU = mybir.ActivationFunctionType.Gelu_apprx_tanh
+COPY = mybir.ActivationFunctionType.Copy
 MULT = mybir.AluOpType.mult
+ADD = mybir.AluOpType.add
 
 P = 128
 PACK = 4
 SCALE_CUTS = [0, 768, 1536]
-GATHER_CUTS = [0, 256, 1024, 1536]
-TOKEN_CUTS = [0, 128, 256, 384, 512, 640, 768]
-GATHER_AFTER = [None, None, ["acts", 1]]
-V_TURNS = [0]
-EARLY = []
-STORE_Q = "ssssss"
-LAST_Q = True
-LAST_PLAIN = False
-G_SIDE = True
-LATE = []
-G_MULT = [2, 3, 4, 5, 6, 7, 8, 9]
-ADD = mybir.AluOpType.add
-WM_SLOT = False
-LAST_SPLIT = False
-GATE_AFTER = 1
-VC = [0, 0, 224, 144, 144, 144, 144, 144, 144, 144, 144, 144]
-S_MULT = []
-COPY = mybir.ActivationFunctionType.Copy
-RES_ENG = "ssssss"
-W0_FIRST = True
+GATHER_CUTS = [0, 256, 640, 1152, 1536]
+GATHER_HOLD = [(None, -1), (None, -1), ("h", 1), ("raw2", 2)]
+QUANT_CUTS = [[0, 512]] * 12
 X_AFTER = 1
-ACT_AFTER = [0, 1]
-WM_AFTER = 11
-WM_COLS = 256
-AHEAD = 4
+BF_TAG = ["h","h","bf","bf","bf","bf","bf","bf","bf","bf","bf","bf"]
+ACTS_TAG = ["raw1",None,"raw3",None,None,None,None,None,None,None,None,None]
+GATED_TAG = [None,None,None,None,None,None,None,None,None,None,None,"last"]
+WM_TAG = ["bf", "last"]
+G_SIDE = False
+TURN_AT = [2,2,4,5,6,7,8,9,10,11,12,13]
+GATE_AFTER = 1
+TOKEN_CUTS = [0, 128, 256, 384, 512, 640, 768]
+SCALES_FIRST = False
+LOAD_CUTS = [[0, 256, 512], [0, 256, 512]] + [[0, 512]] * 10
+CASTS = [[["s",0,256],["s",256,512]],[["s",0,256],["s",256,384],["v",384,512]],[["s",0,128],["v",128,512]],[["s",0,288],["g",288,512]],[["s",0,288],["g",288,512]],[["s",0,288],["g",288,512]],[["s",0,288],["g",288,512]],[["s",0,288],["g",288,512]],[["s",0,288],["g",288,512]],[["s",0,288],["g",288,512]],[["s",0,288],["g",288,512]],[["s",0,288],["g",288,512]]]
+GATE_ENG = "gvhhhhhhhhhh"
+TURN_ENG = "ssssssssssss"
+PIECES = [(2, 1, 0, 256), (3, 0, 0, 192), (4, 0, 192, 384), (5, 1, 256, 512), (6, 0, 384, 640), (7, 1, 512, 768), (8, 0, 640, 896), (9, 1, 768, 1024), (10, 0, 896, 1152), (11, 1, 1024, 1280), (12, 0, 1152, 1344), (13, 0, 1344, 1536), (13, 1, 1280, 1536)]
+WIN0_AFTER = 3
+WM_ENG = "gs"
+AHEAD = 6
 S_CHUNKS = [4, 5]
-LOAD_CUTS = [[0, 256, 512], [0, 256, 512], [0, 512], [0, 512], [0, 512], [0, 512], [0, 512], [0, 512], [0, 512], [0, 512], [0, 512], [0, 512]]
-CUTS = [[0, 256, 512, 768, 1024, 1280, 1536], [0, 320, 576, 832, 1088, 1344, 1536]]
+RES_ENG = "ssssss"
 
 
 def tile_moe_mhm_gelu_kernel(tc, x_words, x_scales, w, wm, gate, offs, out):
@@ -70,8 +67,8 @@ def tile_moe_mhm_gelu_kernel(tc, x_words, x_scales, w, wm, gate, offs, out):
         w_raw = [shared.tile([P, PACK, H], F32, name="w_raw%d" % e, tag="raw%d" % e, align_bytes=64) for e in range(E)]
         wm_raw = keep.tile([P, D, PACK, N], F32, name="wm_raw")
         wm_scales = keep.tile([P, D * N], U8, name="wm_scales", align_bytes=64)
-        turned = shared.tile([P, 2, S], F32, name="turned", tag="turned", align_bytes=64)
-        win = [keep.tile([P, D * T], F32, name="win%d" % u) for u in range(2)]
+        wm_codes = keep.tile([P, D * N], U32, name="wm_codes", align_bytes=64)
+        turned = keep.tile([P, 2, S], F32, name="turned", align_bytes=64)
         both = keep.tile([P, 2, D, T], F32, name="both")
 
         def load_w(e, k):
@@ -81,7 +78,7 @@ def tile_moe_mhm_gelu_kernel(tc, x_words, x_scales, w, wm, gate, offs, out):
         nc.gpsimd.memset(xs[:].bitcast(I32), 0)
         nc.vector.memset(gate_rows[:], 0.0)
         nc.sync.dma_start(offsets[:], offs)
-        if W0_FIRST:
+        if not SCALES_FIRST:
             load_w(0, 0)
         xs_words = xs[:].bitcast(I32).rearrange("p (o t) -> p o t", o=D)
         scale_rows = x_scales.bitcast(I32).rearrange("o b t -> b o t")
@@ -93,7 +90,7 @@ def tile_moe_mhm_gelu_kernel(tc, x_words, x_scales, w, wm, gate, offs, out):
 
         pieces = [(e, k) for e in range(E) for k in range(len(LOAD_CUTS[e]) - 1)]
         for n, (e, k) in enumerate(pieces):
-            if n > 0 or not W0_FIRST:
+            if n > 0 or SCALES_FIRST:
                 load_w(e, k)
             if n == GATE_AFTER:
                 nc.sync.dma_start(out=gate_rows[0:E, :], in_=gate[0].rearrange("(e s) -> e s", s=C))
@@ -117,107 +114,83 @@ def tile_moe_mhm_gelu_kernel(tc, x_words, x_scales, w, wm, gate, offs, out):
             else:
                 nc.scalar.copy(out=d, in_=s)
 
+        def interleave_round(eng, dst, src):
+            if eng == "g":
+                nc.gpsimd.tensor_scalar(dst, src.rearrange("p j c -> p c j"), 1.0, 0.0, MULT, ADD)
+            else:
+                copy_on(eng, dst.rearrange("p (c i) j -> p c j i", i=4), src.rearrange("p j (c i) -> p c j i", i=4))
+
         for a, b in zip(SCALE_CUTS, SCALE_CUTS[1:]):
             nc.vector.tensor_copy(out=gs[:, a:b], in_=xs[:].indirect(offsets[:, a // 16 : b // 16]))
 
-        gw = {}
-        hold = {("gw", k): tuple(GATHER_AFTER[k]) for k in range(len(GATHER_AFTER)) if GATHER_AFTER[k]}
-        for e in ACT_AFTER:
-            hold[("acts", e)] = ("raw", e + 1)
-        for e in G_MULT:
-            hold[("gated", e)] = ("bf", e + 1)
-        hold[("wm", 0)] = ("gated", WM_AFTER)
-
-        for e in range(4, E):
-            if e - 4 in G_MULT:
-                hold[("bf", e)] = ("gated", e - 4)
-
-        def root(key):
-            return root(hold[key]) if key in hold else key
-
-        def alloc(key, shape, dtype):
-            if key in hold or key in hold.values() or key[0] == "gw":
-                return shared.tile(shape, dtype, name="%s%d" % key, tag="%s%d" % root(key), align_bytes=64)
-            return ring.tile(shape, dtype, name=key[0], align_bytes=64)
-
-        def gathers_after(kinds, e):
-            for k in range(len(GATHER_AFTER)):
-                if GATHER_AFTER[k] and GATHER_AFTER[k][0] in kinds and GATHER_AFTER[k][1] == e:
-                    gather(k)
+        gw, w_bf, w_codes, w_scales, sums, acts, gated, turn_ps, win = {}, {}, {}, {}, {}, {}, {}, {}, {}
 
         def gather(k):
             a, b = GATHER_CUTS[k], GATHER_CUTS[k + 1]
-            gw[k] = alloc(("gw", k), [P, b - a], U32)
+            gw[k] = shared.tile([P, b - a], U32, name="gw%d" % k, tag=GATHER_HOLD[k][0] or "gw%d" % k, align_bytes=64)
             nc.vector.tensor_copy(out=gw[k][:], in_=xw[:].bitcast(U32).indirect(offsets[:, a // 16 : b // 16]))
 
-        w_bf, w_codes, w_scales, acts = {}, {}, {}, {}
-
-        CAST_CUTS = [sorted(set(LOAD_CUTS[e] + [H - VC[e]])) for e in range(E)]
-
         def cast_w(e):
-            w_bf[e] = alloc(("bf", e), [P, H, PACK], BF16)
-            cuts = CAST_CUTS[e]
-            for k in range(len(cuts) - 1):
-                a, b = cuts[k], cuts[k + 1]
-                copy_on(
-                    "v" if a >= H - VC[e] else "s",
-                    w_bf[e][:, a:b, :].rearrange("p (c i) j -> p c j i", i=4),
-                    w_raw[e][:, :, a:b].rearrange("p j (c i) -> p c j i", i=4),
-                )
+            w_bf[e] = shared.tile([P, H, PACK], BF16, name="w_bf%d" % e, tag=BF_TAG[e], align_bytes=64)
+            for eng, a, b in CASTS[e]:
+                interleave_round(eng, w_bf[e][:, a:b, :], w_raw[e][:, :, a:b])
 
         def quant_w(e):
-            w_codes[e] = alloc(("codes", e), [P, H], U32)
+            w_codes[e] = ring.tile([P, H], U32, name="w_codes", align_bytes=64)
             w_scales[e] = ring.tile([P, H], U8, name="w_scales", align_bytes=64)
-            nc.vector.quantize_mx(
-                out=w_codes[e][:].bitcast(FP8X4), scales=w_scales[e][:], in_=w_bf[e][:].rearrange("p c j -> p (c j)")
-            )
+            for a, b in zip(QUANT_CUTS[e], QUANT_CUTS[e][1:]):
+                nc.vector.quantize_mx(
+                    out=w_codes[e][:, a:b].bitcast(FP8X4), scales=w_scales[e][:, a:b],
+                    in_=w_bf[e][:, a:b, :].rearrange("p c j -> p (c j)"),
+                )
 
-        def expert(e):
+        def product(e):
             slots = slice(e * C, (e + 1) * C)
             k = max(i for i in range(len(GATHER_CUTS)) if GATHER_CUTS[i] <= e * C)
             words = gw[k][:, e * C - GATHER_CUTS[k] : (e + 1) * C - GATHER_CUTS[k]]
-            sums = psum.tile([P, H], F32, name="sums")
+            sums[e] = psum.tile([P, H], F32, name="sums")
             nc.tensor.matmul_mx(
-                out=sums[:], lhsT=words.bitcast(FP8X4), lhsT_scale=gs[:, slots],
+                out=sums[e][:], lhsT=words.bitcast(FP8X4), lhsT_scale=gs[:, slots],
                 rhs=w_codes[e][:].bitcast(FP8X4), rhs_scale=w_scales[e][:], start=True, stop=True,
             )
-            acts[e] = alloc(("acts", e), [P, 2, P, 2], F32)
-            nc.scalar.activation(out=acts[e][:], in_=sums[:].rearrange("s (m u v) -> s u m v", u=2, v=2), func=GELU)
 
-        gated = {}
+        def activate(e):
+            if ACTS_TAG[e]:
+                acts[e] = shared.tile([P, 2, P, 2], F32, name="acts%d" % e, tag=ACTS_TAG[e], align_bytes=64)
+            else:
+                acts[e] = ring.tile([P, 2, P, 2], F32, name="acts", align_bytes=64)
+            nc.scalar.activation(out=acts[e][:], in_=sums[e][:].rearrange("s (m u v) -> s u m v", u=2, v=2), func=GELU)
 
         def apply_gate(e):
-            gated[e] = alloc(("gated", e), [P, H], BF16)
-            if e in S_MULT:
-                nc.scalar.activation(out=gated[e][:], in_=acts[e][:].rearrange("s u m v -> s (u m v)"), func=COPY, scale=gate_cols[:, e : e + 1])
-            elif e in G_MULT:
-                nc.gpsimd.tensor_scalar(gated[e][:], acts[e][:].rearrange("s u m v -> s (u m v)"), gate_cols[:, e : e + 1], 0.0, MULT, ADD)
+            if GATED_TAG[e]:
+                gated[e] = shared.tile([P, H], BF16, name="gated%d" % e, tag=GATED_TAG[e], align_bytes=64)
             else:
-                nc.vector.tensor_scalar(gated[e][:], acts[e][:].rearrange("s u m v -> s (u m v)"), gate_cols[:, e : e + 1], None, MULT)
+                gated[e] = ring.tile([P, H], BF16, name="gated", align_bytes=64)
+            flat = acts[e][:].rearrange("s u m v -> s (u m v)")
+            if GATE_ENG[e] == "h":
+                half = H // 2
+                nc.vector.tensor_scalar(gated[e][:, :half], flat[:, :half], gate_cols[:, e : e + 1], None, MULT)
+                nc.scalar.activation(out=gated[e][:, half:], in_=flat[:, half:], func=COPY, scale=gate_cols[:, e : e + 1])
+            elif GATE_ENG[e] == "s":
+                nc.scalar.activation(out=gated[e][:], in_=flat, func=COPY, scale=gate_cols[:, e : e + 1])
+            elif GATE_ENG[e] == "g":
+                nc.gpsimd.tensor_scalar(gated[e][:], flat, gate_cols[:, e : e + 1], 0.0, MULT, ADD)
+            else:
+                nc.vector.tensor_scalar(gated[e][:], flat, gate_cols[:, e : e + 1], None, MULT)
 
         def turn(e):
-            ps = psum.tile([P, 2, C], F32, name="turn_ps", tag="acc")
+            turn_ps[e] = psum.tile([P, 2, C], F32, name="turn_ps", tag="acc")
             for u in range(2):
-                nc.tensor.transpose(ps[:, u, :], gated[e][:].bitcast(F32)[:, u * P : (u + 1) * P], ident[:])
-            copy_on("v" if e in V_TURNS else "s", turned[:, :, e * C : (e + 1) * C], ps[:])
+                nc.tensor.transpose(turn_ps[e][:, u, :], gated[e][:].bitcast(F32)[:, u * P : (u + 1) * P], ident[:])
+
+        def turn_out(e):
+            copy_on(TURN_ENG[e], turned[:, :, e * C : (e + 1) * C], turn_ps[e][:])
 
         def scatter(u, a, b):
+            if a == 0:
+                tag = "raw%d" % WIN0_AFTER if u == 0 else "win1"
+                win[u] = shared.tile([P, D * T], F32, name="win%d" % u, tag=tag, align_bytes=64)
             nc.vector.tensor_copy(out=win[u][:].indirect(offsets[:, a // 16 : b // 16]), in_=turned[:, u, a:b])
-
-        def cast_wm():
-            wm_bf = alloc(("wm", 0), [P, D, N, PACK], BF16)
-            for o in range(D):
-                for a in range(0, N, WM_COLS):
-                    nc.scalar.copy(
-                        out=wm_bf[:, o, a : a + WM_COLS, :].rearrange("p (c i) j -> p c j i", i=4),
-                        in_=wm_raw[:, o, :, a : a + WM_COLS].rearrange("p j (c i) -> p c j i", i=4),
-                    )
-            return wm_bf
-
-        def quant_wm(wm_codes, wm_bf):
-            nc.vector.quantize_mx(
-                out=wm_codes[:].bitcast(FP8X4), scales=wm_scales[:], in_=wm_bf[:].rearrange("p o n j -> p (o n j)")
-            )
 
         nch = len(TOKEN_CUTS) - 1
         widths = [TOKEN_CUTS[k + 1] - TOKEN_CUTS[k] for k in range(nch)]
@@ -227,102 +200,92 @@ def tile_moe_mhm_gelu_kernel(tc, x_words, x_scales, w, wm, gate, offs, out):
         result = [keep.tile([P, 2, widths[k]], F32, name="result%d" % k) for k in range(nch)]
         out_v = out.rearrange("(h p) t -> p h t", p=P)
 
-        for k in range(len(GATHER_AFTER)):
-            if GATHER_AFTER[k] is None:
+        for k in range(len(GATHER_HOLD)):
+            if GATHER_HOLD[k][1] < 0:
                 gather(k)
-        def finish(e):
-            apply_gate(e)
-            if e not in LATE:
-                turn(e)
-            if e - 1 in LATE:
-                turn(e - 1)
-            gathers_after(("acts", "gated"), e)
-
-        for step in range(E + 4):
-            if step - 2 in EARLY:
-                finish(step - 2)
+        for step in range(E + 2):
             if step < E:
                 cast_w(step)
+                quant_w(step)
+                for k in range(len(GATHER_HOLD)):
+                    if GATHER_HOLD[k][1] == step:
+                        gather(k)
+                product(step)
             if 0 <= step - 1 < E:
-                quant_w(step - 1)
-                gathers_after(("raw", "bf"), step - 1)
-                expert(step - 1)
-                gathers_after(("codes",), step - 1)
-            if 0 <= step - 2 < E and step - 2 not in EARLY:
-                finish(step - 2)
-            for u in range(2):
-                for a, b in zip(CUTS[u], CUTS[u][1:]):
-                    if (b - 1) // C == step - (4 if (b - 1) // C in LATE else 3):
-                        scatter(u, a, b)
+                activate(step - 1)
+            for e in range(E):
+                if TURN_AT[e] == step and e < step - 1:
+                    turn_out(e)
+            if 0 <= step - 1 < E:
+                apply_gate(step - 1)
+                turn(step - 1)
+                if TURN_AT[step - 1] == step:
+                    turn_out(step - 1)
+            for at, u, a, b in PIECES:
+                if at == step:
+                    scatter(u, a, b)
 
-        wm_bf = cast_wm()
+        wm_bf = [shared.tile([P, N, PACK], BF16, name="wm_bf%d" % o, tag=WM_TAG[o], align_bytes=64) for o in range(D)]
+        for o in range(D):
+            interleave_round(WM_ENG[o], wm_bf[o][:], wm_raw[:, o, :, :])
 
         def side_by_side(u, k):
             t0, t1 = TOKEN_CUTS[k], TOKEN_CUTS[k + 1]
             nc.scalar.copy(out=both[:, u, :, t0:t1], in_=win[u][:].rearrange("p (o t) -> p o t", o=D)[:, :, t0:t1])
 
-        for k in range(AHEAD):
-            side_by_side(0, k)
+        t_ahead = TOKEN_CUTS[AHEAD]
+        nc.scalar.copy(out=both[:, 0, :, 0:t_ahead], in_=win[0][:].rearrange("p (o t) -> p o t", o=D)[:, :, 0:t_ahead])
         if G_SIDE:
-            t0 = TOKEN_CUTS[AHEAD]
-            nc.gpsimd.tensor_copy(out=both[:, 0, :, t0:], in_=win[0][:].rearrange("p (o t) -> p o t", o=D)[:, :, t0:])
+            nc.gpsimd.tensor_copy(out=both[:, 0, :, t_ahead:], in_=win[0][:].rearrange("p (o t) -> p o t", o=D)[:, :, t_ahead:])
         for k in range(nch):
             side_by_side(1, k)
             if k + AHEAD < nch and not G_SIDE:
                 side_by_side(0, k + AHEAD)
 
-        wm_codes = shared.tile([P, D * N], U32, name="wm_codes", tag="turned" if WM_SLOT else "wmc", align_bytes=64)
-        quant_wm(wm_codes, wm_bf)
+        for o in range(D):
+            nc.vector.quantize_mx(
+                out=wm_codes[:, o * N : (o + 1) * N].bitcast(FP8X4), scales=wm_scales[:, o * N : (o + 1) * N],
+                in_=wm_bf[o][:].rearrange("p n j -> p (n j)"),
+            )
 
         def interleave(k, eng):
             copy_on(eng, c_bf[k][:], both[:, :, :, TOKEN_CUTS[k] : TOKEN_CUTS[k + 1]].rearrange("p u o t -> p o t u"))
 
-        def merge(k):
-            t0, t1 = TOKEN_CUTS[k], TOKEN_CUTS[k + 1]
-            width = t1 - t0
+        def quant_c(k):
             nc.vector.quantize_mx(
                 out=c_codes[k][:].bitcast(FP8X4), scales=c_scales[k][:],
                 in_=c_bf[k][:].rearrange("p o t u -> p (o t u)").bitcast(BF16),
             )
-            acc = psum.tile([P, 2, width], F32, name="acc", tag="acc")
+
+        def merge_pass(acc, k, h, o):
+            ncols = slice(o * N + h * P, o * N + (h + 1) * P)
+            tcols = slice(o * widths[k], (o + 1) * widths[k])
+            nc.tensor.matmul_mx(
+                out=acc, lhsT=wm_codes[:, ncols].bitcast(FP8X4), lhsT_scale=wm_scales[:, ncols],
+                rhs=c_codes[k][:, tcols].bitcast(FP8X4), rhs_scale=c_scales[k][:, tcols],
+                start=(o == 0), stop=(o == D - 1),
+            )
+
+        def merge(k):
+            t0, t1 = TOKEN_CUTS[k], TOKEN_CUTS[k + 1]
+            quant_c(k)
+            acc = psum.tile([P, 2, widths[k]], F32, name="acc", tag="acc")
             for h in range(2):
                 for o in range(D):
-                    ncols = slice(o * N + h * P, o * N + (h + 1) * P)
-                    tcols = slice(o * width, (o + 1) * width)
-                    nc.tensor.matmul_mx(
-                        out=acc[:, h, :], lhsT=wm_codes[:, ncols].bitcast(FP8X4), lhsT_scale=wm_scales[:, ncols],
-                        rhs=c_codes[k][:, tcols].bitcast(FP8X4), rhs_scale=c_scales[k][:, tcols],
-                        start=(o == 0), stop=(o == D - 1),
-                    )
+                    merge_pass(acc[:, h, :], k, h, o)
             copy_on(RES_ENG[k], result[k][:], acc[:])
-            (nc.scalar if STORE_Q[k] == "a" else nc.sync).dma_start(out=out_v[:, :, t0:t1], in_=result[k][:])
+            nc.sync.dma_start(out=out_v[:, :, t0:t1], in_=result[k][:])
 
         def last_chunk():
             k = nch - 1
             t0, t1 = TOKEN_CUTS[k], TOKEN_CUTS[k + 1]
-            width = t1 - t0
-            accs = [psum.tile([P, width], F32, name="acc_last%d" % h, tag="last", bufs=2) for h in range(2)]
-            if not LAST_SPLIT:
-                nc.vector.quantize_mx(
-                    out=c_codes[k][:].bitcast(FP8X4), scales=c_scales[k][:],
-                    in_=c_bf[k][:].rearrange("p o t u -> p (o t u)").bitcast(BF16),
-                )
+            accs = [psum.tile([P, widths[k]], F32, name="acc_last%d" % h, tag="last", bufs=2) for h in range(2)]
+            quant_c(k)
             for o in range(D):
-                tcols = slice(o * width, (o + 1) * width)
-                if LAST_SPLIT:
-                    nc.vector.quantize_mx(
-                        out=c_codes[k][:, tcols].bitcast(FP8X4), scales=c_scales[k][:, tcols],
-                        in_=c_bf[k][:, o, :, :].rearrange("p t u -> p (t u)").bitcast(BF16),
-                    )
                 for h in range(2):
-                    ncols = slice(o * N + h * P, o * N + (h + 1) * P)
-                    nc.tensor.matmul_mx(
-                        out=accs[h][:], lhsT=wm_codes[:, ncols].bitcast(FP8X4), lhsT_scale=wm_scales[:, ncols],
-                        rhs=c_codes[k][:, tcols].bitcast(FP8X4), rhs_scale=c_scales[k][:, tcols],
-                        start=(o == 0), stop=(o == D - 1),
-                    )
+                    merge_pass(accs[h][:], k, h, o)
             nc.scalar.copy(out=result[k][:, 0, :], in_=accs[0][:])
-            (nc.scalar if LAST_Q else nc.sync).dma_start(out=out_v[:, 0, t0:t1], in_=result[k][:, 0, :])
+            nc.scalar.dma_start(out=out_v[:, 0, t0:t1], in_=result[k][:, 0, :])
             nc.vector.tensor_copy(out=result[k][:, 1, :], in_=accs[1][:])
             nc.sync.dma_start(out=out_v[:, 1, t0:t1], in_=result[k][:, 1, :])
 
@@ -330,7 +293,4 @@ def tile_moe_mhm_gelu_kernel(tc, x_words, x_scales, w, wm, gate, offs, out):
             interleave(step, "s" if step in S_CHUNKS else "v")
             if step >= 1:
                 merge(step - 1)
-        if LAST_PLAIN:
-            merge(nch - 1)
-        else:
-            last_chunk()
+        last_chunk()

@@ -22,11 +22,15 @@ ADD = mybir.AluOpType.add
 P = 128
 PACK = 4
 SCALE_CUTS = [0, 768, 1536]
-GATHER_CUTS = [0, 256, 640, 1152, 1536]
+GATHER_CUTS = [0, 256, 768, 1152, 1536]
 GATHER_HOLD = [(None, -1), (None, -1), ("h", 1), ("raw2", 2)]
-QUANT_CUTS = [[0, 512]] * 12
+QUANT_CUTS = [[0, 512]] * 3 + [[0, 256, 512]] * 9
 X_AFTER = 1
-BF_TAG = ["h","h","bf","bf","bf","bf","bf","bf","bf","bf","bf","bf"]
+SCALE_HOLD = [(None, -1), (None, -1)]
+GATE_V = 320
+WARM = 0
+RAW_TAG = [None,None,None,None,None,None,None,None,None,None,None,None]
+BF_TAG = [["h"],["h"],["bf"],["a0","bf"],["a1","bf"],["a0","bf"],["a1","bf"],["a0","bf"],["a1","bf"],["a0","bf"],["a1","bf"],["a0","bf"]]
 ACTS_TAG = ["raw1",None,"raw3",None,None,None,None,None,None,None,None,None]
 GATED_TAG = [None,None,None,None,None,None,None,None,None,None,None,"last"]
 WM_TAG = ["bf", "last"]
@@ -36,7 +40,7 @@ GATE_AFTER = 1
 TOKEN_CUTS = [0, 128, 256, 384, 512, 640, 768]
 SCALES_FIRST = False
 LOAD_CUTS = [[0, 256, 512], [0, 256, 512]] + [[0, 512]] * 10
-CASTS = [[["s",0,256],["s",256,512]],[["s",0,256],["s",256,384],["v",384,512]],[["s",0,128],["v",128,512]],[["s",0,288],["g",288,512]],[["s",0,288],["g",288,512]],[["s",0,288],["g",288,512]],[["s",0,288],["g",288,512]],[["s",0,288],["g",288,512]],[["s",0,288],["g",288,512]],[["s",0,288],["g",288,512]],[["s",0,288],["g",288,512]],[["s",0,288],["g",288,512]]]
+CASTS = [[["s",0,256],["s",256,512]],[["s",0,256],["s",256,384],["v",384,512]],[["s",0,128],["v",128,512]],[["s",0,256],["s",256,288],["g",288,512]],[["s",0,256],["s",256,288],["g",288,512]],[["s",0,256],["s",256,288],["g",288,512]],[["s",0,256],["s",256,288],["g",288,512]],[["s",0,256],["s",256,288],["g",288,512]],[["s",0,256],["s",256,288],["g",288,512]],[["s",0,256],["s",256,288],["g",288,512]],[["s",0,256],["s",256,288],["g",288,512]],[["s",0,256],["s",256,288],["g",288,512]]]
 GATE_ENG = "gvhhhhhhhhhh"
 TURN_ENG = "ssssssssssss"
 PIECES = [(2, 1, 0, 256), (3, 0, 0, 192), (4, 0, 192, 384), (5, 1, 256, 512), (6, 0, 384, 640), (7, 1, 512, 768), (8, 0, 640, 896), (9, 1, 768, 1024), (10, 0, 896, 1152), (11, 1, 1024, 1280), (12, 0, 1152, 1344), (13, 0, 1344, 1536), (13, 1, 1280, 1536)]
@@ -53,18 +57,23 @@ def tile_moe_mhm_gelu_kernel(tc, x_words, x_scales, w, wm, gate, offs, out):
         keep = ctx.enter_context(tc.tile_pool(name="keep", bufs=1))
         ring = ctx.enter_context(tc.tile_pool(name="ring", bufs=3))
         shared = ctx.enter_context(tc.tile_pool(name="shared", bufs=1))
+        stacked = ctx.enter_context(tc.tile_pool(name="stacked", bufs=1))
         psum = ctx.enter_context(tc.psum_pool(name="psum", bufs=3))
 
         offsets = keep.tile([P, S // 16], U16, name="offsets")
         xw = keep.tile([P, D * T], I32, name="xw", align_bytes=64)
         xs = keep.tile([P, D * T], U8, name="xs", align_bytes=64)
-        gs = keep.tile([P, S], U8, name="gs", align_bytes=64)
         gate_rows = keep.tile([P, C], F32, name="gate_rows")
         gate_cols = keep.tile([P, E], F32, name="gate_cols")
         ident = keep.tile([P, P], F32, name="ident")
         warm_in = keep.tile([P, 8], F32, name="warm_in")
         warm_out = keep.tile([P, 8], F32, name="warm_out")
-        w_raw = [shared.tile([P, PACK, H], F32, name="w_raw%d" % e, tag="raw%d" % e, align_bytes=64) for e in range(E)]
+        def place(shape, dtype, name, tag):
+            if isinstance(tag, int):
+                return stacked.tile(shape, dtype, name=name, offset=tag, align_bytes=64)
+            return shared.tile(shape, dtype, name=name, tag=tag, align_bytes=64)
+
+        w_raw = [place([P, PACK, H], F32, "w_raw%d" % e, RAW_TAG[e] if RAW_TAG[e] is not None else "raw%d" % e) for e in range(E)]
         wm_raw = keep.tile([P, D, PACK, N], F32, name="wm_raw")
         wm_scales = keep.tile([P, D * N], U8, name="wm_scales", align_bytes=64)
         wm_codes = keep.tile([P, D * N], U32, name="wm_codes", align_bytes=64)
@@ -120,43 +129,57 @@ def tile_moe_mhm_gelu_kernel(tc, x_words, x_scales, w, wm, gate, offs, out):
             else:
                 copy_on(eng, dst.rearrange("p (c i) j -> p c j i", i=4), src.rearrange("p j (c i) -> p c j i", i=4))
 
-        for a, b in zip(SCALE_CUTS, SCALE_CUTS[1:]):
-            nc.vector.tensor_copy(out=gs[:, a:b], in_=xs[:].indirect(offsets[:, a // 16 : b // 16]))
+        gs = {}
+
+        def gather_scales(k):
+            a, b = SCALE_CUTS[k], SCALE_CUTS[k + 1]
+            gs[k] = place([P, b - a], U8, "gs%d" % k, SCALE_HOLD[k][0] or "gs%d" % k)
+            nc.vector.tensor_copy(out=gs[k][:], in_=xs[:].indirect(offsets[:, a // 16 : b // 16]))
+
+        for k in range(len(SCALE_HOLD)):
+            if SCALE_HOLD[k][1] < 0:
+                gather_scales(k)
 
         gw, w_bf, w_codes, w_scales, sums, acts, gated, turn_ps, win = {}, {}, {}, {}, {}, {}, {}, {}, {}
 
         def gather(k):
             a, b = GATHER_CUTS[k], GATHER_CUTS[k + 1]
-            gw[k] = shared.tile([P, b - a], U32, name="gw%d" % k, tag=GATHER_HOLD[k][0] or "gw%d" % k, align_bytes=64)
+            gw[k] = place([P, b - a], U32, "gw%d" % k, GATHER_HOLD[k][0] or "gw%d" % k)
             nc.vector.tensor_copy(out=gw[k][:], in_=xw[:].bitcast(U32).indirect(offsets[:, a // 16 : b // 16]))
 
         def cast_w(e):
-            w_bf[e] = shared.tile([P, H, PACK], BF16, name="w_bf%d" % e, tag=BF_TAG[e], align_bytes=64)
+            cuts = QUANT_CUTS[e]
+            w_bf[e] = [
+                shared.tile([P, cuts[k + 1] - cuts[k], PACK], BF16, name="w_bf%d_%d" % (e, k), tag=BF_TAG[e][k], align_bytes=64)
+                for k in range(len(cuts) - 1)
+            ]
             for eng, a, b in CASTS[e]:
-                interleave_round(eng, w_bf[e][:, a:b, :], w_raw[e][:, :, a:b])
+                k = max(i for i in range(len(cuts)) if cuts[i] <= a)
+                interleave_round(eng, w_bf[e][k][:, a - cuts[k] : b - cuts[k], :], w_raw[e][:, :, a:b])
 
         def quant_w(e):
             w_codes[e] = ring.tile([P, H], U32, name="w_codes", align_bytes=64)
             w_scales[e] = ring.tile([P, H], U8, name="w_scales", align_bytes=64)
-            for a, b in zip(QUANT_CUTS[e], QUANT_CUTS[e][1:]):
+            for k, (a, b) in enumerate(zip(QUANT_CUTS[e], QUANT_CUTS[e][1:])):
                 nc.vector.quantize_mx(
                     out=w_codes[e][:, a:b].bitcast(FP8X4), scales=w_scales[e][:, a:b],
-                    in_=w_bf[e][:, a:b, :].rearrange("p c j -> p (c j)"),
+                    in_=w_bf[e][k][:].rearrange("p c j -> p (c j)"),
                 )
 
         def product(e):
-            slots = slice(e * C, (e + 1) * C)
+            ks = max(i for i in range(len(SCALE_CUTS)) if SCALE_CUTS[i] <= e * C)
+            scale_bytes = gs[ks][:, e * C - SCALE_CUTS[ks] : (e + 1) * C - SCALE_CUTS[ks]]
             k = max(i for i in range(len(GATHER_CUTS)) if GATHER_CUTS[i] <= e * C)
             words = gw[k][:, e * C - GATHER_CUTS[k] : (e + 1) * C - GATHER_CUTS[k]]
             sums[e] = psum.tile([P, H], F32, name="sums")
             nc.tensor.matmul_mx(
-                out=sums[e][:], lhsT=words.bitcast(FP8X4), lhsT_scale=gs[:, slots],
+                out=sums[e][:], lhsT=words.bitcast(FP8X4), lhsT_scale=scale_bytes,
                 rhs=w_codes[e][:].bitcast(FP8X4), rhs_scale=w_scales[e][:], start=True, stop=True,
             )
 
         def activate(e):
-            if ACTS_TAG[e]:
-                acts[e] = shared.tile([P, 2, P, 2], F32, name="acts%d" % e, tag=ACTS_TAG[e], align_bytes=64)
+            if ACTS_TAG[e] is not None:
+                acts[e] = place([P, 2, P, 2], F32, "acts%d" % e, ACTS_TAG[e])
             else:
                 acts[e] = ring.tile([P, 2, P, 2], F32, name="acts", align_bytes=64)
             nc.scalar.activation(out=acts[e][:], in_=sums[e][:].rearrange("s (m u v) -> s u m v", u=2, v=2), func=GELU)
@@ -168,7 +191,7 @@ def tile_moe_mhm_gelu_kernel(tc, x_words, x_scales, w, wm, gate, offs, out):
                 gated[e] = ring.tile([P, H], BF16, name="gated", align_bytes=64)
             flat = acts[e][:].rearrange("s u m v -> s (u m v)")
             if GATE_ENG[e] == "h":
-                half = H // 2
+                half = GATE_V
                 nc.vector.tensor_scalar(gated[e][:, :half], flat[:, :half], gate_cols[:, e : e + 1], None, MULT)
                 nc.scalar.activation(out=gated[e][:, half:], in_=flat[:, half:], func=COPY, scale=gate_cols[:, e : e + 1])
             elif GATE_ENG[e] == "s":
@@ -207,6 +230,9 @@ def tile_moe_mhm_gelu_kernel(tc, x_words, x_scales, w, wm, gate, offs, out):
             if step < E:
                 cast_w(step)
                 quant_w(step)
+                for k in range(len(SCALE_HOLD)):
+                    if SCALE_HOLD[k][1] == step:
+                        gather_scales(k)
                 for k in range(len(GATHER_HOLD)):
                     if GATHER_HOLD[k][1] == step:
                         gather(k)
@@ -221,6 +247,9 @@ def tile_moe_mhm_gelu_kernel(tc, x_words, x_scales, w, wm, gate, offs, out):
                 turn(step - 1)
                 if TURN_AT[step - 1] == step:
                     turn_out(step - 1)
+            for k in range(len(GATHER_HOLD)):
+                if GATHER_HOLD[k][1] == step + 0.5:
+                    gather(k)
             for at, u, a, b in PIECES:
                 if at == step:
                     scatter(u, a, b)
@@ -289,8 +318,18 @@ def tile_moe_mhm_gelu_kernel(tc, x_words, x_scales, w, wm, gate, offs, out):
             nc.vector.tensor_copy(out=result[k][:, 1, :], in_=accs[1][:])
             nc.sync.dma_start(out=out_v[:, 1, t0:t1], in_=result[k][:, 1, :])
 
+        for k in S_CHUNKS:
+            interleave(k, "s")
+        if WARM:
+            warm_ps = psum.tile([P, H], F32, name="warm_ps", tag="sums")
+            for n in range(WARM):
+                nc.tensor.matmul_mx(
+                    out=warm_ps[:], lhsT=wm_codes[:, N : N + P].bitcast(FP8X4), lhsT_scale=wm_scales[:, N : N + P],
+                    rhs=wm_codes[:].bitcast(FP8X4), rhs_scale=wm_scales[:], start=True, stop=True,
+                )
         for step in range(nch):
-            interleave(step, "s" if step in S_CHUNKS else "v")
+            if step not in S_CHUNKS:
+                interleave(step, "v")
             if step >= 1:
                 merge(step - 1)
         last_chunk()

@@ -23,15 +23,14 @@ P = 128
 PACK = 4
 SCALE_CUTS = [0, 768, 1536]
 GATHER_CUTS = [0, 256, 768, 1152, 1536]
-GATHER_HOLD = [(None, -1), (None, -1), ("h", 1), ("raw2", 2)]
-QUANT_CUTS = [[0, 512]] * 3 + [[0, 256, 512]] * 9
+GATHER_HOLD = [(None, -1), (None, -1), ("h", 1), ("raw2_0", 2)]
+QUANT_CUTS = [[0,512],[0,512],[0,512],[0,512],[0,256,512],[0,256,512],[0,256,512],[0,256,512],[0,256,512],[0,256,512],[0,256,512],[0,256,512]]
 X_AFTER = 1
 SCALE_HOLD = [(None, -1), (None, -1)]
 GATE_V = 320
 WARM = 0
-RAW_TAG = [None,None,None,None,None,None,None,None,None,None,None,None]
-BF_TAG = [["h"],["h"],["bf"],["a0","bf"],["a1","bf"],["a0","bf"],["a1","bf"],["a0","bf"],["a1","bf"],["a0","bf"],["a1","bf"],["a0","bf"]]
-ACTS_TAG = ["raw1",None,"raw3",None,None,None,None,None,None,None,None,None]
+BF_TAG = [["h"],["h"],["bf"],["bf"],["a1","bf"],["a0","bf"],["a1","bf"],["a0","bf"],["a1","bf"],["a0","bf"],["a1","bf"],["a0","bf"]]
+ACTS_TAG = ["raw1_1",None,"raw3_0",None,None,None,None,None,None,None,None,None]
 GATED_TAG = [None,None,None,None,None,None,None,None,None,None,None,"last"]
 WM_TAG = ["bf", "last"]
 G_SIDE = False
@@ -39,12 +38,12 @@ TURN_AT = [2,2,4,5,6,7,8,9,10,11,12,13]
 GATE_AFTER = 1
 TOKEN_CUTS = [0, 128, 256, 384, 512, 640, 768]
 SCALES_FIRST = False
-LOAD_CUTS = [[0, 256, 512], [0, 256, 512]] + [[0, 512]] * 10
-CASTS = [[["s",0,256],["s",256,512]],[["s",0,256],["s",256,384],["v",384,512]],[["s",0,128],["v",128,512]],[["s",0,256],["s",256,288],["g",288,512]],[["s",0,256],["s",256,288],["g",288,512]],[["s",0,256],["s",256,288],["g",288,512]],[["s",0,256],["s",256,288],["g",288,512]],[["s",0,256],["s",256,288],["g",288,512]],[["s",0,256],["s",256,288],["g",288,512]],[["s",0,256],["s",256,288],["g",288,512]],[["s",0,256],["s",256,288],["g",288,512]],[["s",0,256],["s",256,288],["g",288,512]]]
+LOAD_CUTS = [[0,256,512],[0,256,512],[0,512],[0,512],[0,512],[0,512],[0,512],[0,512],[0,512],[0,512],[0,512],[0,512]]
+CASTS = [[["s",0,256],["s",256,512]],[["s",0,256],["s",256,384],["v",384,512]],[["s",0,128],["v",128,512]],[["s",0,304],["g",304,512]],[["s",0,256],["s",256,272],["g",272,512]],[["s",0,256],["s",256,272],["g",272,512]],[["s",0,256],["s",256,272],["g",272,512]],[["s",0,256],["s",256,272],["g",272,512]],[["s",0,256],["s",256,272],["g",272,512]],[["s",0,256],["s",256,272],["g",272,512]],[["s",0,256],["s",256,272],["g",272,512]],[["s",0,256],["s",256,272],["g",272,512]]]
 GATE_ENG = "gvhhhhhhhhhh"
 TURN_ENG = "ssssssssssss"
 PIECES = [(2, 1, 0, 256), (3, 0, 0, 192), (4, 0, 192, 384), (5, 1, 256, 512), (6, 0, 384, 640), (7, 1, 512, 768), (8, 0, 640, 896), (9, 1, 768, 1024), (10, 0, 896, 1152), (11, 1, 1024, 1280), (12, 0, 1152, 1344), (13, 0, 1344, 1536), (13, 1, 1280, 1536)]
-WIN0_AFTER = 3
+WIN0_AFTER = "raw3_0"
 WM_ENG = "gs"
 AHEAD = 6
 S_CHUNKS = [4, 5]
@@ -73,7 +72,10 @@ def tile_moe_mhm_gelu_kernel(tc, x_words, x_scales, w, wm, gate, offs, out):
                 return stacked.tile(shape, dtype, name=name, offset=tag, align_bytes=64)
             return shared.tile(shape, dtype, name=name, tag=tag, align_bytes=64)
 
-        w_raw = [place([P, PACK, H], F32, "w_raw%d" % e, RAW_TAG[e] if RAW_TAG[e] is not None else "raw%d" % e) for e in range(E)]
+        w_raw = [
+            [place([P, PACK, LOAD_CUTS[e][k + 1] - LOAD_CUTS[e][k]], F32, "w_raw%d_%d" % (e, k), "raw%d_%d" % (e, k)) for k in range(len(LOAD_CUTS[e]) - 1)]
+            for e in range(E)
+        ]
         wm_raw = keep.tile([P, D, PACK, N], F32, name="wm_raw")
         wm_scales = keep.tile([P, D * N], U8, name="wm_scales", align_bytes=64)
         wm_codes = keep.tile([P, D * N], U32, name="wm_codes", align_bytes=64)
@@ -82,7 +84,7 @@ def tile_moe_mhm_gelu_kernel(tc, x_words, x_scales, w, wm, gate, offs, out):
 
         def load_w(e, k):
             a, b = LOAD_CUTS[e][k], LOAD_CUTS[e][k + 1]
-            nc.sync.dma_start(out=w_raw[e][:, :, a:b], in_=w[e].rearrange("(p j) c -> p j c", j=PACK)[:, :, a:b])
+            nc.sync.dma_start(out=w_raw[e][k][:], in_=w[e].rearrange("(p j) c -> p j c", j=PACK)[:, :, a:b])
 
         nc.gpsimd.memset(xs[:].bitcast(I32), 0)
         nc.vector.memset(gate_rows[:], 0.0)
@@ -155,7 +157,9 @@ def tile_moe_mhm_gelu_kernel(tc, x_words, x_scales, w, wm, gate, offs, out):
             ]
             for eng, a, b in CASTS[e]:
                 k = max(i for i in range(len(cuts)) if cuts[i] <= a)
-                interleave_round(eng, w_bf[e][k][:, a - cuts[k] : b - cuts[k], :], w_raw[e][:, :, a:b])
+                n = max(i for i in range(len(LOAD_CUTS[e])) if LOAD_CUTS[e][i] <= a)
+                first = LOAD_CUTS[e][n]
+                interleave_round(eng, w_bf[e][k][:, a - cuts[k] : b - cuts[k], :], w_raw[e][n][:, :, a - first : b - first])
 
         def quant_w(e):
             w_codes[e] = ring.tile([P, H], U32, name="w_codes", align_bytes=64)
@@ -171,7 +175,7 @@ def tile_moe_mhm_gelu_kernel(tc, x_words, x_scales, w, wm, gate, offs, out):
             scale_bytes = gs[ks][:, e * C - SCALE_CUTS[ks] : (e + 1) * C - SCALE_CUTS[ks]]
             k = max(i for i in range(len(GATHER_CUTS)) if GATHER_CUTS[i] <= e * C)
             words = gw[k][:, e * C - GATHER_CUTS[k] : (e + 1) * C - GATHER_CUTS[k]]
-            sums[e] = psum.tile([P, H], F32, name="sums")
+            sums[e] = psum.tile([P, H], F32, name="sums%d" % e, tag="expert%d" % (e % 2), bufs=1)
             nc.tensor.matmul_mx(
                 out=sums[e][:], lhsT=words.bitcast(FP8X4), lhsT_scale=scale_bytes,
                 rhs=w_codes[e][:].bitcast(FP8X4), rhs_scale=w_scales[e][:], start=True, stop=True,
@@ -202,7 +206,7 @@ def tile_moe_mhm_gelu_kernel(tc, x_words, x_scales, w, wm, gate, offs, out):
                 nc.vector.tensor_scalar(gated[e][:], flat, gate_cols[:, e : e + 1], None, MULT)
 
         def turn(e):
-            turn_ps[e] = psum.tile([P, 2, C], F32, name="turn_ps", tag="acc")
+            turn_ps[e] = psum.tile([P, 2, C], F32, name="turn_ps%d" % e, tag="expert%d" % (e % 2), bufs=1)
             for u in range(2):
                 nc.tensor.transpose(turn_ps[e][:, u, :], gated[e][:].bitcast(F32)[:, u * P : (u + 1) * P], ident[:])
 
@@ -211,7 +215,7 @@ def tile_moe_mhm_gelu_kernel(tc, x_words, x_scales, w, wm, gate, offs, out):
 
         def scatter(u, a, b):
             if a == 0:
-                tag = "raw%d" % WIN0_AFTER if u == 0 else "win1"
+                tag = WIN0_AFTER if u == 0 else "win1"
                 win[u] = shared.tile([P, D * T], F32, name="win%d" % u, tag=tag, align_bytes=64)
             nc.vector.tensor_copy(out=win[u][:].indirect(offsets[:, a // 16 : b // 16]), in_=turned[:, u, a:b])
 
@@ -321,7 +325,7 @@ def tile_moe_mhm_gelu_kernel(tc, x_words, x_scales, w, wm, gate, offs, out):
         for k in S_CHUNKS:
             interleave(k, "s")
         if WARM:
-            warm_ps = psum.tile([P, H], F32, name="warm_ps", tag="sums")
+            warm_ps = psum.tile([P, H], F32, name="warm_ps", tag="expert0", bufs=1)
             for n in range(WARM):
                 nc.tensor.matmul_mx(
                     out=warm_ps[:], lhsT=wm_codes[:, N : N + P].bitcast(FP8X4), lhsT_scale=wm_scales[:, N : N + P],

@@ -24,11 +24,12 @@ PACK = 4
 SCALE_CUTS = [0, 768, 1536]
 GATHER_CUTS = [0, 256, 768, 1152, 1536]
 GATHER_HOLD = [(None, -1), (None, -1), ("h", 1), ("raw2_0", 2)]
-QUANT_CUTS = [[0,512],[0,512],[0,512],[0,512],[0,256,512],[0,256,512],[0,256,512],[0,256,512],[0,256,512],[0,256,512],[0,256,512],[0,256,512]]
+QUANT_CUTS = [[0,512],[0,512],[0,512],[0,512],[0,512],[0,512],[0,512],[0,512],[0,512],[0,512],[0,512],[0,512]]
 X_AFTER = 1
 SCALE_HOLD = [(None, -1), (None, -1)]
 GATE_V = 320
-WARM = 0
+WARM = 2
+DIRECT = 0
 BF_TAG = [["h"],["h"],["bf"],["bf"],["a1","bf"],["a0","bf"],["a1","bf"],["a0","bf"],["a1","bf"],["a0","bf"],["a1","bf"],["a0","bf"]]
 ACTS_TAG = ["raw1_1",None,"raw3_0",None,None,None,None,None,None,None,None,None]
 GATED_TAG = [None,None,None,None,None,None,None,None,None,None,None,"last"]
@@ -39,11 +40,18 @@ GATE_AFTER = 1
 TOKEN_CUTS = [0, 128, 256, 384, 512, 640, 768]
 SCALES_FIRST = False
 LOAD_CUTS = [[0,256,512],[0,256,512],[0,512],[0,512],[0,512],[0,512],[0,512],[0,512],[0,512],[0,512],[0,512],[0,512]]
-CASTS = [[["s",0,256],["s",256,512]],[["s",0,256],["s",256,384],["v",384,512]],[["s",0,128],["v",128,512]],[["s",0,304],["g",304,512]],[["s",0,256],["s",256,272],["g",272,512]],[["s",0,256],["s",256,272],["g",272,512]],[["s",0,256],["s",256,272],["g",272,512]],[["s",0,256],["s",256,272],["g",272,512]],[["s",0,256],["s",256,272],["g",272,512]],[["s",0,256],["s",256,272],["g",272,512]],[["s",0,256],["s",256,272],["g",272,512]],[["s",0,256],["s",256,272],["g",272,512]]]
-GATE_ENG = "gvhhhhhhhhhh"
+CASTS = [[["s",0,256],["s",256,512]],[["s",0,256],["s",256,384],["v",384,512]],[["s",0,128],["v",128,512]],[["s",208,512],["g",0,208]],[["s",0,272],["g",272,512]],[["s",240,512],["g",0,240]],[["s",0,272],["g",272,512]],[["s",240,512],["g",0,240]],[["s",0,272],["g",272,512]],[["s",240,512],["g",0,240]],[["s",0,272],["g",272,512]],[["s",240,512],["g",0,240]]]
+GATE_ENG = "svhhhhhhhhhh"
 TURN_ENG = "ssssssssssss"
 PIECES = [(2, 1, 0, 256), (3, 0, 0, 192), (4, 0, 192, 384), (5, 1, 256, 512), (6, 0, 384, 640), (7, 1, 512, 768), (8, 0, 640, 896), (9, 1, 768, 1024), (10, 0, 896, 1152), (11, 1, 1024, 1280), (12, 0, 1152, 1344), (13, 0, 1344, 1536), (13, 1, 1280, 1536)]
 WIN0_AFTER = "raw3_0"
+WIN1_AFTER = "win1"
+LOAD_BACK = []
+S_COLS = 272
+WM_SPLIT = False
+U_SPLIT = {}
+V_SIDE = 1
+OWN_BANK = {3: "expert1", 4: "spare"}
 WM_ENG = "gs"
 AHEAD = 6
 S_CHUNKS = [4, 5]
@@ -76,7 +84,11 @@ def tile_moe_mhm_gelu_kernel(tc, x_words, x_scales, w, wm, gate, offs, out):
             [place([P, PACK, LOAD_CUTS[e][k + 1] - LOAD_CUTS[e][k]], F32, "w_raw%d_%d" % (e, k), "raw%d_%d" % (e, k)) for k in range(len(LOAD_CUTS[e]) - 1)]
             for e in range(E)
         ]
-        wm_raw = keep.tile([P, D, PACK, N], F32, name="wm_raw")
+        if WM_SPLIT:
+            wm_raw = [keep.tile([P, PACK, N], F32, name="wm_raw%d" % o) for o in range(D)]
+        else:
+            wm_whole = keep.tile([P, D, PACK, N], F32, name="wm_raw")
+            wm_raw = [wm_whole[:, o, :, :] for o in range(D)]
         wm_scales = keep.tile([P, D * N], U8, name="wm_scales", align_bytes=64)
         wm_codes = keep.tile([P, D * N], U32, name="wm_codes", align_bytes=64)
         turned = keep.tile([P, 2, S], F32, name="turned", align_bytes=64)
@@ -99,7 +111,7 @@ def tile_moe_mhm_gelu_kernel(tc, x_words, x_scales, w, wm, gate, offs, out):
         make_identity(nc, ident[:])
         nc.scalar.activation(out=warm_out[:], in_=warm_in[:], func=GELU)
 
-        pieces = [(e, k) for e in range(E) for k in range(len(LOAD_CUTS[e]) - 1)]
+        pieces = [(e, k) for e in range(E) for k in (reversed(range(len(LOAD_CUTS[e]) - 1)) if e in LOAD_BACK else range(len(LOAD_CUTS[e]) - 1))]
         for n, (e, k) in enumerate(pieces):
             if n > 0 or SCALES_FIRST:
                 load_w(e, k)
@@ -110,10 +122,14 @@ def tile_moe_mhm_gelu_kernel(tc, x_words, x_scales, w, wm, gate, offs, out):
                     out=xw[:].rearrange("p (o t) -> p o t", o=D),
                     in_=x_words.rearrange("o p t d -> p o (t d)").bitcast(I32),
                 )
-        nc.sync.dma_start(
-            out=wm_raw[:].rearrange("p o j n -> p o (j n)"),
-            in_=wm.rearrange("(o p j) n -> p o (j n)", o=D, j=PACK),
-        )
+        if WM_SPLIT:
+            for o in range(D):
+                nc.sync.dma_start(out=wm_raw[o][:], in_=wm[o * H : (o + 1) * H].rearrange("(p j) n -> p j n", j=PACK))
+        else:
+            nc.sync.dma_start(
+                out=wm_whole[:].rearrange("p o j n -> p o (j n)"),
+                in_=wm.rearrange("(o p j) n -> p o (j n)", o=D, j=PACK),
+            )
 
         gate_ps = psum.tile([P, P], F32, name="gate_ps", tag="acc")
         nc.tensor.transpose(gate_ps[:], gate_rows[:], ident[:])
@@ -149,7 +165,15 @@ def tile_moe_mhm_gelu_kernel(tc, x_words, x_scales, w, wm, gate, offs, out):
             gw[k] = place([P, b - a], U32, "gw%d" % k, GATHER_HOLD[k][0] or "gw%d" % k)
             nc.vector.tensor_copy(out=gw[k][:], in_=xw[:].bitcast(U32).indirect(offsets[:, a // 16 : b // 16]))
 
+        rounded = keep.tile([P, H + S_COLS, PACK], BF16, name="rounded", align_bytes=64)
+
         def cast_w(e):
+            if e >= 2:
+                base = S_COLS * (e % 2)
+                w_bf[e] = [rounded[:, base : base + H, :]]
+                for eng, a, b in CASTS[e]:
+                    interleave_round(eng, w_bf[e][0][:, a:b, :], w_raw[e][0][:, :, a:b])
+                return
             cuts = QUANT_CUTS[e]
             w_bf[e] = [
                 shared.tile([P, cuts[k + 1] - cuts[k], PACK], BF16, name="w_bf%d_%d" % (e, k), tag=BF_TAG[e][k], align_bytes=64)
@@ -167,7 +191,7 @@ def tile_moe_mhm_gelu_kernel(tc, x_words, x_scales, w, wm, gate, offs, out):
             for k, (a, b) in enumerate(zip(QUANT_CUTS[e], QUANT_CUTS[e][1:])):
                 nc.vector.quantize_mx(
                     out=w_codes[e][:, a:b].bitcast(FP8X4), scales=w_scales[e][:, a:b],
-                    in_=w_bf[e][k][:].rearrange("p c j -> p (c j)"),
+                    in_=w_bf[e][k][:, :, :].rearrange("p c j -> p (c j)"),
                 )
 
         def product(e):
@@ -206,16 +230,25 @@ def tile_moe_mhm_gelu_kernel(tc, x_words, x_scales, w, wm, gate, offs, out):
                 nc.vector.tensor_scalar(gated[e][:], flat, gate_cols[:, e : e + 1], None, MULT)
 
         def turn(e):
+            if e in U_SPLIT:
+                turn_ps[e] = [psum.tile([P, C], F32, name="turn_a%d" % e, tag="expert%d" % (e % 2), bufs=1), psum.tile([P, C], F32, name="turn_b%d" % e, tag="acc")]
+                for n, u in enumerate(U_SPLIT[e]):
+                    nc.tensor.transpose(turn_ps[e][n][:], gated[e][:].bitcast(F32)[:, u * P : (u + 1) * P], ident[:])
+                return
             turn_ps[e] = psum.tile([P, 2, C], F32, name="turn_ps%d" % e, tag="expert%d" % (e % 2), bufs=1)
             for u in range(2):
                 nc.tensor.transpose(turn_ps[e][:, u, :], gated[e][:].bitcast(F32)[:, u * P : (u + 1) * P], ident[:])
 
         def turn_out(e):
+            if e in U_SPLIT:
+                for n, u in enumerate(U_SPLIT[e]):
+                    copy_on(TURN_ENG[e], turned[:, u, e * C : (e + 1) * C], turn_ps[e][n][:])
+                return
             copy_on(TURN_ENG[e], turned[:, :, e * C : (e + 1) * C], turn_ps[e][:])
 
         def scatter(u, a, b):
             if a == 0:
-                tag = WIN0_AFTER if u == 0 else "win1"
+                tag = WIN0_AFTER if u == 0 else WIN1_AFTER
                 win[u] = shared.tile([P, D * T], F32, name="win%d" % u, tag=tag, align_bytes=64)
             nc.vector.tensor_copy(out=win[u][:].indirect(offsets[:, a // 16 : b // 16]), in_=turned[:, u, a:b])
 
@@ -258,19 +291,27 @@ def tile_moe_mhm_gelu_kernel(tc, x_words, x_scales, w, wm, gate, offs, out):
                 if at == step:
                     scatter(u, a, b)
 
-        wm_bf = [shared.tile([P, N, PACK], BF16, name="wm_bf%d" % o, tag=WM_TAG[o], align_bytes=64) for o in range(D)]
+        wm_bf = [rounded[:, S_COLS : S_COLS + N, :], shared.tile([P, N, PACK], BF16, name="wm_bf1", tag=WM_TAG[1], align_bytes=64)]
         for o in range(D):
-            interleave_round(WM_ENG[o], wm_bf[o][:], wm_raw[:, o, :, :])
+            interleave_round(WM_ENG[o], wm_bf[o][:, :, :], wm_raw[o][:])
 
         def side_by_side(u, k):
             t0, t1 = TOKEN_CUTS[k], TOKEN_CUTS[k + 1]
             nc.scalar.copy(out=both[:, u, :, t0:t1], in_=win[u][:].rearrange("p (o t) -> p o t", o=D)[:, :, t0:t1])
 
+        def direct(eng, u, k):
+            t0, t1 = TOKEN_CUTS[k], TOKEN_CUTS[k + 1]
+            copy_on(eng, c_bf[k][:, :, :, u], win[u][:].rearrange("p (o t) -> p o t", o=D)[:, :, t0:t1])
+
+        for k in range(DIRECT):
+            direct("s", 0, k)
         t_ahead = TOKEN_CUTS[AHEAD]
-        nc.scalar.copy(out=both[:, 0, :, 0:t_ahead], in_=win[0][:].rearrange("p (o t) -> p o t", o=D)[:, :, 0:t_ahead])
+        t_first = TOKEN_CUTS[DIRECT]
+        if t_ahead > t_first:
+            nc.scalar.copy(out=both[:, 0, :, t_first:t_ahead], in_=win[0][:].rearrange("p (o t) -> p o t", o=D)[:, :, t_first:t_ahead])
         if G_SIDE:
             nc.gpsimd.tensor_copy(out=both[:, 0, :, t_ahead:], in_=win[0][:].rearrange("p (o t) -> p o t", o=D)[:, :, t_ahead:])
-        for k in range(nch):
+        for k in range(max(DIRECT, V_SIDE), nch):
             side_by_side(1, k)
             if k + AHEAD < nch and not G_SIDE:
                 side_by_side(0, k + AHEAD)
@@ -278,8 +319,12 @@ def tile_moe_mhm_gelu_kernel(tc, x_words, x_scales, w, wm, gate, offs, out):
         for o in range(D):
             nc.vector.quantize_mx(
                 out=wm_codes[:, o * N : (o + 1) * N].bitcast(FP8X4), scales=wm_scales[:, o * N : (o + 1) * N],
-                in_=wm_bf[o][:].rearrange("p n j -> p (n j)"),
+                in_=wm_bf[o][:, :, :].rearrange("p n j -> p (n j)"),
             )
+
+        if V_SIDE:
+            t1 = TOKEN_CUTS[V_SIDE]
+            nc.vector.tensor_copy(out=both[:, 1, :, 0:t1], in_=win[1][:].rearrange("p (o t) -> p o t", o=D)[:, :, 0:t1])
 
         def interleave(k, eng):
             copy_on(eng, c_bf[k][:], both[:, :, :, TOKEN_CUTS[k] : TOKEN_CUTS[k + 1]].rearrange("p u o t -> p o t u"))
@@ -302,7 +347,10 @@ def tile_moe_mhm_gelu_kernel(tc, x_words, x_scales, w, wm, gate, offs, out):
         def merge(k):
             t0, t1 = TOKEN_CUTS[k], TOKEN_CUTS[k + 1]
             quant_c(k)
-            acc = psum.tile([P, 2, widths[k]], F32, name="acc", tag="acc")
+            if k in OWN_BANK:
+                acc = psum.tile([P, 2, widths[k]], F32, name="acc_own%d" % k, tag=OWN_BANK[k], bufs=1)
+            else:
+                acc = psum.tile([P, 2, widths[k]], F32, name="acc", tag="acc")
             for h in range(2):
                 for o in range(D):
                     merge_pass(acc[:, h, :], k, h, o)
@@ -332,7 +380,9 @@ def tile_moe_mhm_gelu_kernel(tc, x_words, x_scales, w, wm, gate, offs, out):
                     rhs=wm_codes[:].bitcast(FP8X4), rhs_scale=wm_scales[:], start=True, stop=True,
                 )
         for step in range(nch):
-            if step not in S_CHUNKS:
+            if step < DIRECT:
+                direct("v", 1, step)
+            elif step not in S_CHUNKS:
                 interleave(step, "v")
             if step >= 1:
                 merge(step - 1)

@@ -28,7 +28,7 @@ QUANT_CUTS = [[0,512],[0,512],[0,512],[0,512],[0,512],[0,512],[0,512],[0,512],[0
 X_AFTER = 1
 SCALE_HOLD = [(None, -1), (None, -1)]
 GATE_V = 320
-WARM = 2
+WARM = 0
 DIRECT = 0
 BF_TAG = [["h"],["h"],["bf"],["bf"],["a1","bf"],["a0","bf"],["a1","bf"],["a0","bf"],["a1","bf"],["a0","bf"],["a1","bf"],["a0","bf"]]
 ACTS_TAG = ["raw1_1",None,"raw3_0",None,None,None,None,None,None,None,None,None]
@@ -50,7 +50,7 @@ LOAD_BACK = []
 S_COLS = 272
 WM_SPLIT = False
 U_SPLIT = {}
-V_SIDE = 1
+V_SIDE = 0
 OWN_BANK = {3: "expert1", 4: "spare"}
 WM_ENG = "gs"
 AHEAD = 6

@@ -52,6 +52,8 @@ WM_SPLIT = False
 U_SPLIT = {}
 V_SIDE = 0
 OWN_BANK = {3: "expert1", 4: "spare"}
+TWO_FROM = 4
+IN_RAW = []
 WM_ENG = "gs"
 AHEAD = 6
 S_CHUNKS = [4, 5]
@@ -188,6 +190,14 @@ def tile_moe_mhm_gelu_kernel(tc, x_words, x_scales, w, wm, gate, offs, out):
         def quant_w(e):
             w_codes[e] = ring.tile([P, H], U32, name="w_codes", align_bytes=64)
             w_scales[e] = ring.tile([P, H], U8, name="w_scales", align_bytes=64)
+            if e >= TWO_FROM:
+                halves = [(0, H // 2), (H // 2, H)]
+                for a, b in halves if e % 2 == 0 else halves[::-1]:
+                    nc.vector.quantize_mx(
+                        out=w_codes[e][:, a:b].bitcast(FP8X4), scales=w_scales[e][:, a:b],
+                        in_=w_bf[e][0][:, a:b, :].rearrange("p c j -> p (c j)"),
+                    )
+                return
             for k, (a, b) in enumerate(zip(QUANT_CUTS[e], QUANT_CUTS[e][1:])):
                 nc.vector.quantize_mx(
                     out=w_codes[e][:, a:b].bitcast(FP8X4), scales=w_scales[e][:, a:b],
@@ -206,17 +216,28 @@ def tile_moe_mhm_gelu_kernel(tc, x_words, x_scales, w, wm, gate, offs, out):
             )
 
         def activate(e):
-            if ACTS_TAG[e] is not None:
+            if e in IN_RAW:
+                first = 0 if e % 2 else H // 2
+                acts[e] = w_raw[e + 1][0][:, 0:2, first : first + H // 2].rearrange("s u (m v) -> s u m v", v=2)
+            elif ACTS_TAG[e] is not None:
                 acts[e] = place([P, 2, P, 2], F32, "acts%d" % e, ACTS_TAG[e])
             else:
                 acts[e] = ring.tile([P, 2, P, 2], F32, name="acts", align_bytes=64)
-            nc.scalar.activation(out=acts[e][:], in_=sums[e][:].rearrange("s (m u v) -> s u m v", u=2, v=2), func=GELU)
+            nc.scalar.activation(out=acts[e][:, :, :, :], in_=sums[e][:].rearrange("s (m u v) -> s u m v", u=2, v=2), func=GELU)
 
         def apply_gate(e):
             if GATED_TAG[e]:
                 gated[e] = shared.tile([P, H], BF16, name="gated%d" % e, tag=GATED_TAG[e], align_bytes=64)
             else:
                 gated[e] = ring.tile([P, H], BF16, name="gated", align_bytes=64)
+            if e in IN_RAW:
+                rows = acts[e].rearrange("s u m v -> s u (m v)")
+                if GATE_ENG[e] == "v":
+                    nc.vector.tensor_scalar(gated[e][:].rearrange("s (u x) -> s u x", u=2), rows, gate_cols[:, e : e + 1], None, MULT)
+                else:
+                    nc.vector.tensor_scalar(gated[e][:, : H // 2], rows[:, 0, :], gate_cols[:, e : e + 1], None, MULT)
+                    nc.scalar.activation(out=gated[e][:, H // 2 :], in_=rows[:, 1, :], func=COPY, scale=gate_cols[:, e : e + 1])
+                return
             flat = acts[e][:].rearrange("s u m v -> s (u m v)")
             if GATE_ENG[e] == "h":
                 half = GATE_V

@@ -22,16 +22,16 @@ ADD = mybir.AluOpType.add
 P = 128
 PACK = 4
 SCALE_CUTS = [0, 768, 1536]
-GATHER_CUTS = [0, 256, 768, 1152, 1536]
-GATHER_HOLD = [(None, -1), (None, -1), ("h", 1), ("raw2_0", 2)]
+GATHER_CUTS = [0,256,768,1536]
+GATHER_HOLD = [(None,-1),(None,-1),("h1",1)]
 QUANT_CUTS = [[0,512],[0,512],[0,512],[0,512],[0,512],[0,512],[0,512],[0,512],[0,512],[0,512],[0,512],[0,512]]
 X_AFTER = 1
 SCALE_HOLD = [(None, -1), (None, -1)]
 GATE_V = 320
 WARM = 0
 DIRECT = 0
-BF_TAG = [["h"],["h"],["bf"],["bf"],["a1","bf"],["a0","bf"],["a1","bf"],["a0","bf"],["a1","bf"],["a0","bf"],["a1","bf"],["a0","bf"]]
-ACTS_TAG = ["raw1_1",None,"raw3_0",None,None,None,None,None,None,None,None,None]
+BF_TAG = [["h0"],["h1"]]
+ACTS_TAG = ["raw1_1"]+[None]*11
 GATED_TAG = [None,None,None,None,None,None,None,None,None,None,None,"last"]
 WM_TAG = ["bf", "last"]
 G_SIDE = False
@@ -40,24 +40,38 @@ GATE_AFTER = 1
 TOKEN_CUTS = [0, 128, 256, 384, 512, 640, 768]
 SCALES_FIRST = False
 LOAD_CUTS = [[0,256,512],[0,256,512],[0,512],[0,512],[0,512],[0,512],[0,512],[0,512],[0,512],[0,512],[0,512],[0,512]]
-CASTS = [[["s",0,256],["s",256,512]],[["s",0,256],["s",256,384],["v",384,512]],[["s",0,128],["v",128,512]],[["s",208,512],["g",0,208]],[["s",0,272],["g",272,512]],[["s",240,512],["g",0,240]],[["s",0,272],["g",272,512]],[["s",240,512],["g",0,240]],[["s",0,272],["g",272,512]],[["s",240,512],["g",0,240]],[["s",0,272],["g",272,512]],[["s",240,512],["g",0,240]]]
-GATE_ENG = "svhhhhhhhhhh"
+CASTS = [[["s",0,256],["s",256,512]],[["g",0,256],["s",256,384],["v",384,512]],[["v",0,256],["g",256,512]],[["s",208,512],["g",0,208]]]+[[["s",0,272],["g",272,512]],[["s",240,512],["g",0,240]]]*4
+GATE_ENG = "svvhhhhhhhhh"
 TURN_ENG = "ssssssssssss"
 PIECES = [(2, 1, 0, 256), (3, 0, 0, 192), (4, 0, 192, 384), (5, 1, 256, 512), (6, 0, 384, 640), (7, 1, 512, 768), (8, 0, 640, 896), (9, 1, 768, 1024), (10, 0, 896, 1152), (11, 1, 1024, 1280), (12, 0, 1152, 1344), (13, 0, 1344, 1536), (13, 1, 1280, 1536)]
 WIN0_AFTER = "raw3_0"
-WIN1_AFTER = "win1"
+WIN1_AFTER = "raw2_0"
 LOAD_BACK = []
 S_COLS = 272
 WM_SPLIT = False
-U_SPLIT = {}
+U_SPLIT = {1:(1,0)}
 V_SIDE = 0
 OWN_BANK = {3: "expert1", 4: "spare"}
 TWO_FROM = 4
-IN_RAW = []
+IN_RAW = [2]
 WM_ENG = "gs"
 AHEAD = 6
 S_CHUNKS = [4, 5]
 RES_ENG = "ssssss"
+TURNED_TAG = None
+BF1_CUT = None
+SPLIT_TURN = {}
+GATE_SHARE = {}
+BASE = {3:304}
+Q_ORDER = {}
+WMQ_AT = [99, 99]
+G_SIDE_FROM = None
+WM_CASTS = None
+WM1_TAG = "last"
+GELU_SPLIT = {1:"ss"}
+GATE_FIRST = True
+ROOM = 304
+TURN_LATE = [0]
 
 
 def tile_moe_mhm_gelu_kernel(tc, x_words, x_scales, w, wm, gate, offs, out):
@@ -93,7 +107,7 @@ def tile_moe_mhm_gelu_kernel(tc, x_words, x_scales, w, wm, gate, offs, out):
             wm_raw = [wm_whole[:, o, :, :] for o in range(D)]
         wm_scales = keep.tile([P, D * N], U8, name="wm_scales", align_bytes=64)
         wm_codes = keep.tile([P, D * N], U32, name="wm_codes", align_bytes=64)
-        turned = keep.tile([P, 2, S], F32, name="turned", align_bytes=64)
+        turned = place([P, 2, S], F32, "turned", TURNED_TAG or "turned")
         both = keep.tile([P, 2, D, T], F32, name="both")
 
         def load_w(e, k):
@@ -117,13 +131,15 @@ def tile_moe_mhm_gelu_kernel(tc, x_words, x_scales, w, wm, gate, offs, out):
         for n, (e, k) in enumerate(pieces):
             if n > 0 or SCALES_FIRST:
                 load_w(e, k)
-            if n == GATE_AFTER:
+            if n == GATE_AFTER and GATE_FIRST:
                 nc.sync.dma_start(out=gate_rows[0:E, :], in_=gate[0].rearrange("(e s) -> e s", s=C))
             if n == X_AFTER:
                 nc.sync.dma_start(
                     out=xw[:].rearrange("p (o t) -> p o t", o=D),
                     in_=x_words.rearrange("o p t d -> p o (t d)").bitcast(I32),
                 )
+            if n == GATE_AFTER and not GATE_FIRST:
+                nc.sync.dma_start(out=gate_rows[0:E, :], in_=gate[0].rearrange("(e s) -> e s", s=C))
         if WM_SPLIT:
             for o in range(D):
                 nc.sync.dma_start(out=wm_raw[o][:], in_=wm[o * H : (o + 1) * H].rearrange("(p j) n -> p j n", j=PACK))
@@ -167,11 +183,11 @@ def tile_moe_mhm_gelu_kernel(tc, x_words, x_scales, w, wm, gate, offs, out):
             gw[k] = place([P, b - a], U32, "gw%d" % k, GATHER_HOLD[k][0] or "gw%d" % k)
             nc.vector.tensor_copy(out=gw[k][:], in_=xw[:].bitcast(U32).indirect(offsets[:, a // 16 : b // 16]))
 
-        rounded = keep.tile([P, H + S_COLS, PACK], BF16, name="rounded", align_bytes=64)
+        rounded = keep.tile([P, H + ROOM, PACK], BF16, name="rounded", align_bytes=64)
 
         def cast_w(e):
             if e >= 2:
-                base = S_COLS * (e % 2)
+                base = BASE.get(e, S_COLS * (e % 2))
                 w_bf[e] = [rounded[:, base : base + H, :]]
                 for eng, a, b in CASTS[e]:
                     interleave_round(eng, w_bf[e][0][:, a:b, :], w_raw[e][0][:, :, a:b])
@@ -223,6 +239,10 @@ def tile_moe_mhm_gelu_kernel(tc, x_words, x_scales, w, wm, gate, offs, out):
                 acts[e] = place([P, 2, P, 2], F32, "acts%d" % e, ACTS_TAG[e])
             else:
                 acts[e] = ring.tile([P, 2, P, 2], F32, name="acts", align_bytes=64)
+            if e in GELU_SPLIT:
+                for u in U_SPLIT[e]:
+                    nc.scalar.activation(out=acts[e][:, u, :, :], in_=sums[e][:].rearrange("s (m u v) -> s u m v", u=2, v=2)[:, u, :, :], func=GELU)
+                return
             nc.scalar.activation(out=acts[e][:, :, :, :], in_=sums[e][:].rearrange("s (m u v) -> s u m v", u=2, v=2), func=GELU)
 
         def apply_gate(e):
@@ -230,6 +250,15 @@ def tile_moe_mhm_gelu_kernel(tc, x_words, x_scales, w, wm, gate, offs, out):
                 gated[e] = shared.tile([P, H], BF16, name="gated%d" % e, tag=GATED_TAG[e], align_bytes=64)
             else:
                 gated[e] = ring.tile([P, H], BF16, name="gated", align_bytes=64)
+            if e in GELU_SPLIT:
+                for u, eng in zip(U_SPLIT[e], GELU_SPLIT[e]):
+                    d = gated[e][:, u * (H // 2) : (u + 1) * (H // 2)]
+                    s_in = acts[e][:, u, :, :].rearrange("s m v -> s (m v)")
+                    if eng == "v":
+                        nc.vector.tensor_scalar(d, s_in, gate_cols[:, e : e + 1], None, MULT)
+                    else:
+                        nc.scalar.activation(out=d, in_=s_in, func=COPY, scale=gate_cols[:, e : e + 1])
+                return
             if e in IN_RAW:
                 rows = acts[e].rearrange("s u m v -> s u (m v)")
                 if GATE_ENG[e] == "v":
@@ -240,7 +269,7 @@ def tile_moe_mhm_gelu_kernel(tc, x_words, x_scales, w, wm, gate, offs, out):
                 return
             flat = acts[e][:].rearrange("s u m v -> s (u m v)")
             if GATE_ENG[e] == "h":
-                half = GATE_V
+                half = GATE_SHARE.get(e, GATE_V)
                 nc.vector.tensor_scalar(gated[e][:, :half], flat[:, :half], gate_cols[:, e : e + 1], None, MULT)
                 nc.scalar.activation(out=gated[e][:, half:], in_=flat[:, half:], func=COPY, scale=gate_cols[:, e : e + 1])
             elif GATE_ENG[e] == "s":
@@ -265,7 +294,12 @@ def tile_moe_mhm_gelu_kernel(tc, x_words, x_scales, w, wm, gate, offs, out):
                 for n, u in enumerate(U_SPLIT[e]):
                     copy_on(TURN_ENG[e], turned[:, u, e * C : (e + 1) * C], turn_ps[e][n][:])
                 return
+            if e in SPLIT_TURN:
+                return
             copy_on(TURN_ENG[e], turned[:, :, e * C : (e + 1) * C], turn_ps[e][:])
+
+        def turn_half(e, u, eng):
+            copy_on(eng, turned[:, u, e * C : (e + 1) * C], turn_ps[e][:, u, :])
 
         def scatter(u, a, b):
             if a == 0:
@@ -298,13 +332,18 @@ def tile_moe_mhm_gelu_kernel(tc, x_words, x_scales, w, wm, gate, offs, out):
             if 0 <= step - 1 < E:
                 activate(step - 1)
             for e in range(E):
-                if TURN_AT[e] == step and e < step - 1:
+                if TURN_AT[e] == step and e < step - 1 and e not in TURN_LATE:
                     turn_out(e)
             if 0 <= step - 1 < E:
                 apply_gate(step - 1)
                 turn(step - 1)
+                for e in TURN_LATE:
+                    if TURN_AT[e] == step:
+                        turn_out(e)
                 if TURN_AT[step - 1] == step:
                     turn_out(step - 1)
+            for e, u, eng in [x for v in SPLIT_TURN.values() for x in v.get(step, [])]:
+                turn_half(e, u, eng)
             for k in range(len(GATHER_HOLD)):
                 if GATHER_HOLD[k][1] == step + 0.5:
                     gather(k)

@@ -40,7 +40,7 @@ GATE_AFTER = 1
 TOKEN_CUTS = [0, 128, 256, 384, 512, 640, 768]
 SCALES_FIRST = False
 LOAD_CUTS = [[0,256,512],[0,256,512],[0,512],[0,512],[0,512],[0,512],[0,512],[0,512],[0,512],[0,512],[0,512],[0,512]]
-CASTS = [[["s",0,256],["s",256,512]],[["g",0,256],["s",256,384],["v",384,512]],[["v",0,256],["g",256,512]],[["s",208,512],["g",0,208]]]+[[["s",0,272],["g",272,512]],[["s",240,512],["g",0,240]]]*4
+CASTS = [[["s",0,256],["s",256,512]],[["g",0,256],["s",256,384],["v",384,512]],[["v",0,320],["g",320,512]],[["s",208,512],["g",0,208]]]+[[["s",0,272],["g",272,512]],[["s",240,512],["g",0,240]]]*4
 GATE_ENG = "svvhhhhhhhhh"
 TURN_ENG = "ssssssssssss"
 PIECES = [(2, 1, 0, 256), (3, 0, 0, 192), (4, 0, 192, 384), (5, 1, 256, 512), (6, 0, 384, 640), (7, 1, 512, 768), (8, 0, 640, 896), (9, 1, 768, 1024), (10, 0, 896, 1152), (11, 1, 1024, 1280), (12, 0, 1152, 1344), (13, 0, 1344, 1536), (13, 1, 1280, 1536)]
@@ -50,13 +50,13 @@ LOAD_BACK = []
 S_COLS = 272
 WM_SPLIT = False
 U_SPLIT = {1:(1,0)}
-V_SIDE = 0
+V_SIDE = 1
 OWN_BANK = {3: "expert1", 4: "spare"}
 TWO_FROM = 4
 IN_RAW = [2]
 WM_ENG = "gs"
 AHEAD = 6
-S_CHUNKS = [4, 5]
+S_CHUNKS = [3]
 RES_ENG = "ssssss"
 TURNED_TAG = None
 BF1_CUT = None
@@ -71,6 +71,10 @@ WM1_TAG = "last"
 GELU_SPLIT = {1:"ss"}
 GATE_FIRST = True
 ROOM = 304
+G_RUN = 2
+HALF_CHUNKS = [5]
+GATE_EARLY = []
+GELU_WHOLE = []
 TURN_LATE = [0]
 
 
@@ -161,7 +165,10 @@ def tile_moe_mhm_gelu_kernel(tc, x_words, x_scales, w, wm, gate, offs, out):
 
         def interleave_round(eng, dst, src):
             if eng == "g":
-                nc.gpsimd.tensor_scalar(dst, src.rearrange("p j c -> p c j"), 1.0, 0.0, MULT, ADD)
+                if G_RUN == 1:
+                    nc.gpsimd.tensor_scalar(dst, src.rearrange("p j c -> p c j"), 1.0, 0.0, MULT, ADD)
+                else:
+                    nc.gpsimd.tensor_scalar(dst.rearrange("p (c i) j -> p c j i", i=G_RUN), src.rearrange("p j (c i) -> p c j i", i=G_RUN), 1.0, 0.0, MULT, ADD)
             else:
                 copy_on(eng, dst.rearrange("p (c i) j -> p c j i", i=4), src.rearrange("p j (c i) -> p c j i", i=4))
 
@@ -239,13 +246,24 @@ def tile_moe_mhm_gelu_kernel(tc, x_words, x_scales, w, wm, gate, offs, out):
                 acts[e] = place([P, 2, P, 2], F32, "acts%d" % e, ACTS_TAG[e])
             else:
                 acts[e] = ring.tile([P, 2, P, 2], F32, name="acts", align_bytes=64)
-            if e in GELU_SPLIT:
+            if e in GATE_EARLY:
+                for u in (1, 0):
+                    nc.scalar.activation(out=acts[e][:, u, :, :], in_=sums[e][:].rearrange("s (m u v) -> s u m v", u=2, v=2)[:, u, :, :], func=GELU)
+                gated[e] = ring.tile([P, H], BF16, name="gated", align_bytes=64)
+                half = GATE_SHARE.get(e, GATE_V)
+                nc.scalar.activation(out=gated[e][:, half:], in_=acts[e][:].rearrange("s u m v -> s (u m v)")[:, half:], func=COPY, scale=gate_cols[:, e : e + 1])
+                return
+            if e in GELU_SPLIT and e not in GELU_WHOLE:
                 for u in U_SPLIT[e]:
                     nc.scalar.activation(out=acts[e][:, u, :, :], in_=sums[e][:].rearrange("s (m u v) -> s u m v", u=2, v=2)[:, u, :, :], func=GELU)
                 return
             nc.scalar.activation(out=acts[e][:, :, :, :], in_=sums[e][:].rearrange("s (m u v) -> s u m v", u=2, v=2), func=GELU)
 
         def apply_gate(e):
+            if e in GATE_EARLY:
+                half = GATE_SHARE.get(e, GATE_V)
+                nc.vector.tensor_scalar(gated[e][:, :half], acts[e][:].rearrange("s u m v -> s (u m v)")[:, :half], gate_cols[:, e : e + 1], None, MULT)
+                return
             if GATED_TAG[e]:
                 gated[e] = shared.tile([P, H], BF16, name="gated%d" % e, tag=GATED_TAG[e], align_bytes=64)
             else:
@@ -430,8 +448,13 @@ def tile_moe_mhm_gelu_kernel(tc, x_words, x_scales, w, wm, gate, offs, out):
             nc.vector.tensor_copy(out=result[k][:, 1, :], in_=accs[1][:])
             nc.sync.dma_start(out=out_v[:, 1, t0:t1], in_=result[k][:, 1, :])
 
+        def interleave_head(k, o, eng):
+            copy_on(eng, c_bf[k][:, o, :, :], both[:, :, o, TOKEN_CUTS[k] : TOKEN_CUTS[k + 1]].rearrange("p u t -> p t u"))
+
         for k in S_CHUNKS:
             interleave(k, "s")
+        for k in HALF_CHUNKS:
+            interleave_head(k, 1, "s")
         if WARM:
             warm_ps = psum.tile([P, H], F32, name="warm_ps", tag="expert0", bufs=1)
             for n in range(WARM):
@@ -442,6 +465,8 @@ def tile_moe_mhm_gelu_kernel(tc, x_words, x_scales, w, wm, gate, offs, out):
         for step in range(nch):
             if step < DIRECT:
                 direct("v", 1, step)
+            elif step in HALF_CHUNKS:
+                interleave_head(step, 0, "v")
             elif step not in S_CHUNKS:
                 interleave(step, "v")
             if step >= 1:

@@ -21,393 +21,333 @@ ADD = mybir.AluOpType.add
 
 P = 128
 PACK = 4
-SCALE_CUTS = [0, 768, 1536]
-GATHER_CUTS = [0,256,768,1536]
-GATHER_HOLD = [(None,-1),(None,-1),("h1",1)]
-QUANT_CUTS = [[0,512],[0,512],[0,512],[0,512],[0,512],[0,512],[0,512],[0,512],[0,512],[0,512],[0,512],[0,512]]
-X_AFTER = 1
-SCALE_HOLD = [(None, -1), (None, -1)]
-GATE_V = 320
-WARM = 0
-DIRECT = 0
-BF_TAG = [["h0"],["h1"]]
-ACTS_TAG = ["raw1_1"]+[None]*11
-GATED_TAG = [None,None,None,None,None,None,None,None,None,None,None,"last"]
-WM_TAG = ["bf", "last"]
-G_SIDE = False
-TURN_AT = [2,2,4,5,6,7,8,9,10,11,12,13]
-GATE_AFTER = 1
-TOKEN_CUTS = [0, 128, 256, 384, 512, 640, 768]
-SCALES_FIRST = False
-LOAD_CUTS = [[0,256,512],[0,256,512],[0,512],[0,512],[0,512],[0,512],[0,512],[0,512],[0,512],[0,512],[0,512],[0,512]]
-CASTS = [[["s",0,256],["s",256,512]],[["g",0,256],["s",256,384],["v",384,512]],[["v",0,320],["g",320,512]],[["s",208,512],["g",0,208]]]+[[["s",0,272],["g",272,512]],[["s",240,512],["g",0,240]]]*4
-GATE_ENG = "svvhhhhhhhhh"
-TURN_ENG = "ssssssssssss"
-PIECES = [(2, 1, 0, 256), (3, 0, 0, 192), (4, 0, 192, 384), (5, 1, 256, 512), (6, 0, 384, 640), (7, 1, 512, 768), (8, 0, 640, 896), (9, 1, 768, 1024), (10, 0, 896, 1152), (11, 1, 1024, 1280), (12, 0, 1152, 1344), (13, 0, 1344, 1536), (13, 1, 1280, 1536)]
-WIN0_AFTER = "raw3_0"
-WIN1_AFTER = "raw2_0"
-LOAD_BACK = []
-S_COLS = 272
-WM_SPLIT = False
-U_SPLIT = {1:(1,0)}
-V_SIDE = 1
-OWN_BANK = {3: "expert1", 4: "spare"}
-TWO_FROM = 4
-IN_RAW = [2]
-WM_ENG = "gs"
-AHEAD = 6
-S_CHUNKS = [3]
-RES_ENG = "ssssss"
-TURNED_TAG = None
-BF1_CUT = None
-SPLIT_TURN = {}
-GATE_SHARE = {}
-BASE = {3:304}
-Q_ORDER = {}
-WMQ_AT = [99, 99]
-G_SIDE_FROM = None
-WM_CASTS = None
-WM1_TAG = "last"
-GELU_SPLIT = {1:"ss"}
-GATE_FIRST = True
-ROOM = 304
+HALF = H // 2
+QUARTER = H // 4
+OFFS_ROWS = 16
+SCALE_GROUPS = 4
 G_RUN = 2
-HALF_CHUNKS = [5]
-GATE_EARLY = []
-GELU_WHOLE = []
-TURN_LATE = [0]
+S_RUN = 4
+
+SCALAR_COLUMNS = 272
+SCALAR_COLUMNS_W3 = 304
+VECTOR_GATE = 224
+W1_CUT = 320
+LAP = 16
+LEAST_PIECE = D * T // 8
+PIECE = 2 * C
+FIRST_WORDS = 2 * C
+LATE_WORDS = 8 * C
+CHUNK = 128
+CHUNKS = T // CHUNK
+RING = 3
+ACC_BANKS = 3
+SCALAR_CHUNKS = (3, 5)
 
 
 def tile_moe_mhm_gelu_kernel(tc, x_words, x_scales, w, wm, gate, offs, out):
     nc = tc.nc
     with ExitStack() as ctx:
         keep = ctx.enter_context(tc.tile_pool(name="keep", bufs=1))
-        ring = ctx.enter_context(tc.tile_pool(name="ring", bufs=3))
+        ring = ctx.enter_context(tc.tile_pool(name="ring", bufs=RING))
         shared = ctx.enter_context(tc.tile_pool(name="shared", bufs=1))
-        stacked = ctx.enter_context(tc.tile_pool(name="stacked", bufs=1))
-        psum = ctx.enter_context(tc.psum_pool(name="psum", bufs=3))
+        psum = ctx.enter_context(tc.psum_pool(name="psum", bufs=ACC_BANKS))
 
-        offsets = keep.tile([P, S // 16], U16, name="offsets")
+        offsets = keep.tile([P, S // OFFS_ROWS], U16, name="offsets")
         xw = keep.tile([P, D * T], I32, name="xw", align_bytes=64)
         xs = keep.tile([P, D * T], U8, name="xs", align_bytes=64)
         gate_rows = keep.tile([P, C], F32, name="gate_rows")
         gate_cols = keep.tile([P, E], F32, name="gate_cols")
         ident = keep.tile([P, P], F32, name="ident")
-        warm_in = keep.tile([P, 8], F32, name="warm_in")
-        warm_out = keep.tile([P, 8], F32, name="warm_out")
-        def place(shape, dtype, name, tag):
-            if isinstance(tag, int):
-                return stacked.tile(shape, dtype, name=name, offset=tag, align_bytes=64)
+        zeros = keep.tile([P, C], F32, name="zeros")
+
+        def own(shape, dtype, name, tag):
             return shared.tile(shape, dtype, name=name, tag=tag, align_bytes=64)
 
-        w_raw = [
-            [place([P, PACK, LOAD_CUTS[e][k + 1] - LOAD_CUTS[e][k]], F32, "w_raw%d_%d" % (e, k), "raw%d_%d" % (e, k)) for k in range(len(LOAD_CUTS[e]) - 1)]
-            for e in range(E)
-        ]
-        if WM_SPLIT:
-            wm_raw = [keep.tile([P, PACK, N], F32, name="wm_raw%d" % o) for o in range(D)]
-        else:
-            wm_whole = keep.tile([P, D, PACK, N], F32, name="wm_raw")
-            wm_raw = [wm_whole[:, o, :, :] for o in range(D)]
+        load_cuts = [[0, HALF, H], [0, W1_CUT, H]] + [[0, H]] * (E - 2)
+        w3_and_acts2 = own([P, PACK * H + H - LAP], F32, "w3_and_acts2", "raw3_0")
+        w_raw = []
+        for e in range(E):
+            views = []
+            for k, (a, b) in enumerate(zip(load_cuts[e], load_cuts[e][1:])):
+                if e == 3:
+                    views.append((a, w3_and_acts2[:, : PACK * H].rearrange("p (j c) -> p j c", j=PACK)))
+                else:
+                    views.append((a, own([P, PACK, b - a], F32, "w_raw%d_%d" % (e, k), "raw%d_%d" % (e, k))[:, :, :]))
+            w_raw.append(views)
+        wm_raw = keep.tile([P, D, PACK, N], F32, name="wm_raw")
         wm_scales = keep.tile([P, D * N], U8, name="wm_scales", align_bytes=64)
         wm_codes = keep.tile([P, D * N], U32, name="wm_codes", align_bytes=64)
-        turned = place([P, 2, S], F32, "turned", TURNED_TAG or "turned")
+        turned = keep.tile([P, 2, S], F32, name="turned", align_bytes=64)
         both = keep.tile([P, 2, D, T], F32, name="both")
 
         def load_w(e, k):
-            a, b = LOAD_CUTS[e][k], LOAD_CUTS[e][k + 1]
-            nc.sync.dma_start(out=w_raw[e][k][:], in_=w[e].rearrange("(p j) c -> p j c", j=PACK)[:, :, a:b])
+            a, b = load_cuts[e][k], load_cuts[e][k + 1]
+            nc.sync.dma_start(out=w_raw[e][k][1], in_=w[e].rearrange("(p j) c -> p j c", j=PACK)[:, :, a:b])
 
         nc.gpsimd.memset(xs[:].bitcast(I32), 0)
-        nc.vector.memset(gate_rows[:], 0.0)
+        nc.vector.memset(gate_rows[: P // 2, :], 0.0)
         nc.sync.dma_start(offsets[:], offs)
-        if not SCALES_FIRST:
-            load_w(0, 0)
+        load_w(0, 0)
         xs_words = xs[:].bitcast(I32).rearrange("p (o t) -> p o t", o=D)
         scale_rows = x_scales.bitcast(I32).rearrange("o b t -> b o t")
-        for q in range(4):
+        for q in range(SCALE_GROUPS):
             nc.sync.dma_start(out=xs_words[32 * q : 32 * q + 4, :, :], in_=scale_rows[4 * q : 4 * q + 4, :, :])
-        nc.gpsimd.memset(warm_in[:], 0.0)
+        nc.gpsimd.memset(zeros[P // 2 :, :], 0.0)
         make_identity(nc, ident[:])
-        nc.scalar.activation(out=warm_out[:], in_=warm_in[:], func=GELU)
-
-        pieces = [(e, k) for e in range(E) for k in (reversed(range(len(LOAD_CUTS[e]) - 1)) if e in LOAD_BACK else range(len(LOAD_CUTS[e]) - 1))]
-        for n, (e, k) in enumerate(pieces):
-            if n > 0 or SCALES_FIRST:
+        nc.scalar.activation(out=gate_rows[P // 2 :, :], in_=zeros[P // 2 :, :], func=GELU)
+        load_w(0, 1)
+        nc.sync.dma_start(out=gate_rows[0:E, :], in_=gate[0].rearrange("(e s) -> e s", s=C))
+        nc.sync.dma_start(
+            out=xw[:].rearrange("p (o t) -> p o t", o=D),
+            in_=x_words.rearrange("o p t d -> p o (t d)").bitcast(I32),
+        )
+        for e in range(1, E):
+            for k in range(len(w_raw[e])):
                 load_w(e, k)
-            if n == GATE_AFTER and GATE_FIRST:
-                nc.sync.dma_start(out=gate_rows[0:E, :], in_=gate[0].rearrange("(e s) -> e s", s=C))
-            if n == X_AFTER:
-                nc.sync.dma_start(
-                    out=xw[:].rearrange("p (o t) -> p o t", o=D),
-                    in_=x_words.rearrange("o p t d -> p o (t d)").bitcast(I32),
-                )
-            if n == GATE_AFTER and not GATE_FIRST:
-                nc.sync.dma_start(out=gate_rows[0:E, :], in_=gate[0].rearrange("(e s) -> e s", s=C))
-        if WM_SPLIT:
-            for o in range(D):
-                nc.sync.dma_start(out=wm_raw[o][:], in_=wm[o * H : (o + 1) * H].rearrange("(p j) n -> p j n", j=PACK))
-        else:
-            nc.sync.dma_start(
-                out=wm_whole[:].rearrange("p o j n -> p o (j n)"),
-                in_=wm.rearrange("(o p j) n -> p o (j n)", o=D, j=PACK),
-            )
-
+        nc.sync.dma_start(
+            out=wm_raw[:].rearrange("p o j n -> p o (j n)"),
+            in_=wm.rearrange("(o p j) n -> p o (j n)", o=D, j=PACK),
+        )
         gate_ps = psum.tile([P, P], F32, name="gate_ps", tag="acc")
         nc.tensor.transpose(gate_ps[:], gate_rows[:], ident[:])
         nc.scalar.copy(out=gate_cols[:], in_=gate_ps[:, 0:E])
 
-        def copy_on(eng, d, s):
-            if eng == "v":
-                nc.vector.tensor_copy(out=d, in_=s)
+        def copy_on(eng, dst, src):
+            if eng is nc.vector:
+                nc.vector.tensor_copy(out=dst, in_=src)
             else:
-                nc.scalar.copy(out=d, in_=s)
+                nc.scalar.copy(out=dst, in_=src)
 
-        def interleave_round(eng, dst, src):
-            if eng == "g":
-                if G_RUN == 1:
-                    nc.gpsimd.tensor_scalar(dst, src.rearrange("p j c -> p c j"), 1.0, 0.0, MULT, ADD)
-                else:
-                    nc.gpsimd.tensor_scalar(dst.rearrange("p (c i) j -> p c j i", i=G_RUN), src.rearrange("p j (c i) -> p c j i", i=G_RUN), 1.0, 0.0, MULT, ADD)
+        def round_and_interleave(eng, dst, src):
+            run = G_RUN if eng is nc.gpsimd else S_RUN
+            dst = dst.rearrange("p (c i) j -> p c j i", i=run)
+            src = src.rearrange("p j (c i) -> p c j i", i=run)
+            if eng is nc.gpsimd:
+                nc.gpsimd.tensor_scalar(dst, src, 1.0, 0.0, MULT, ADD)
             else:
-                copy_on(eng, dst.rearrange("p (c i) j -> p c j i", i=4), src.rearrange("p j (c i) -> p c j i", i=4))
+                copy_on(eng, dst, src)
 
-        gs = {}
+        slot_scales, slot_words = [], []
 
-        def gather_scales(k):
-            a, b = SCALE_CUTS[k], SCALE_CUTS[k + 1]
-            gs[k] = place([P, b - a], U8, "gs%d" % k, SCALE_HOLD[k][0] or "gs%d" % k)
-            nc.vector.tensor_copy(out=gs[k][:], in_=xs[:].indirect(offsets[:, a // 16 : b // 16]))
+        def gather(into, window, dtype, a, b, tag):
+            piece = own([P, b - a], dtype, "gathered_%s" % tag, tag)
+            nc.vector.tensor_copy(out=piece[:], in_=window.indirect(offsets[:, a // OFFS_ROWS : b // OFFS_ROWS]))
+            into.append((a, piece))
 
-        for k in range(len(SCALE_HOLD)):
-            if SCALE_HOLD[k][1] < 0:
-                gather_scales(k)
+        def slots_of(pieces, e):
+            first, piece = [x for x in pieces if x[0] <= e * C][-1]
+            return piece[:, e * C - first : (e + 1) * C - first]
 
-        gw, w_bf, w_codes, w_scales, sums, acts, gated, turn_ps, win = {}, {}, {}, {}, {}, {}, {}, {}, {}
+        rounded = keep.tile([P, H + SCALAR_COLUMNS_W3, PACK], BF16, name="rounded", align_bytes=64)
+        w_bf, w_codes, w_scales, sums, acts, gated, turn_ps, win = {}, {}, {}, {}, {}, {}, {}, {}
 
-        def gather(k):
-            a, b = GATHER_CUTS[k], GATHER_CUTS[k + 1]
-            gw[k] = place([P, b - a], U32, "gw%d" % k, GATHER_HOLD[k][0] or "gw%d" % k)
-            nc.vector.tensor_copy(out=gw[k][:], in_=xw[:].bitcast(U32).indirect(offsets[:, a // 16 : b // 16]))
+        def rounded_cols(e, a, b):
+            first, view = [x for x in w_bf[e] if x[0] <= a][-1]
+            return view[:, a - first : b - first, :]
 
-        rounded = keep.tile([P, H + ROOM, PACK], BF16, name="rounded", align_bytes=64)
+        def round_w(eng, e, a, b):
+            first, raw = [x for x in w_raw[e] if x[0] <= a][-1]
+            round_and_interleave(eng, rounded_cols(e, a, b), raw[:, :, a - first : b - first])
 
-        def cast_w(e):
-            if e >= 2:
-                base = BASE.get(e, S_COLS * (e % 2))
-                w_bf[e] = [rounded[:, base : base + H, :]]
-                for eng, a, b in CASTS[e]:
-                    interleave_round(eng, w_bf[e][0][:, a:b, :], w_raw[e][0][:, :, a:b])
-                return
-            cuts = QUANT_CUTS[e]
-            w_bf[e] = [
-                shared.tile([P, cuts[k + 1] - cuts[k], PACK], BF16, name="w_bf%d_%d" % (e, k), tag=BF_TAG[e][k], align_bytes=64)
-                for k in range(len(cuts) - 1)
-            ]
-            for eng, a, b in CASTS[e]:
-                k = max(i for i in range(len(cuts)) if cuts[i] <= a)
-                n = max(i for i in range(len(LOAD_CUTS[e])) if LOAD_CUTS[e][i] <= a)
-                first = LOAD_CUTS[e][n]
-                interleave_round(eng, w_bf[e][k][:, a - cuts[k] : b - cuts[k], :], w_raw[e][n][:, :, a - first : b - first])
-
-        def quant_w(e):
+        def quantise_w(e, ranges):
             w_codes[e] = ring.tile([P, H], U32, name="w_codes", align_bytes=64)
             w_scales[e] = ring.tile([P, H], U8, name="w_scales", align_bytes=64)
-            if e >= TWO_FROM:
-                halves = [(0, H // 2), (H // 2, H)]
-                for a, b in halves if e % 2 == 0 else halves[::-1]:
-                    nc.vector.quantize_mx(
-                        out=w_codes[e][:, a:b].bitcast(FP8X4), scales=w_scales[e][:, a:b],
-                        in_=w_bf[e][0][:, a:b, :].rearrange("p c j -> p (c j)"),
-                    )
-                return
-            for k, (a, b) in enumerate(zip(QUANT_CUTS[e], QUANT_CUTS[e][1:])):
+            for a, b in ranges:
                 nc.vector.quantize_mx(
                     out=w_codes[e][:, a:b].bitcast(FP8X4), scales=w_scales[e][:, a:b],
-                    in_=w_bf[e][k][:, :, :].rearrange("p c j -> p (c j)"),
+                    in_=rounded_cols(e, a, b).rearrange("p c j -> p (c j)"),
                 )
 
-        def product(e):
-            ks = max(i for i in range(len(SCALE_CUTS)) if SCALE_CUTS[i] <= e * C)
-            scale_bytes = gs[ks][:, e * C - SCALE_CUTS[ks] : (e + 1) * C - SCALE_CUTS[ks]]
-            k = max(i for i in range(len(GATHER_CUTS)) if GATHER_CUTS[i] <= e * C)
-            words = gw[k][:, e * C - GATHER_CUTS[k] : (e + 1) * C - GATHER_CUTS[k]]
+        def product(e, ranges=((0, H),)):
             sums[e] = psum.tile([P, H], F32, name="sums%d" % e, tag="expert%d" % (e % 2), bufs=1)
-            nc.tensor.matmul_mx(
-                out=sums[e][:], lhsT=words.bitcast(FP8X4), lhsT_scale=scale_bytes,
-                rhs=w_codes[e][:].bitcast(FP8X4), rhs_scale=w_scales[e][:], start=True, stop=True,
+            for a, b in ranges:
+                nc.tensor.matmul_mx(
+                    out=sums[e][:, a:b], lhsT=slots_of(slot_words, e).bitcast(FP8X4), lhsT_scale=slots_of(slot_scales, e),
+                    rhs=w_codes[e][:, a:b].bitcast(FP8X4), rhs_scale=w_scales[e][:, a:b], start=True, stop=True,
+                )
+
+        def gelu(e, pairs):
+            nc.scalar.activation(
+                out=acts[e][:, pairs, :, :], in_=sums[e][:].rearrange("s (m u v) -> s u m v", u=2, v=2)[:, pairs, :, :], func=GELU
             )
 
-        def activate(e):
-            if e in IN_RAW:
-                first = 0 if e % 2 else H // 2
-                acts[e] = w_raw[e + 1][0][:, 0:2, first : first + H // 2].rearrange("s u (m v) -> s u m v", v=2)
-            elif ACTS_TAG[e] is not None:
-                acts[e] = place([P, 2, P, 2], F32, "acts%d" % e, ACTS_TAG[e])
+        def apply_gate(eng, e, a, b):
+            values = acts[e].rearrange("s u m v -> s (u m v)")[:, a:b]
+            if eng is nc.vector:
+                nc.vector.tensor_scalar(gated[e][:, a:b], values, gate_cols[:, e : e + 1], None, MULT)
             else:
-                acts[e] = ring.tile([P, 2, P, 2], F32, name="acts", align_bytes=64)
-            if e in GATE_EARLY:
-                for u in (1, 0):
-                    nc.scalar.activation(out=acts[e][:, u, :, :], in_=sums[e][:].rearrange("s (m u v) -> s u m v", u=2, v=2)[:, u, :, :], func=GELU)
-                gated[e] = ring.tile([P, H], BF16, name="gated", align_bytes=64)
-                half = GATE_SHARE.get(e, GATE_V)
-                nc.scalar.activation(out=gated[e][:, half:], in_=acts[e][:].rearrange("s u m v -> s (u m v)")[:, half:], func=COPY, scale=gate_cols[:, e : e + 1])
-                return
-            if e in GELU_SPLIT and e not in GELU_WHOLE:
-                for u in U_SPLIT[e]:
-                    nc.scalar.activation(out=acts[e][:, u, :, :], in_=sums[e][:].rearrange("s (m u v) -> s u m v", u=2, v=2)[:, u, :, :], func=GELU)
-                return
-            nc.scalar.activation(out=acts[e][:, :, :, :], in_=sums[e][:].rearrange("s (m u v) -> s u m v", u=2, v=2), func=GELU)
+                nc.scalar.activation(out=gated[e][:, a:b], in_=values, func=COPY, scale=gate_cols[:, e : e + 1])
 
-        def apply_gate(e):
-            if e in GATE_EARLY:
-                half = GATE_SHARE.get(e, GATE_V)
-                nc.vector.tensor_scalar(gated[e][:, :half], acts[e][:].rearrange("s u m v -> s (u m v)")[:, :half], gate_cols[:, e : e + 1], None, MULT)
-                return
-            if GATED_TAG[e]:
-                gated[e] = shared.tile([P, H], BF16, name="gated%d" % e, tag=GATED_TAG[e], align_bytes=64)
-            else:
-                gated[e] = ring.tile([P, H], BF16, name="gated", align_bytes=64)
-            if e in GELU_SPLIT:
-                for u, eng in zip(U_SPLIT[e], GELU_SPLIT[e]):
-                    d = gated[e][:, u * (H // 2) : (u + 1) * (H // 2)]
-                    s_in = acts[e][:, u, :, :].rearrange("s m v -> s (m v)")
-                    if eng == "v":
-                        nc.vector.tensor_scalar(d, s_in, gate_cols[:, e : e + 1], None, MULT)
-                    else:
-                        nc.scalar.activation(out=d, in_=s_in, func=COPY, scale=gate_cols[:, e : e + 1])
-                return
-            if e in IN_RAW:
-                rows = acts[e].rearrange("s u m v -> s u (m v)")
-                if GATE_ENG[e] == "v":
-                    nc.vector.tensor_scalar(gated[e][:].rearrange("s (u x) -> s u x", u=2), rows, gate_cols[:, e : e + 1], None, MULT)
-                else:
-                    nc.vector.tensor_scalar(gated[e][:, : H // 2], rows[:, 0, :], gate_cols[:, e : e + 1], None, MULT)
-                    nc.scalar.activation(out=gated[e][:, H // 2 :], in_=rows[:, 1, :], func=COPY, scale=gate_cols[:, e : e + 1])
-                return
-            flat = acts[e][:].rearrange("s u m v -> s (u m v)")
-            if GATE_ENG[e] == "h":
-                half = GATE_SHARE.get(e, GATE_V)
-                nc.vector.tensor_scalar(gated[e][:, :half], flat[:, :half], gate_cols[:, e : e + 1], None, MULT)
-                nc.scalar.activation(out=gated[e][:, half:], in_=flat[:, half:], func=COPY, scale=gate_cols[:, e : e + 1])
-            elif GATE_ENG[e] == "s":
-                nc.scalar.activation(out=gated[e][:], in_=flat, func=COPY, scale=gate_cols[:, e : e + 1])
-            elif GATE_ENG[e] == "g":
-                nc.gpsimd.tensor_scalar(gated[e][:], flat, gate_cols[:, e : e + 1], 0.0, MULT, ADD)
-            else:
-                nc.vector.tensor_scalar(gated[e][:], flat, gate_cols[:, e : e + 1], None, MULT)
+        def new_acts(e):
+            acts[e] = ring.tile([P, 2, P, 2], F32, name="acts", align_bytes=64)[:, :, :, :]
+
+        def new_gated(e):
+            gated[e] = ring.tile([P, H], BF16, name="gated", align_bytes=64)
+
+        def pair_words(e, u):
+            return gated[e][:].bitcast(F32)[:, u * P : (u + 1) * P]
 
         def turn(e):
-            if e in U_SPLIT:
-                turn_ps[e] = [psum.tile([P, C], F32, name="turn_a%d" % e, tag="expert%d" % (e % 2), bufs=1), psum.tile([P, C], F32, name="turn_b%d" % e, tag="acc")]
-                for n, u in enumerate(U_SPLIT[e]):
-                    nc.tensor.transpose(turn_ps[e][n][:], gated[e][:].bitcast(F32)[:, u * P : (u + 1) * P], ident[:])
-                return
             turn_ps[e] = psum.tile([P, 2, C], F32, name="turn_ps%d" % e, tag="expert%d" % (e % 2), bufs=1)
             for u in range(2):
-                nc.tensor.transpose(turn_ps[e][:, u, :], gated[e][:].bitcast(F32)[:, u * P : (u + 1) * P], ident[:])
+                nc.tensor.transpose(turn_ps[e][:, u, :], pair_words(e, u), ident[:])
 
-        def turn_out(e):
-            if e in U_SPLIT:
-                for n, u in enumerate(U_SPLIT[e]):
-                    copy_on(TURN_ENG[e], turned[:, u, e * C : (e + 1) * C], turn_ps[e][n][:])
-                return
-            if e in SPLIT_TURN:
-                return
-            copy_on(TURN_ENG[e], turned[:, :, e * C : (e + 1) * C], turn_ps[e][:])
+        def empty(e):
+            nc.scalar.copy(out=turned[:, :, e * C : (e + 1) * C], in_=turn_ps[e][:])
 
-        def turn_half(e, u, eng):
-            copy_on(eng, turned[:, u, e * C : (e + 1) * C], turn_ps[e][:, u, :])
+        def turn_pair(e, u, tag, bufs):
+            turn_ps[e, u] = psum.tile([P, C], F32, name="turn_ps%d_%d" % (e, u), tag=tag, bufs=bufs)
+            nc.tensor.transpose(turn_ps[e, u][:], pair_words(e, u), ident[:])
+
+        def empty_pair(eng, e, u):
+            copy_on(eng, turned[:, u, e * C : (e + 1) * C], turn_ps[e, u][:])
 
         def scatter(u, a, b):
-            if a == 0:
-                tag = WIN0_AFTER if u == 0 else WIN1_AFTER
-                win[u] = shared.tile([P, D * T], F32, name="win%d" % u, tag=tag, align_bytes=64)
-            nc.vector.tensor_copy(out=win[u][:].indirect(offsets[:, a // 16 : b // 16]), in_=turned[:, u, a:b])
+            nc.vector.tensor_copy(out=win[u][:].indirect(offsets[:, a // OFFS_ROWS : b // OFFS_ROWS]), in_=turned[:, u, a:b])
 
-        nch = len(TOKEN_CUTS) - 1
-        widths = [TOKEN_CUTS[k + 1] - TOKEN_CUTS[k] for k in range(nch)]
-        c_bf = [keep.tile([P, D, widths[k], 2], F32, name="c_bf%d" % k, align_bytes=64) for k in range(nch)]
-        c_codes = [keep.tile([P, D * widths[k]], U32, name="c_codes%d" % k, align_bytes=64) for k in range(nch)]
-        c_scales = [keep.tile([P, D * widths[k]], U8, name="c_scales%d" % k, align_bytes=64) for k in range(nch)]
-        result = [keep.tile([P, 2, widths[k]], F32, name="result%d" % k) for k in range(nch)]
+        both_pairs = slice(0, 2)
+        pair = [slice(0, 1), slice(1, 2)]
+        low_first = [(0, HALF), (HALF, H)]
+        c_bf = [keep.tile([P, D, CHUNK, 2], F32, name="c_bf%d" % k, align_bytes=64) for k in range(CHUNKS)]
+        c_codes = [keep.tile([P, D * CHUNK], U32, name="c_codes%d" % k, align_bytes=64) for k in range(CHUNKS)]
+        c_scales = [keep.tile([P, D * CHUNK], U8, name="c_scales%d" % k, align_bytes=64) for k in range(CHUNKS)]
+        result = [keep.tile([P, 2, CHUNK], F32, name="result%d" % k) for k in range(CHUNKS)]
         out_v = out.rearrange("(h p) t -> p h t", p=P)
 
-        for k in range(len(GATHER_HOLD)):
-            if GATHER_HOLD[k][1] < 0:
-                gather(k)
-        for step in range(E + 2):
-            if step < E:
-                cast_w(step)
-                quant_w(step)
-                for k in range(len(SCALE_HOLD)):
-                    if SCALE_HOLD[k][1] == step:
-                        gather_scales(k)
-                for k in range(len(GATHER_HOLD)):
-                    if GATHER_HOLD[k][1] == step:
-                        gather(k)
-                product(step)
-            if 0 <= step - 1 < E:
-                activate(step - 1)
-            for e in range(E):
-                if TURN_AT[e] == step and e < step - 1 and e not in TURN_LATE:
-                    turn_out(e)
-            if 0 <= step - 1 < E:
-                apply_gate(step - 1)
-                turn(step - 1)
-                for e in TURN_LATE:
-                    if TURN_AT[e] == step:
-                        turn_out(e)
-                if TURN_AT[step - 1] == step:
-                    turn_out(step - 1)
-            for e, u, eng in [x for v in SPLIT_TURN.values() for x in v.get(step, [])]:
-                turn_half(e, u, eng)
-            for k in range(len(GATHER_HOLD)):
-                if GATHER_HOLD[k][1] == step + 0.5:
-                    gather(k)
-            for at, u, a, b in PIECES:
-                if at == step:
-                    scatter(u, a, b)
+        gather(slot_scales, xs[:], U8, 0, S // 2, "scales0")
+        gather(slot_scales, xs[:], U8, S // 2, S, "scales1")
+        gather(slot_words, xw[:].bitcast(U32), U32, 0, FIRST_WORDS, "words0")
+        gather(slot_words, xw[:].bitcast(U32), U32, FIRST_WORDS, LATE_WORDS, "words1")
 
-        wm_bf = [rounded[:, S_COLS : S_COLS + N, :], shared.tile([P, N, PACK], BF16, name="wm_bf1", tag=WM_TAG[1], align_bytes=64)]
-        for o in range(D):
-            interleave_round(WM_ENG[o], wm_bf[o][:, :, :], wm_raw[o][:])
+        w_bf[0] = [(0, own([P, H, PACK], BF16, "w_bf0", "bf0")[:, :, :])]
+        round_w(nc.scalar, 0, 0, HALF)
+        round_w(nc.scalar, 0, HALF, H)
+        quantise_w(0, [(0, H)])
+        product(0)
 
-        def side_by_side(u, k):
-            t0, t1 = TOKEN_CUTS[k], TOKEN_CUTS[k + 1]
-            nc.scalar.copy(out=both[:, u, :, t0:t1], in_=win[u][:].rearrange("p (o t) -> p o t", o=D)[:, :, t0:t1])
+        w_bf[1] = [(0, own([P, HALF, PACK], BF16, "w_bf1", "bf1")[:, :, :]), (HALF, rounded[:, HALF:H, :])]
+        round_w(nc.scalar, 1, 0, HALF)
+        round_w(nc.scalar, 1, HALF, W1_CUT)
+        round_w(nc.scalar, 1, W1_CUT, H - QUARTER)
+        round_w(nc.gpsimd, 1, H - QUARTER, H)
+        quantise_w(1, low_first)
+        gather(slot_words, xw[:].bitcast(U32), U32, LATE_WORDS, S, "raw1_1")
+        product(1, low_first)
+        acts[0] = own([P, 2, P, 2], F32, "acts0", "raw1_0")[:, :, :, :]
+        gelu(0, both_pairs)
+        new_gated(0)
+        apply_gate(nc.scalar, 0, 0, H)
+        turn(0)
 
-        def direct(eng, u, k):
-            t0, t1 = TOKEN_CUTS[k], TOKEN_CUTS[k + 1]
-            copy_on(eng, c_bf[k][:, :, :, u], win[u][:].rearrange("p (o t) -> p o t", o=D)[:, :, t0:t1])
+        w_bf[2] = [(0, rounded[:, 0:H, :])]
+        for a, b in low_first:
+            round_w(nc.vector, 2, a, b)
+        quantise_w(2, low_first)
+        product(2)
+        new_acts(1)
+        new_gated(1)
+        for u in (1, 0):
+            gelu(1, pair[u])
+        for u in (1, 0):
+            apply_gate(nc.scalar, 1, u * HALF, (u + 1) * HALF)
+        turn_pair(1, 1, "expert1", 1)
+        turn_pair(1, 0, "acc", ACC_BANKS)
+        empty(0)
+        empty_pair(nc.scalar, 1, 1)
+        empty_pair(nc.scalar, 1, 0)
+        win[1] = own([P, D * T], F32, "win1", "raw2_0")
+        scatter(1, 0, PIECE)
 
-        for k in range(DIRECT):
-            direct("s", 0, k)
-        t_ahead = TOKEN_CUTS[AHEAD]
-        t_first = TOKEN_CUTS[DIRECT]
-        if t_ahead > t_first:
-            nc.scalar.copy(out=both[:, 0, :, t_first:t_ahead], in_=win[0][:].rearrange("p (o t) -> p o t", o=D)[:, :, t_first:t_ahead])
-        if G_SIDE:
-            nc.gpsimd.tensor_copy(out=both[:, 0, :, t_ahead:], in_=win[0][:].rearrange("p (o t) -> p o t", o=D)[:, :, t_ahead:])
-        for k in range(max(DIRECT, V_SIDE), nch):
-            side_by_side(1, k)
-            if k + AHEAD < nch and not G_SIDE:
-                side_by_side(0, k + AHEAD)
+        w_bf[3] = [(0, rounded[:, SCALAR_COLUMNS_W3 : SCALAR_COLUMNS_W3 + H, :])]
+        round_w(nc.scalar, 3, H - LAP, H)
+        round_w(nc.scalar, 3, H - SCALAR_COLUMNS_W3, H - LAP)
+        round_w(nc.gpsimd, 3, 0, H - SCALAR_COLUMNS_W3)
+        quantise_w(3, low_first[::-1])
+        product(3)
+        acts[2] = w3_and_acts2[:, PACK * H - LAP :].rearrange("s (u m v) -> s u m v", u=2, v=2)
+        gelu(2, both_pairs)
+        new_gated(2)
+        apply_gate(nc.vector, 2, 0, H)
+        turn(2)
+        win[0] = own([P, D * T], F32, "win0", "raw3_0")
+        scatter(0, 0, LEAST_PIECE)
 
+        done = [LEAST_PIECE, PIECE]
+        for e in range(4, E):
+            if e % 2 == 0:
+                w_bf[e] = [(0, rounded[:, 0:H, :])]
+                round_w(nc.scalar, e, 0, SCALAR_COLUMNS)
+                round_w(nc.gpsimd, e, SCALAR_COLUMNS, H)
+                quantise_w(e, low_first)
+            else:
+                w_bf[e] = [(0, rounded[:, SCALAR_COLUMNS : SCALAR_COLUMNS + H, :])]
+                round_w(nc.scalar, e, H - SCALAR_COLUMNS, H)
+                round_w(nc.gpsimd, e, 0, H - SCALAR_COLUMNS)
+                quantise_w(e, low_first[::-1])
+            if e < E - 1:
+                product(e)
+            else:
+                product(e, low_first[::-1])
+            new_acts(e - 1)
+            new_gated(e - 1)
+            if e < E - 1:
+                gelu(e - 1, both_pairs)
+                empty(e - 2)
+                apply_gate(nc.vector, e - 1, 0, VECTOR_GATE)
+                apply_gate(nc.scalar, e - 1, VECTOR_GATE, H)
+                turn(e - 1)
+            else:
+                gelu(e - 1, pair[0])
+                empty(e - 2)
+                gelu(e - 1, pair[1])
+                apply_gate(nc.scalar, e - 1, 0, HALF)
+                apply_gate(nc.scalar, e - 1, HALF, H)
+                turn_pair(e - 1, 0, "expert0", 1)
+                turn_pair(e - 1, 1, "acc", ACC_BANKS)
+            scatter(e % 2, done[e % 2], (e - 1) * C)
+            done[e % 2] = (e - 1) * C
+
+        last = E - 1
+        new_acts(last)
+        gated[last] = own([P, H], BF16, "gated_last", "last")
+        empty_pair(nc.scalar, last - 1, 0)
+        for u in range(2):
+            gelu(last, pair[u])
+        apply_gate(nc.scalar, last, 0, HALF)
+        empty_pair(nc.scalar, last - 1, 1)
+        apply_gate(nc.scalar, last, HALF, H)
+        turn_pair(last, 0, "expert1", 1)
+        turn_pair(last, 1, "acc", ACC_BANKS)
+        scatter(0, done[0], S - LEAST_PIECE)
+        empty_pair(nc.scalar, last, 0)
+        empty_pair(nc.scalar, last, 1)
+        scatter(0, S - LEAST_PIECE, S)
+        scatter(1, done[1], S)
+
+        wm_bf = [rounded[:, SCALAR_COLUMNS : SCALAR_COLUMNS + N, :], own([P, N, PACK], BF16, "wm_bf1", "last")[:, :, :]]
+        round_and_interleave(nc.gpsimd, wm_bf[0], wm_raw[:, 0, :, :])
+        round_and_interleave(nc.scalar, wm_bf[1], wm_raw[:, 1, :, :])
+
+        def tokens(k):
+            return slice(k * CHUNK, (k + 1) * CHUNK)
+
+        def window_by_head(u):
+            return win[u][:].rearrange("p (o t) -> p o t", o=D)
+
+        nc.scalar.copy(out=both[:, 0, :, :], in_=window_by_head(0))
+        for k in range(1, CHUNKS):
+            nc.scalar.copy(out=both[:, 1, :, tokens(k)], in_=window_by_head(1)[:, :, tokens(k)])
         for o in range(D):
             nc.vector.quantize_mx(
                 out=wm_codes[:, o * N : (o + 1) * N].bitcast(FP8X4), scales=wm_scales[:, o * N : (o + 1) * N],
-                in_=wm_bf[o][:, :, :].rearrange("p n j -> p (n j)"),
+                in_=wm_bf[o].rearrange("p n j -> p (n j)"),
             )
+        nc.vector.tensor_copy(out=both[:, 1, :, tokens(0)], in_=window_by_head(1)[:, :, tokens(0)])
 
-        if V_SIDE:
-            t1 = TOKEN_CUTS[V_SIDE]
-            nc.vector.tensor_copy(out=both[:, 1, :, 0:t1], in_=win[1][:].rearrange("p (o t) -> p o t", o=D)[:, :, 0:t1])
+        def interleave(eng, k):
+            copy_on(eng, c_bf[k][:], both[:, :, :, tokens(k)].rearrange("p u o t -> p o t u"))
 
-        def interleave(k, eng):
-            copy_on(eng, c_bf[k][:], both[:, :, :, TOKEN_CUTS[k] : TOKEN_CUTS[k + 1]].rearrange("p u o t -> p o t u"))
-
-        def quant_c(k):
+        def quantise_c(k):
             nc.vector.quantize_mx(
                 out=c_codes[k][:].bitcast(FP8X4), scales=c_scales[k][:],
                 in_=c_bf[k][:].rearrange("p o t u -> p (o t u)").bitcast(BF16),
@@ -415,60 +355,39 @@ def tile_moe_mhm_gelu_kernel(tc, x_words, x_scales, w, wm, gate, offs, out):
 
         def merge_pass(acc, k, h, o):
             ncols = slice(o * N + h * P, o * N + (h + 1) * P)
-            tcols = slice(o * widths[k], (o + 1) * widths[k])
+            tcols = slice(o * CHUNK, (o + 1) * CHUNK)
             nc.tensor.matmul_mx(
                 out=acc, lhsT=wm_codes[:, ncols].bitcast(FP8X4), lhsT_scale=wm_scales[:, ncols],
                 rhs=c_codes[k][:, tcols].bitcast(FP8X4), rhs_scale=c_scales[k][:, tcols],
                 start=(o == 0), stop=(o == D - 1),
             )
 
+        chunk_banks = [("acc", ACC_BANKS)] * ACC_BANKS + [("expert1", 1), ("spare", 1)]
+
         def merge(k):
-            t0, t1 = TOKEN_CUTS[k], TOKEN_CUTS[k + 1]
-            quant_c(k)
-            if k in OWN_BANK:
-                acc = psum.tile([P, 2, widths[k]], F32, name="acc_own%d" % k, tag=OWN_BANK[k], bufs=1)
-            else:
-                acc = psum.tile([P, 2, widths[k]], F32, name="acc", tag="acc")
+            quantise_c(k)
+            acc = psum.tile([P, 2, CHUNK], F32, name="acc%d" % k, tag=chunk_banks[k][0], bufs=chunk_banks[k][1])
             for h in range(2):
                 for o in range(D):
                     merge_pass(acc[:, h, :], k, h, o)
-            copy_on(RES_ENG[k], result[k][:], acc[:])
-            nc.sync.dma_start(out=out_v[:, :, t0:t1], in_=result[k][:])
+            nc.scalar.copy(out=result[k][:], in_=acc[:])
+            nc.sync.dma_start(out=out_v[:, :, tokens(k)], in_=result[k][:])
 
-        def last_chunk():
-            k = nch - 1
-            t0, t1 = TOKEN_CUTS[k], TOKEN_CUTS[k + 1]
-            accs = [psum.tile([P, widths[k]], F32, name="acc_last%d" % h, tag="last", bufs=2) for h in range(2)]
-            quant_c(k)
-            for o in range(D):
-                for h in range(2):
-                    merge_pass(accs[h][:], k, h, o)
-            nc.scalar.copy(out=result[k][:, 0, :], in_=accs[0][:])
-            nc.scalar.dma_start(out=out_v[:, 0, t0:t1], in_=result[k][:, 0, :])
-            nc.vector.tensor_copy(out=result[k][:, 1, :], in_=accs[1][:])
-            nc.sync.dma_start(out=out_v[:, 1, t0:t1], in_=result[k][:, 1, :])
+        for k in SCALAR_CHUNKS:
+            interleave(nc.scalar, k)
+        for k in range(CHUNKS):
+            if k not in SCALAR_CHUNKS:
+                interleave(nc.vector, k)
+            if k >= 1:
+                merge(k - 1)
 
-        def interleave_head(k, o, eng):
-            copy_on(eng, c_bf[k][:, o, :, :], both[:, :, o, TOKEN_CUTS[k] : TOKEN_CUTS[k + 1]].rearrange("p u t -> p t u"))
-
-        for k in S_CHUNKS:
-            interleave(k, "s")
-        for k in HALF_CHUNKS:
-            interleave_head(k, 1, "s")
-        if WARM:
-            warm_ps = psum.tile([P, H], F32, name="warm_ps", tag="expert0", bufs=1)
-            for n in range(WARM):
-                nc.tensor.matmul_mx(
-                    out=warm_ps[:], lhsT=wm_codes[:, N : N + P].bitcast(FP8X4), lhsT_scale=wm_scales[:, N : N + P],
-                    rhs=wm_codes[:].bitcast(FP8X4), rhs_scale=wm_scales[:], start=True, stop=True,
-                )
-        for step in range(nch):
-            if step < DIRECT:
-                direct("v", 1, step)
-            elif step in HALF_CHUNKS:
-                interleave_head(step, 0, "v")
-            elif step not in S_CHUNKS:
-                interleave(step, "v")
-            if step >= 1:
-                merge(step - 1)
-        last_chunk()
+        k = CHUNKS - 1
+        accs = [psum.tile([P, CHUNK], F32, name="acc_last%d" % h, tag="last", bufs=2) for h in range(2)]
+        quantise_c(k)
+        for o in range(D):
+            for h in range(2):
+                merge_pass(accs[h][:], k, h, o)
+        nc.scalar.copy(out=result[k][:, 0, :], in_=accs[0][:])
+        nc.scalar.dma_start(out=out_v[:, 0, tokens(k)], in_=result[k][:, 0, :])
+        nc.vector.tensor_copy(out=result[k][:, 1, :], in_=accs[1][:])
+        nc.sync.dma_start(out=out_v[:, 1, tokens(k)], in_=result[k][:, 1, :])

@@ -25,10 +25,11 @@ HALF = H // 2
 QUARTER = H // 4
 OFFS_ROWS = 16
 SCALE_GROUPS = 4
-G_RUN = 2
-S_RUN = 4
+RUN = 4
 
-SCALAR_COLUMNS = 272
+STEADY_FROM = 6
+STEADY_COLUMNS = 184
+EARLY_COLUMNS = 272
 SCALAR_COLUMNS_W3 = 304
 VECTOR_GATE = 224
 W1_CUT = 320
@@ -119,9 +120,8 @@ def tile_moe_mhm_gelu_kernel(tc, x_words, x_scales, w, wm, gate, offs, out):
                 nc.scalar.copy(out=dst, in_=src)
 
         def round_and_interleave(eng, dst, src):
-            run = G_RUN if eng is nc.gpsimd else S_RUN
-            dst = dst.rearrange("p (c i) j -> p c j i", i=run)
-            src = src.rearrange("p j (c i) -> p c j i", i=run)
+            dst = dst.rearrange("p (c i) j -> p c j i", i=RUN)
+            src = src.rearrange("p j (c i) -> p c j i", i=RUN)
             if eng is nc.gpsimd:
                 nc.gpsimd.tensor_scalar(dst, src, 1.0, 0.0, MULT, ADD)
             else:
@@ -138,7 +138,10 @@ def tile_moe_mhm_gelu_kernel(tc, x_words, x_scales, w, wm, gate, offs, out):
             first, piece = [x for x in pieces if x[0] <= e * C][-1]
             return piece[:, e * C - first : (e + 1) * C - first]
 
-        rounded = keep.tile([P, H + SCALAR_COLUMNS_W3, PACK], BF16, name="rounded", align_bytes=64)
+        def steady_place(e):
+            return EARLY_COLUMNS + (e - STEADY_FROM + 1) * HALF
+
+        rounded = keep.tile([P, steady_place(E - 1) + H, PACK], BF16, name="rounded", align_bytes=64)
         w_bf, w_codes, w_scales, sums, acts, gated, turn_ps, win = {}, {}, {}, {}, {}, {}, {}, {}
 
         def rounded_cols(e, a, b):
@@ -182,13 +185,14 @@ def tile_moe_mhm_gelu_kernel(tc, x_words, x_scales, w, wm, gate, offs, out):
             acts[e] = ring.tile([P, 2, P, 2], F32, name="acts", align_bytes=64)[:, :, :, :]
 
         def new_gated(e):
-            gated[e] = ring.tile([P, H], BF16, name="gated", align_bytes=64)
+            gated[e] = ring.tile([P, H], BF16, name="gated", align_bytes=64)[:, :]
 
         def pair_words(e, u):
-            return gated[e][:].bitcast(F32)[:, u * P : (u + 1) * P]
+            return gated[e].bitcast(F32)[:, u * P : (u + 1) * P]
 
         def turn(e):
-            turn_ps[e] = psum.tile([P, 2, C], F32, name="turn_ps%d" % e, tag="expert%d" % (e % 2), bufs=1)
+            bank = "expert%d" % (e % 2) if e < STEADY_FROM - 2 else "spare"
+            turn_ps[e] = psum.tile([P, 2, C], F32, name="turn_ps%d" % e, tag=bank, bufs=1)
             for u in range(2):
                 nc.tensor.transpose(turn_ps[e][:, u, :], pair_words(e, u), ident[:])
 
@@ -272,34 +276,46 @@ def tile_moe_mhm_gelu_kernel(tc, x_words, x_scales, w, wm, gate, offs, out):
         win[0] = own([P, D * T], F32, "win0", "raw3_0")
         scatter(0, 0, LEAST_PIECE)
 
+        laps = [keep.tile([P, H + P], F32, name="laps%d" % k, align_bytes=64) for k in range(2)]
         done = [LEAST_PIECE, PIECE]
         for e in range(4, E):
-            if e % 2 == 0:
+            if e >= STEADY_FROM:
+                w_bf[e] = [(0, rounded[:, steady_place(e) : steady_place(e) + H, :])]
+                round_w(nc.scalar, e, H - STEADY_COLUMNS, H)
+                round_w(nc.gpsimd, e, 0, H - STEADY_COLUMNS)
+                quantise_w(e, [(H - QUARTER, H), (HALF, H - QUARTER), (0, HALF)])
+            elif e % 2 == 0:
                 w_bf[e] = [(0, rounded[:, 0:H, :])]
-                round_w(nc.scalar, e, 0, SCALAR_COLUMNS)
-                round_w(nc.gpsimd, e, SCALAR_COLUMNS, H)
+                round_w(nc.scalar, e, 0, EARLY_COLUMNS)
+                round_w(nc.gpsimd, e, EARLY_COLUMNS, H)
                 quantise_w(e, low_first)
             else:
-                w_bf[e] = [(0, rounded[:, SCALAR_COLUMNS : SCALAR_COLUMNS + H, :])]
-                round_w(nc.scalar, e, H - SCALAR_COLUMNS, H)
-                round_w(nc.gpsimd, e, 0, H - SCALAR_COLUMNS)
+                w_bf[e] = [(0, rounded[:, EARLY_COLUMNS : EARLY_COLUMNS + H, :])]
+                round_w(nc.scalar, e, H - EARLY_COLUMNS, H)
+                round_w(nc.gpsimd, e, 0, H - EARLY_COLUMNS)
                 quantise_w(e, low_first[::-1])
-            if e < E - 1:
+            if e < STEADY_FROM:
                 product(e)
             else:
                 product(e, low_first[::-1])
-            new_acts(e - 1)
-            new_gated(e - 1)
+            if e < STEADY_FROM:
+                new_acts(e - 1)
+            else:
+                acts[e - 1] = laps[(e - 1) % 2][:, 0:H].rearrange("s (u m v) -> s u m v", u=2, v=2)
+            if e < STEADY_FROM - 1:
+                new_gated(e - 1)
+            else:
+                gated[e - 1] = laps[e % 2][:, H - P : H + P].bitcast(BF16)
+            gelu(e - 1, both_pairs)
+            empty(e - 2)
             if e < E - 1:
-                gelu(e - 1, both_pairs)
-                empty(e - 2)
-                apply_gate(nc.vector, e - 1, 0, VECTOR_GATE)
-                apply_gate(nc.scalar, e - 1, VECTOR_GATE, H)
+                if e < STEADY_FROM - 1:
+                    apply_gate(nc.vector, e - 1, 0, VECTOR_GATE)
+                    apply_gate(nc.scalar, e - 1, VECTOR_GATE, H)
+                else:
+                    apply_gate(nc.scalar, e - 1, 0, H)
                 turn(e - 1)
             else:
-                gelu(e - 1, pair[0])
-                empty(e - 2)
-                gelu(e - 1, pair[1])
                 apply_gate(nc.scalar, e - 1, 0, HALF)
                 apply_gate(nc.scalar, e - 1, HALF, H)
                 turn_pair(e - 1, 0, "expert0", 1)
@@ -309,7 +325,7 @@ def tile_moe_mhm_gelu_kernel(tc, x_words, x_scales, w, wm, gate, offs, out):
 
         last = E - 1
         new_acts(last)
-        gated[last] = own([P, H], BF16, "gated_last", "last")
+        gated[last] = own([P, H], BF16, "gated_last", "last")[:, :]
         empty_pair(nc.scalar, last - 1, 0)
         for u in range(2):
             gelu(last, pair[u])
@@ -324,7 +340,7 @@ def tile_moe_mhm_gelu_kernel(tc, x_words, x_scales, w, wm, gate, offs, out):
         scatter(0, S - LEAST_PIECE, S)
         scatter(1, done[1], S)
 
-        wm_bf = [rounded[:, SCALAR_COLUMNS : SCALAR_COLUMNS + N, :], own([P, N, PACK], BF16, "wm_bf1", "last")[:, :, :]]
+        wm_bf = [rounded[:, steady_place(E) : steady_place(E) + N, :], own([P, N, PACK], BF16, "wm_bf1", "last")[:, :, :]]
         round_and_interleave(nc.gpsimd, wm_bf[0], wm_raw[:, 0, :, :])
         round_and_interleave(nc.scalar, wm_bf[1], wm_raw[:, 1, :, :])
 

@@ -54,15 +54,15 @@ def tile_moe_mhm_gelu_kernel(tc, x_words, x_scales, w, wm, gate, offs, out):
         psum = ctx.enter_context(tc.psum_pool(name="psum", bufs=ACC_BANKS))
 
         offsets = keep.tile([P, S // OFFS_ROWS], U16, name="offsets")
-        xw = keep.tile([P, D * T], I32, name="xw", align_bytes=64)
-        xs = keep.tile([P, D * T], U8, name="xs", align_bytes=64)
+        xw = keep.tile([P, D * T], I32, name="xw", align_bytes=256)
+        xs = keep.tile([P, D * T], U8, name="xs", align_bytes=256)
         gate_rows = keep.tile([P, C], F32, name="gate_rows")
         gate_cols = keep.tile([P, E], F32, name="gate_cols")
         ident = keep.tile([P, P], F32, name="ident")
         zeros = keep.tile([P, C], F32, name="zeros")
 
         def own(shape, dtype, name, tag):
-            return shared.tile(shape, dtype, name=name, tag=tag, align_bytes=64)
+            return shared.tile(shape, dtype, name=name, tag=tag, align_bytes=256)
 
         load_cuts = [[0, HALF, H], [0, W1_CUT, H]] + [[0, H]] * (E - 2)
         w3_and_acts2 = own([P, PACK * H + H - LAP], F32, "w3_and_acts2", "raw3_0")
@@ -75,7 +75,7 @@ def tile_moe_mhm_gelu_kernel(tc, x_words, x_scales, w, wm, gate, offs, out):
                 else:
                     views.append((a, own([P, PACK, b - a], F32, "w_raw%d_%d" % (e, k), "raw%d_%d" % (e, k))[:, :, :]))
             w_raw.append(views)
-        wm_raw = keep.tile([P, D, PACK, N], F32, name="wm_raw")
+        wm_raw = keep.tile([P, D, PACK, N], F32, name="wm_raw", align_bytes=256)
         wm_scales = keep.tile([P, D * N], U8, name="wm_scales", align_bytes=64)
         wm_codes = keep.tile([P, D * N], U32, name="wm_codes", align_bytes=64)
         turned = keep.tile([P, 2, S], F32, name="turned", align_bytes=64)
@@ -215,7 +215,7 @@ def tile_moe_mhm_gelu_kernel(tc, x_words, x_scales, w, wm, gate, offs, out):
         c_bf = [keep.tile([P, D, CHUNK, 2], F32, name="c_bf%d" % k, align_bytes=64) for k in range(CHUNKS)]
         c_codes = [keep.tile([P, D * CHUNK], U32, name="c_codes%d" % k, align_bytes=64) for k in range(CHUNKS)]
         c_scales = [keep.tile([P, D * CHUNK], U8, name="c_scales%d" % k, align_bytes=64) for k in range(CHUNKS)]
-        result = [keep.tile([P, 2, CHUNK], F32, name="result%d" % k) for k in range(CHUNKS)]
+        result = [keep.tile([P, 2, CHUNK], F32, name="result%d" % k, align_bytes=256) for k in range(CHUNKS)]
         out_v = out.rearrange("(h p) t -> p h t", p=P)
 
         gather(slot_scales, xs[:], U8, 0, S // 2, "scales0")

@@ -17,7 +17,6 @@ FP8X4 = mybir.dt.float8_e4m3fn_x4
 GELU = mybir.ActivationFunctionType.Gelu_apprx_tanh
 COPY = mybir.ActivationFunctionType.Copy
 MULT = mybir.AluOpType.mult
-ADD = mybir.AluOpType.add
 
 P = 128
 PACK = 4
@@ -33,11 +32,12 @@ EARLY_COLUMNS = 272
 SCALAR_COLUMNS_W3 = 304
 VECTOR_GATE = 224
 W1_CUT = 320
+COVER_ROWS = 1
 LAP = 16
 LEAST_PIECE = D * T // 8
 PIECE = 2 * C
 FIRST_WORDS = 2 * C
-LATE_WORDS = 8 * C
+LATE_WORDS = 9 * C
 CHUNK = 128
 CHUNKS = T // CHUNK
 RING = 3
@@ -64,7 +64,7 @@ def tile_moe_mhm_gelu_kernel(tc, x_words, x_scales, w, wm, gate, offs, out):
         def own(shape, dtype, name, tag):
             return shared.tile(shape, dtype, name=name, tag=tag, align_bytes=256)
 
-        load_cuts = [[0, HALF, H], [0, W1_CUT, H]] + [[0, H]] * (E - 2)
+        load_cuts = [[0, H], [0, W1_CUT, H]] + [[0, H]] * (E - 2)
         w3_and_acts2 = own([P, PACK * H + H - LAP], F32, "w3_and_acts2", "raw3_0")
         w_raw = []
         for e in range(E):
@@ -88,7 +88,8 @@ def tile_moe_mhm_gelu_kernel(tc, x_words, x_scales, w, wm, gate, offs, out):
         nc.gpsimd.memset(xs[:].bitcast(I32), 0)
         nc.vector.memset(gate_rows[: P // 2, :], 0.0)
         nc.sync.dma_start(offsets[:], offs)
-        load_w(0, 0)
+        w0_rows = w[0].rearrange("(p j) c -> p j c", j=PACK)
+        nc.sync.dma_start(out=w_raw[0][0][1][:, :COVER_ROWS, :], in_=w0_rows[:, :COVER_ROWS, :])
         xs_words = xs[:].bitcast(I32).rearrange("p (o t) -> p o t", o=D)
         scale_rows = x_scales.bitcast(I32).rearrange("o b t -> b o t")
         for q in range(SCALE_GROUPS):
@@ -96,12 +97,12 @@ def tile_moe_mhm_gelu_kernel(tc, x_words, x_scales, w, wm, gate, offs, out):
         nc.gpsimd.memset(zeros[P // 2 :, :], 0.0)
         make_identity(nc, ident[:])
         nc.scalar.activation(out=gate_rows[P // 2 :, :], in_=zeros[P // 2 :, :], func=GELU)
-        load_w(0, 1)
-        nc.sync.dma_start(out=gate_rows[0:E, :], in_=gate[0].rearrange("(e s) -> e s", s=C))
+        nc.sync.dma_start(out=w_raw[0][0][1][:, COVER_ROWS:, :], in_=w0_rows[:, COVER_ROWS:, :])
         nc.sync.dma_start(
             out=xw[:].rearrange("p (o t) -> p o t", o=D),
             in_=x_words.rearrange("o p t d -> p o (t d)").bitcast(I32),
         )
+        nc.sync.dma_start(out=gate_rows[0:E, :], in_=gate[0].rearrange("(e s) -> e s", s=C))
         for e in range(1, E):
             for k in range(len(w_raw[e])):
                 load_w(e, k)
@@ -114,18 +115,15 @@ def tile_moe_mhm_gelu_kernel(tc, x_words, x_scales, w, wm, gate, offs, out):
         nc.scalar.copy(out=gate_cols[:], in_=gate_ps[:, 0:E])
 
         def copy_on(eng, dst, src):
-            if eng is nc.vector:
-                nc.vector.tensor_copy(out=dst, in_=src)
-            else:
+            if eng is nc.scalar:
                 nc.scalar.copy(out=dst, in_=src)
+            else:
+                eng.tensor_copy(out=dst, in_=src)
 
         def round_and_interleave(eng, dst, src):
-            dst = dst.rearrange("p (c i) j -> p c j i", i=RUN)
-            src = src.rearrange("p j (c i) -> p c j i", i=RUN)
-            if eng is nc.gpsimd:
-                nc.gpsimd.tensor_scalar(dst, src, 1.0, 0.0, MULT, ADD)
-            else:
-                copy_on(eng, dst, src)
+            dst = dst.rearrange("p (c i) (u v) -> p c u i v", i=RUN, u=2)
+            src = src.rearrange("p (u v) (c i) -> p c u i v", i=RUN, u=2)
+            copy_on(eng, dst, src)
 
         slot_scales, slot_words = [], []
 
@@ -221,13 +219,12 @@ def tile_moe_mhm_gelu_kernel(tc, x_words, x_scales, w, wm, gate, offs, out):
         gather(slot_scales, xs[:], U8, 0, S // 2, "scales0")
         gather(slot_scales, xs[:], U8, S // 2, S, "scales1")
         gather(slot_words, xw[:].bitcast(U32), U32, 0, FIRST_WORDS, "words0")
-        gather(slot_words, xw[:].bitcast(U32), U32, FIRST_WORDS, LATE_WORDS, "words1")
 
         w_bf[0] = [(0, own([P, H, PACK], BF16, "w_bf0", "bf0")[:, :, :])]
-        round_w(nc.scalar, 0, 0, HALF)
-        round_w(nc.scalar, 0, HALF, H)
+        round_w(nc.scalar, 0, 0, H)
         quantise_w(0, [(0, H)])
         product(0)
+        gather(slot_words, xw[:].bitcast(U32), U32, FIRST_WORDS, LATE_WORDS, "raw0_0")
 
         w_bf[1] = [(0, own([P, HALF, PACK], BF16, "w_bf1", "bf1")[:, :, :]), (HALF, rounded[:, HALF:H, :])]
         round_w(nc.scalar, 1, 0, HALF)

@@ -42,6 +42,7 @@ CHUNK = 128
 CHUNKS = T // CHUNK
 RING = 3
 ACC_BANKS = 3
+WARM_UP_COLUMNS = (512, 128,)
 SCALAR_CHUNKS = (3, 5)
 
 
@@ -356,6 +357,13 @@ def tile_moe_mhm_gelu_kernel(tc, x_words, x_scales, w, wm, gate, offs, out):
                 in_=wm_bf[o].rearrange("p n j -> p (n j)"),
             )
         nc.vector.tensor_copy(out=both[:, 1, :, tokens(0)], in_=window_by_head(1)[:, :, tokens(0)])
+
+        idle_bank = psum.tile([P, H], F32, name="idle_bank", tag="expert0", bufs=1)
+        for n in WARM_UP_COLUMNS:
+            nc.tensor.matmul_mx(
+                out=idle_bank[:, 0:n], lhsT=wm_codes[:, 0:P].bitcast(FP8X4), lhsT_scale=wm_scales[:, 0:P],
+                rhs=wm_codes[:, H - n : H].bitcast(FP8X4), rhs_scale=wm_scales[:, H - n : H], start=True, stop=True,
+            )
 
         def interleave(eng, k):
             copy_on(eng, c_bf[k][:], both[:, :, :, tokens(k)].rearrange("p u o t -> p o t u"))

from contextlib import ExitStack

import concourse.mybir as mybir
from concourse.masks import make_identity

D, T, E, C, H, N = 2, 768, 12, 128, 512, 256
S = E * C
FLOPS = 2 * H * H * S + 2 * D * H * N * T

F32 = mybir.dt.float32
BF16 = mybir.dt.bfloat16
I32 = mybir.dt.int32
U32 = mybir.dt.uint32
U16 = mybir.dt.uint16
U8 = mybir.dt.uint8
FP8X4 = mybir.dt.float8_e4m3fn_x4
GELU = mybir.ActivationFunctionType.Gelu_apprx_tanh
COPY = mybir.ActivationFunctionType.Copy
MULT = mybir.AluOpType.mult

P = 128
PACK = 4
HALF = H // 2
QUARTER = H // 4
OFFS_ROWS = 16
SCALE_GROUPS = 4
RUN = 4

STEADY_FROM = 6
STEADY_COLUMNS = 184
EARLY_COLUMNS = 272
SCALAR_COLUMNS_W3 = 304
VECTOR_GATE = 224
W1_CUT = 320
COVER_ROWS = 1
LAP = 16
LEAST_PIECE = D * T // 8
PIECE = 2 * C
FIRST_WORDS = 2 * C
LATE_WORDS = 9 * C
CHUNK = 128
CHUNKS = T // CHUNK
RING = 3
ACC_BANKS = 3
WARM_UP_COLUMNS = (512, 128,)
SCALAR_CHUNKS = (3, 5)


def tile_moe_mhm_gelu_kernel(tc, x_words, x_scales, w, wm, gate, offs, out):
    nc = tc.nc
    with ExitStack() as ctx:
        keep = ctx.enter_context(tc.tile_pool(name="keep", bufs=1))
        ring = ctx.enter_context(tc.tile_pool(name="ring", bufs=RING))
        shared = ctx.enter_context(tc.tile_pool(name="shared", bufs=1))
        psum = ctx.enter_context(tc.psum_pool(name="psum", bufs=ACC_BANKS))

        offsets = keep.tile([P, S // OFFS_ROWS], U16, name="offsets")
        xw = keep.tile([P, D * T], I32, name="xw", align_bytes=256)
        xs = keep.tile([P, D * T], U8, name="xs", align_bytes=256)
        gate_rows = keep.tile([P, C], F32, name="gate_rows")
        gate_cols = keep.tile([P, E], F32, name="gate_cols")
        ident = keep.tile([P, P], F32, name="ident")
        zeros = keep.tile([P, C], F32, name="zeros")

        def own(shape, dtype, name, tag):
            return shared.tile(shape, dtype, name=name, tag=tag, align_bytes=256)

        load_cuts = [[0, H], [0, W1_CUT, H]] + [[0, H]] * (E - 2)
        w3_and_acts2 = own([P, PACK * H + H - LAP], F32, "w3_and_acts2", "raw3_0")
        w_raw = []
        for e in range(E):
            views = []
            for k, (a, b) in enumerate(zip(load_cuts[e], load_cuts[e][1:])):
                if e == 3:
                    views.append((a, w3_and_acts2[:, : PACK * H].rearrange("p (j c) -> p j c", j=PACK)))
                else:
                    views.append((a, own([P, PACK, b - a], F32, "w_raw%d_%d" % (e, k), "raw%d_%d" % (e, k))[:, :, :]))
            w_raw.append(views)
        wm_raw = keep.tile([P, D, PACK, N], F32, name="wm_raw", align_bytes=256)
        wm_scales = keep.tile([P, D * N], U8, name="wm_scales", align_bytes=64)
        wm_codes = keep.tile([P, D * N], U32, name="wm_codes", align_bytes=64)
        turned = keep.tile([P, 2, S], F32, name="turned", align_bytes=64)
        both = keep.tile([P, 2, D, T], F32, name="both")

        def load_w(e, k):
            a, b = load_cuts[e][k], load_cuts[e][k + 1]
            nc.sync.dma_start(out=w_raw[e][k][1], in_=w[e].rearrange("(p j) c -> p j c", j=PACK)[:, :, a:b])

        nc.gpsimd.memset(xs[:].bitcast(I32), 0)
        nc.vector.memset(gate_rows[: P // 2, :], 0.0)
        nc.sync.dma_start(offsets[:], offs)
        w0_rows = w[0].rearrange("(p j) c -> p j c", j=PACK)
        nc.sync.dma_start(out=w_raw[0][0][1][:, :COVER_ROWS, :], in_=w0_rows[:, :COVER_ROWS, :])
        xs_words = xs[:].bitcast(I32).rearrange("p (o t) -> p o t", o=D)
        scale_rows = x_scales.bitcast(I32).rearrange("o b t -> b o t")
        for q in range(SCALE_GROUPS):
            nc.sync.dma_start(out=xs_words[32 * q : 32 * q + 4, :, :], in_=scale_rows[4 * q : 4 * q + 4, :, :])
        nc.gpsimd.memset(zeros[P // 2 :, :], 0.0)
        make_identity(nc, ident[:])
        nc.scalar.activation(out=gate_rows[P // 2 :, :], in_=zeros[P // 2 :, :], func=GELU)
        nc.sync.dma_start(out=w_raw[0][0][1][:, COVER_ROWS:, :], in_=w0_rows[:, COVER_ROWS:, :])
        nc.sync.dma_start(
            out=xw[:].rearrange("p (o t) -> p o t", o=D),
            in_=x_words.rearrange("o p t d -> p o (t d)").bitcast(I32),
        )
        nc.sync.dma_start(out=gate_rows[0:E, :], in_=gate[0].rearrange("(e s) -> e s", s=C))
        for e in range(1, E):
            for k in range(len(w_raw[e])):
                load_w(e, k)
        nc.sync.dma_start(
            out=wm_raw[:].rearrange("p o j n -> p o (j n)"),
            in_=wm.rearrange("(o p j) n -> p o (j n)", o=D, j=PACK),
        )
        gate_ps = psum.tile([P, P], F32, name="gate_ps", tag="acc")
        nc.tensor.transpose(gate_ps[:], gate_rows[:], ident[:])
        nc.scalar.copy(out=gate_cols[:], in_=gate_ps[:, 0:E])

        def copy_on(eng, dst, src):
            if eng is nc.scalar:
                nc.scalar.copy(out=dst, in_=src)
            else:
                eng.tensor_copy(out=dst, in_=src)

        def round_and_interleave(eng, dst, src):
            dst = dst.rearrange("p (c i) (u v) -> p c u i v", i=RUN, u=2)
            src = src.rearrange("p (u v) (c i) -> p c u i v", i=RUN, u=2)
            copy_on(eng, dst, src)

        slot_scales, slot_words = [], []

        def gather(into, window, dtype, a, b, tag):
            piece = own([P, b - a], dtype, "gathered_%s" % tag, tag)
            nc.vector.tensor_copy(out=piece[:], in_=window.indirect(offsets[:, a // OFFS_ROWS : b // OFFS_ROWS]))
            into.append((a, piece))

        def slots_of(pieces, e):
            first, piece = [x for x in pieces if x[0] <= e * C][-1]
            return piece[:, e * C - first : (e + 1) * C - first]

        def steady_place(e):
            return EARLY_COLUMNS + (e - STEADY_FROM + 1) * HALF

        rounded = keep.tile([P, steady_place(E - 1) + H, PACK], BF16, name="rounded", align_bytes=64)
        w_bf, w_codes, w_scales, sums, acts, gated, turn_ps, win = {}, {}, {}, {}, {}, {}, {}, {}

        def rounded_cols(e, a, b):
            first, view = [x for x in w_bf[e] if x[0] <= a][-1]
            return view[:, a - first : b - first, :]

        def round_w(eng, e, a, b):
            first, raw = [x for x in w_raw[e] if x[0] <= a][-1]
            round_and_interleave(eng, rounded_cols(e, a, b), raw[:, :, a - first : b - first])

        def quantise_w(e, ranges):
            w_codes[e] = ring.tile([P, H], U32, name="w_codes", align_bytes=64)
            w_scales[e] = ring.tile([P, H], U8, name="w_scales", align_bytes=64)
            for a, b in ranges:
                nc.vector.quantize_mx(
                    out=w_codes[e][:, a:b].bitcast(FP8X4), scales=w_scales[e][:, a:b],
                    in_=rounded_cols(e, a, b).rearrange("p c j -> p (c j)"),
                )

        def product(e, ranges=((0, H),)):
            sums[e] = psum.tile([P, H], F32, name="sums%d" % e, tag="expert%d" % (e % 2), bufs=1)
            for a, b in ranges:
                nc.tensor.matmul_mx(
                    out=sums[e][:, a:b], lhsT=slots_of(slot_words, e).bitcast(FP8X4), lhsT_scale=slots_of(slot_scales, e),
                    rhs=w_codes[e][:, a:b].bitcast(FP8X4), rhs_scale=w_scales[e][:, a:b], start=True, stop=True,
                )

        def gelu(e, pairs):
            nc.scalar.activation(
                out=acts[e][:, pairs, :, :], in_=sums[e][:].rearrange("s (m u v) -> s u m v", u=2, v=2)[:, pairs, :, :], func=GELU
            )

        def apply_gate(eng, e, a, b):
            values = acts[e].rearrange("s u m v -> s (u m v)")[:, a:b]
            if eng is nc.vector:
                nc.vector.tensor_scalar(gated[e][:, a:b], values, gate_cols[:, e : e + 1], None, MULT)
            else:
                nc.scalar.activation(out=gated[e][:, a:b], in_=values, func=COPY, scale=gate_cols[:, e : e + 1])

        def new_acts(e):
            acts[e] = ring.tile([P, 2, P, 2], F32, name="acts", align_bytes=64)[:, :, :, :]

        def new_gated(e):
            gated[e] = ring.tile([P, H], BF16, name="gated", align_bytes=64)[:, :]

        def pair_words(e, u):
            return gated[e].bitcast(F32)[:, u * P : (u + 1) * P]

        def turn(e):
            bank = "expert%d" % (e % 2) if e < STEADY_FROM - 2 else "spare"
            turn_ps[e] = psum.tile([P, 2, C], F32, name="turn_ps%d" % e, tag=bank, bufs=1)
            for u in range(2):
                nc.tensor.transpose(turn_ps[e][:, u, :], pair_words(e, u), ident[:])

        def empty(e):
            nc.scalar.copy(out=turned[:, :, e * C : (e + 1) * C], in_=turn_ps[e][:])

        def turn_pair(e, u, tag, bufs):
            turn_ps[e, u] = psum.tile([P, C], F32, name="turn_ps%d_%d" % (e, u), tag=tag, bufs=bufs)
            nc.tensor.transpose(turn_ps[e, u][:], pair_words(e, u), ident[:])

        def empty_pair(eng, e, u):
            copy_on(eng, turned[:, u, e * C : (e + 1) * C], turn_ps[e, u][:])

        def scatter(u, a, b):
            nc.vector.tensor_copy(out=win[u][:].indirect(offsets[:, a // OFFS_ROWS : b // OFFS_ROWS]), in_=turned[:, u, a:b])

        both_pairs = slice(0, 2)
        pair = [slice(0, 1), slice(1, 2)]
        low_first = [(0, HALF), (HALF, H)]
        c_bf = [keep.tile([P, D, CHUNK, 2], F32, name="c_bf%d" % k, align_bytes=64) for k in range(CHUNKS)]
        c_codes = [keep.tile([P, D * CHUNK], U32, name="c_codes%d" % k, align_bytes=64) for k in range(CHUNKS)]
        c_scales = [keep.tile([P, D * CHUNK], U8, name="c_scales%d" % k, align_bytes=64) for k in range(CHUNKS)]
        result = [keep.tile([P, 2, CHUNK], F32, name="result%d" % k, align_bytes=256) for k in range(CHUNKS)]
        out_v = out.rearrange("(h p) t -> p h t", p=P)

        gather(slot_scales, xs[:], U8, 0, S // 2, "scales0")
        gather(slot_scales, xs[:], U8, S // 2, S, "scales1")
        gather(slot_words, xw[:].bitcast(U32), U32, 0, FIRST_WORDS, "words0")

        w_bf[0] = [(0, own([P, H, PACK], BF16, "w_bf0", "bf0")[:, :, :])]
        round_w(nc.scalar, 0, 0, H)
        quantise_w(0, [(0, H)])
        product(0)
        gather(slot_words, xw[:].bitcast(U32), U32, FIRST_WORDS, LATE_WORDS, "raw0_0")

        w_bf[1] = [(0, own([P, HALF, PACK], BF16, "w_bf1", "bf1")[:, :, :]), (HALF, rounded[:, HALF:H, :])]
        round_w(nc.scalar, 1, 0, HALF)
        round_w(nc.scalar, 1, HALF, W1_CUT)
        round_w(nc.scalar, 1, W1_CUT, H - QUARTER)
        round_w(nc.gpsimd, 1, H - QUARTER, H)
        quantise_w(1, low_first)
        gather(slot_words, xw[:].bitcast(U32), U32, LATE_WORDS, S, "raw1_1")
        product(1, low_first)
        acts[0] = own([P, 2, P, 2], F32, "acts0", "raw1_0")[:, :, :, :]
        gelu(0, both_pairs)
        new_gated(0)
        apply_gate(nc.scalar, 0, 0, H)
        turn(0)

        w_bf[2] = [(0, rounded[:, 0:H, :])]
        for a, b in low_first:
            round_w(nc.vector, 2, a, b)
        quantise_w(2, low_first)
        product(2)
        new_acts(1)
        new_gated(1)
        for u in (1, 0):
            gelu(1, pair[u])
        for u in (1, 0):
            apply_gate(nc.scalar, 1, u * HALF, (u + 1) * HALF)
        turn_pair(1, 1, "expert1", 1)
        turn_pair(1, 0, "acc", ACC_BANKS)
        empty(0)
        empty_pair(nc.scalar, 1, 1)
        empty_pair(nc.scalar, 1, 0)
        win[1] = own([P, D * T], F32, "win1", "raw2_0")
        scatter(1, 0, PIECE)

        w_bf[3] = [(0, rounded[:, SCALAR_COLUMNS_W3 : SCALAR_COLUMNS_W3 + H, :])]
        round_w(nc.scalar, 3, H - LAP, H)
        round_w(nc.scalar, 3, H - SCALAR_COLUMNS_W3, H - LAP)
        round_w(nc.gpsimd, 3, 0, H - SCALAR_COLUMNS_W3)
        quantise_w(3, low_first[::-1])
        product(3)
        acts[2] = w3_and_acts2[:, PACK * H - LAP :].rearrange("s (u m v) -> s u m v", u=2, v=2)
        gelu(2, both_pairs)
        new_gated(2)
        apply_gate(nc.vector, 2, 0, H)
        turn(2)
        win[0] = own([P, D * T], F32, "win0", "raw3_0")
        scatter(0, 0, LEAST_PIECE)

        laps = [keep.tile([P, H + P], F32, name="laps%d" % k, align_bytes=64) for k in range(2)]
        done = [LEAST_PIECE, PIECE]
        for e in range(4, E):
            if e >= STEADY_FROM:
                w_bf[e] = [(0, rounded[:, steady_place(e) : steady_place(e) + H, :])]
                round_w(nc.scalar, e, H - STEADY_COLUMNS, H)
                round_w(nc.gpsimd, e, 0, H - STEADY_COLUMNS)
                quantise_w(e, [(H - QUARTER, H), (HALF, H - QUARTER), (0, HALF)])
            elif e % 2 == 0:
                w_bf[e] = [(0, rounded[:, 0:H, :])]
                round_w(nc.scalar, e, 0, EARLY_COLUMNS)
                round_w(nc.gpsimd, e, EARLY_COLUMNS, H)
                quantise_w(e, low_first)
            else:
                w_bf[e] = [(0, rounded[:, EARLY_COLUMNS : EARLY_COLUMNS + H, :])]
                round_w(nc.scalar, e, H - EARLY_COLUMNS, H)
                round_w(nc.gpsimd, e, 0, H - EARLY_COLUMNS)
                quantise_w(e, low_first[::-1])
            if e < STEADY_FROM:
                product(e)
            else:
                product(e, low_first[::-1])
            if e < STEADY_FROM:
                new_acts(e - 1)
            else:
                acts[e - 1] = laps[(e - 1) % 2][:, 0:H].rearrange("s (u m v) -> s u m v", u=2, v=2)
            if e < STEADY_FROM - 1:
                new_gated(e - 1)
            else:
                gated[e - 1] = laps[e % 2][:, H - P : H + P].bitcast(BF16)
            gelu(e - 1, both_pairs)
            empty(e - 2)
            if e < E - 1:
                if e < STEADY_FROM - 1:
                    apply_gate(nc.vector, e - 1, 0, VECTOR_GATE)
                    apply_gate(nc.scalar, e - 1, VECTOR_GATE, H)
                else:
                    apply_gate(nc.scalar, e - 1, 0, H)
                turn(e - 1)
            else:
                apply_gate(nc.scalar, e - 1, 0, HALF)
                apply_gate(nc.scalar, e - 1, HALF, H)
                turn_pair(e - 1, 0, "expert0", 1)
                turn_pair(e - 1, 1, "acc", ACC_BANKS)
            scatter(e % 2, done[e % 2], (e - 1) * C)
            done[e % 2] = (e - 1) * C

        last = E - 1
        new_acts(last)
        gated[last] = own([P, H], BF16, "gated_last", "last")[:, :]
        empty_pair(nc.scalar, last - 1, 0)
        for u in range(2):
            gelu(last, pair[u])
        apply_gate(nc.scalar, last, 0, HALF)
        empty_pair(nc.scalar, last - 1, 1)
        apply_gate(nc.scalar, last, HALF, H)
        turn_pair(last, 0, "expert1", 1)
        turn_pair(last, 1, "acc", ACC_BANKS)
        scatter(0, done[0], S - LEAST_PIECE)
        empty_pair(nc.scalar, last, 0)
        empty_pair(nc.scalar, last, 1)
        scatter(0, S - LEAST_PIECE, S)
        scatter(1, done[1], S)

        wm_bf = [rounded[:, steady_place(E) : steady_place(E) + N, :], own([P, N, PACK], BF16, "wm_bf1", "last")[:, :, :]]
        round_and_interleave(nc.gpsimd, wm_bf[0], wm_raw[:, 0, :, :])
        round_and_interleave(nc.scalar, wm_bf[1], wm_raw[:, 1, :, :])

        def tokens(k):
            return slice(k * CHUNK, (k + 1) * CHUNK)

        def window_by_head(u):
            return win[u][:].rearrange("p (o t) -> p o t", o=D)

        nc.scalar.copy(out=both[:, 0, :, :], in_=window_by_head(0))
        for k in range(1, CHUNKS):
            nc.scalar.copy(out=both[:, 1, :, tokens(k)], in_=window_by_head(1)[:, :, tokens(k)])
        for o in range(D):
            nc.vector.quantize_mx(
                out=wm_codes[:, o * N : (o + 1) * N].bitcast(FP8X4), scales=wm_scales[:, o * N : (o + 1) * N],
                in_=wm_bf[o].rearrange("p n j -> p (n j)"),
            )
        nc.vector.tensor_copy(out=both[:, 1, :, tokens(0)], in_=window_by_head(1)[:, :, tokens(0)])

        idle_bank = psum.tile([P, H], F32, name="idle_bank", tag="expert0", bufs=1)
        for n in WARM_UP_COLUMNS:
            nc.tensor.matmul_mx(
                out=idle_bank[:, 0:n], lhsT=wm_codes[:, 0:P].bitcast(FP8X4), lhsT_scale=wm_scales[:, 0:P],
                rhs=wm_codes[:, H - n : H].bitcast(FP8X4), rhs_scale=wm_scales[:, H - n : H], start=True, stop=True,
            )

        def interleave(eng, k):
            copy_on(eng, c_bf[k][:], both[:, :, :, tokens(k)].rearrange("p u o t -> p o t u"))

        def quantise_c(k):
            nc.vector.quantize_mx(
                out=c_codes[k][:].bitcast(FP8X4), scales=c_scales[k][:],
                in_=c_bf[k][:].rearrange("p o t u -> p (o t u)").bitcast(BF16),
            )

        def merge_pass(acc, k, h, o):
            ncols = slice(o * N + h * P, o * N + (h + 1) * P)
            tcols = slice(o * CHUNK, (o + 1) * CHUNK)
            nc.tensor.matmul_mx(
                out=acc, lhsT=wm_codes[:, ncols].bitcast(FP8X4), lhsT_scale=wm_scales[:, ncols],
                rhs=c_codes[k][:, tcols].bitcast(FP8X4), rhs_scale=c_scales[k][:, tcols],
                start=(o == 0), stop=(o == D - 1),
            )

        chunk_banks = [("acc", ACC_BANKS)] * ACC_BANKS + [("expert1", 1), ("spare", 1)]

        def merge(k):
            quantise_c(k)
            acc = psum.tile([P, 2, CHUNK], F32, name="acc%d" % k, tag=chunk_banks[k][0], bufs=chunk_banks[k][1])
            for h in range(2):
                for o in range(D):
                    merge_pass(acc[:, h, :], k, h, o)
            nc.scalar.copy(out=result[k][:], in_=acc[:])
            nc.sync.dma_start(out=out_v[:, :, tokens(k)], in_=result[k][:])

        for k in SCALAR_CHUNKS:
            interleave(nc.scalar, k)
        for k in range(CHUNKS):
            if k not in SCALAR_CHUNKS:
                interleave(nc.vector, k)
            if k >= 1:
                merge(k - 1)

        k = CHUNKS - 1
        accs = [psum.tile([P, CHUNK], F32, name="acc_last%d" % h, tag="last", bufs=2) for h in range(2)]
        quantise_c(k)
        for o in range(D):
            for h in range(2):
                merge_pass(accs[h][:], k, h, o)
        nc.scalar.copy(out=result[k][:, 0, :], in_=accs[0][:])
        nc.scalar.dma_start(out=out_v[:, 0, tokens(k)], in_=result[k][:, 0, :])
        nc.vector.tensor_copy(out=result[k][:, 1, :], in_=accs[1][:])
        nc.sync.dma_start(out=out_v[:, 1, tokens(k)], in_=result[k][:, 1, :])
